import numpy as np, ml_dtypes
CORES = [5,29,101,125,133,157,229,253]
N = 8
import mx_ref
BF = ml_dtypes.bfloat16
def entries(a):
    return np.ascontiguousarray(a.T).reshape(-1)
def table(e):
    return np.ascontiguousarray(np.reshape(e, (-1, 16)).T).astype(np.int32)
def gentries(a):
    return np.ascontiguousarray(a.reshape(8, 16, -1).transpose(0, 2, 1)).reshape(8, -1)
def gtable(e):
    e = np.asarray(e); return np.ascontiguousarray(e.reshape(8, -1, 16).transpose(0, 2, 1)).reshape(128, -1).astype(np.int32)
def gcols(t, e):
    v = np.concatenate([t.reshape(8, 16, -1, 4), np.zeros((8, 16, 1, 4), BF)], axis=2)
    return np.ascontiguousarray(np.stack([v[g][:, e[g]] for g in range(8)])).reshape(128, -1)
def tile(rs):
    return np.stack(rs, axis=2).reshape(128, -1).astype(BF)
def cut(t, i, w=512):
    return t[:, w * i:w * i + w]
def pick(q, e):
    c = np.concatenate([q[0].reshape(128, -1, 4), np.zeros((128, 1, 4), np.uint8)], axis=1); s = np.concatenate([q[1], np.ones((16, 1), np.uint8)], axis=1)
    return (np.ascontiguousarray(c[:, e].reshape(128, -1)), np.ascontiguousarray(s[:, e]))
def join(*qs):
    return (np.concatenate([q[0] for q in qs], axis=1), np.concatenate([q[1] for q in qs], axis=1))
def put(q, e, v):
    c, s = q[0].reshape(128, -1, 4).copy(), q[1].copy(); c[:, e] = v[0].reshape(128, -1, 4); s[:, e] = v[1]
    return (c.reshape(128, -1), s)
def pk(c, s):
    return (np.ascontiguousarray(c), mx_ref.live(s))
def emit(q):
    return q[0], q[1]
def packed(v, rng):
    q = [mx_ref.quantize(np.ascontiguousarray(v[r])) for r in range(N)]
    return np.stack([a for a, b in q]), np.stack([mx_ref.plane(b, rng) for a, b in q])
def values_of_codes():
    e, c = np.zeros((128, 128, 4), np.float32), np.zeros((128, 2, 4), np.uint8)
    e[np.arange(128), np.arange(128), 0] = 1
    c[:127, :, 0] = np.arange(256).reshape(2, 128).T[:127]
    return mx_ref.matmul(mx_ref.quantize(e.reshape(128, 512).astype(BF)), (c.reshape(128, 8), np.full((16, 2), 127, np.uint8))).T.reshape(-1).astype(np.float64)
CODE_VALUE, SCALE_VALUE = values_of_codes(), 2.0 ** (np.arange(256) - 127.0)
def decode(q):
    return (CODE_VALUE[q[0]].reshape(16, 8, -1, 4) * SCALE_VALUE[q[1]][:, None, :, None] + 0.0).reshape(128, -1).astype(np.float32)
def f(rng, *shape):
    return mx_ref.flush((rng.standard_normal(shape, dtype=np.float32) * np.exp2(rng.integers(-2, 3, shape[:-1] + (1,)))).astype(BF))
def wide(rng, *shape, cols=0):
    v = rng.standard_normal(shape, dtype=np.float32) * np.exp2(rng.integers(-12, 13, shape)).astype(np.float32)
    if cols: v *= np.repeat(np.exp2(rng.integers(-cols, cols + 1, shape[:-2] + (1, shape[-1] // 4))) * (rng.random(shape[:-2] + (1, shape[-1] // 4)) > 0.0625), 4, axis=-1).astype(np.float32)
    return mx_ref.flush(v.astype(BF))
H, A, C, L, M, R = 4, 88, 352, 256, 40, 3
WAY = [(-1, -1), (-1, 0), (-1, 1), (0, -1), (0, 1), (1, -1), (1, 0), (1, 1)]
ROW, COL = np.arange(C) // A, np.arange(C) % A
def seen(place, life):
    e = np.full((N, 8, C), -1)
    for g in range(8):
        k = place[:, g]
        lives = np.take_along_axis(life, k, axis=1)
        b = [np.where(lives, k + C * i, -1).reshape(N, H, A) for i in range(3)]
        field = np.concatenate([np.roll(b[0], 1, axis=0), b[1], np.roll(b[2], -1, axis=0)], axis=1)
        near = np.full((N, C), -1)
        for n in range(A + 2 * H, 0, -1):
            i, j = H + ROW + n * WAY[g][0], COL + n * WAY[g][1]
            ok = (i >= 0) & (i < 3 * H) & (j >= 0) & (j < A)
            z = field[:, np.where(ok, i, 0), np.where(ok, j, 0)]
            near = np.where(ok & (z >= 0), z, near)
        np.put_along_axis(e[:, g], k, near, axis=1)
    return e
def big(v):
    v = v.astype(np.float32)
    v[np.abs(v) < np.float32(2.0 ** -16)] = 0
    return v.astype(BF)
def numbers_of(rng):
    return {"x": big(f(rng, N, 128, 4 * C)), "u": np.array(f(rng, N, 128, 512)), "v": np.array(f(rng, N, 128, 512))}
def layers(rng, still=[]):
    w = np.array(f(rng, N, 128, 2048)).reshape(N, 8, 16, 4, 8, 16, 4)
    for i in still:
        w[:, :, i] = 0
        w[:, :, :, :, :, i] = 0
    return w
def weights(rng, w):
    c, p = packed(np.ascontiguousarray(w).reshape(N, 128, 2048), rng)
    return {"wc": c, "ws": p}
def signs(rng):
    return np.stack([rng.permutation(8) % 2 * 2.0 - 1.0 for r in range(N)])
def lives_of(rng):
    return np.stack([rng.permutation(C) < L for r in range(N)])
def seats_of(rng):
    return np.argsort(rng.random((N, 8, C)), axis=2)
def lists_of(place, life):
    return {"seat": np.stack([gtable(place[r]) for r in range(N)]), "alive": np.stack([table(life[r].astype(int)) for r in range(N)])}
def sit(e, squares, cells):
    others = e[~np.isin(e, cells)]
    e[squares] = cells
    e[np.setdiff1d(np.arange(C), squares)] = others
def marks(d, a, m):
    x, u = d["x"].reshape(N, 8, 16, C, 4), d["u"].reshape(N, 128, 128, 4)
    x[:, :, 0] = 0
    x[:, :, 0, :, 0] = a.astype(np.float32).astype(BF)
    x[:, 3, 8] = 0
    x[:, 3, 8, :, 0] = m.astype(np.float32).astype(BF)
    u[:, :, ::16] = 0
    u[:, :, 1] = 0
    for i in range(0, 128, 16): u[:, i, i, 0] = 1
    u[:, 56, 1, 0] = 1
def setup_inputs(rng):
    return {**numbers_of(rng), **weights(rng, layers(rng)), **lists_of(seats_of(rng), lives_of(rng))}
def setup_inputs_ties(rng):
    d = numbers_of(rng)
    k = np.array([1.5, 0.0, -1.25])
    a, m = k[rng.integers(0, 3, (N, 8, C))], k[rng.integers(0, 3, (N, C))]
    e = rng.permutation(N)
    a[e[0]], m[e[0]] = 1.5, 1.5
    marks(d, a, m)
    d["x"][e[1]] = 0
    return {**d, **weights(rng, layers(rng, [0, 8])), **lists_of(seats_of(rng), lives_of(rng))}
def setup_inputs_near(rng):
    d = numbers_of(rng)
    life, place = lives_of(rng), seats_of(rng)
    x = np.zeros((N, 8, 16, C, 4), np.float32)
    u = d["u"].reshape(N, 128, 128, 4)
    u[:, :, ::16] = 0
    u[:, :, 1] = 0
    w = layers(rng, [0, 8, 9, 10, 11, 12, 13, 14, 15])
    o, c = rng.permutation(N) % 4, signs(rng)
    j = np.arange(C)
    for r in range(N):
        place[r, 3] = j
        s = j // 2
        size = 1.0 if o[r] < 2 else 2.0 ** -4
        if o[r] < 2:
            x[r, :, 1:8] = d["x"][r].astype(np.float32).reshape(8, 16, C, 4)[:, 1:8]
            x[r, :, 0, :, 0] = c[r][:, None]
            for i in rng.permutation(8)[:4]: x[r, i, 0, rng.choice(np.flatnonzero(life[r])), 0] *= np.float32(2.0 ** 30)
        else: w[r] = 0
        if o[r] == 3:
            h = rng.permutation(C // 2) < L // 2
            life[r] = np.concatenate([h, h])
            s = j % (C // 2)
            x[r, :, 0, :, 0] = (8 + j // (C // 2)) * 2.0 ** -33
            n = np.flatnonzero(life[r])
            x[r, 3, 0, n[0], 0] = 2.0 ** -18
            who, left = n[1:], n[:-1]
            low = who[(who // A == left // A) & (who < C // 2)][-(M // 2):]
            fight = np.concatenate([n[1:2], low, low + C // 2])
            behind = rng.permutation(np.setdiff1d(n, np.concatenate([fight, left[np.isin(who, fight)]])))[:3 * M + 3]
            sit(place[r, 6], (np.arange(4)[:, None] * A + np.arange(M + 1)).reshape(-1), np.concatenate([fight, behind]))
            x[r, 6, 0, behind, 0] = -2.0 ** -18
        z = ((s[:, None] >> np.arange(8)) & 1) * np.exp2(np.arange(8) - 23.0) * size
        x[r, :, 8] = z[:, :4]
        x[r, :, 9] = z[:, 4:]
        x[r, :, 10:] = rng.integers(4, 8, (8, 6, C, 4)) * rng.choice([-1.0, 1.0], (8, 6, C, 4)) * 2.0 ** -20 * size
        k = 1.0 if o[r] == 0 else 2.0 ** -30
        for h in range(0, 128, 16):
            u[r, h, h, 0] = k
            u[r, h + 8:h + 10, h] = k
        u[r, 48, 1, 0] = k
        u[r, 56:58, 1] = k
    d["x"] = x.reshape(N, 128, 4 * C).astype(BF)
    return {**d, **weights(rng, w), **lists_of(place, life)}
def setup_inputs_huge(rng):
    d = numbers_of(rng)
    life, place = lives_of(rng), seats_of(rng)
    x = 2.0 ** 30 * (0.75 + 0.15 * rng.random((N, 128, C, 4)))
    a = 2.0 ** 30 * (1 - 0.1 * rng.random((N, 8, 16, 9, 4)))
    a[:, :, :, 8] *= -1
    a[:, [1, 6], :, 8] = 0
    c = signs(rng)
    for r in rng.permutation(N)[:N // 2]:
        x[r] *= (rng.permutation(C) % 2 * 2.0 - 1.0)[:, None]
        for g in range(8):
            a[r, np.arange(8) != g, :, g] = 0
            a[r, :, :, g] *= c[r, g]
        a[r, np.arange(8) != 3, :, 8] = 0
    u = d["u"].reshape(N, 128, 128, 4)
    a = a.reshape(N, 128, 9, 4).astype(np.float32).astype(BF)
    u[:, :, ::16] = a[:, :, :8]
    u[:, :, 1] = a[:, :, 8]
    corner = [0, 0, A - 1, 0, A - 1, C - A, C - A, C - 1]
    for g in range(8):
        k, way = rng.permutation(A), WAY[g][0] * WAY[g][1]
        q = rng.integers(H)
        for r in range(N):
            z = (ROW == q) & (COL > 0) & (COL < A - 1)
            if WAY[g][0]:
                n = k[(COL - way * (ROW + H * r)) % A]
                kept = (n + r) % 4
                z = (n < (C - L) // H) & ~((ROW == 0) & (kept % 2 == 1)) & ~((ROW == H - 1) & (kept >= 2))
            z[corner[g]] = False
            free = rng.permutation(np.flatnonzero(~z & (np.arange(C) != corner[g])))
            z[free[:C - L - int(np.sum(z))]] = True
            e = place[r, g]
            e[z] = rng.permutation(np.flatnonzero(~life[r]))
            e[~z] = rng.permutation(np.flatnonzero(life[r]))
            lone = np.flatnonzero(life[r])[0]
            e[np.flatnonzero(e == lone)[0]] = e[corner[g]]
            e[corner[g]] = lone
    w = np.zeros((N, 128, 4, 128, 4), np.float32)
    i = np.arange(128)
    for b in range(4): w[:, i, b, i, b] = -1
    d["x"] = x.astype(np.float32).reshape(N, 128, 4 * C).astype(BF)
    return {**d, **weights(rng, w.astype(BF)), **lists_of(place, life)}
def setup_inputs_deaths(rng):
    d = numbers_of(rng)
    life, place = lives_of(rng), seats_of(rng)
    a, m = rng.integers(8, 16, (N, 8, C)) * 0.125, np.zeros((N, C))
    o = rng.permutation(N) % 2
    for r in range(N):
        life[r] = np.roll(life[r], -int(np.flatnonzero(life[r])[0]))
        k = rng.permutation(np.flatnonzero(life[r])[1:])
        fight, behind = k[:M], k[M + 1:4 * M + 1]
        n = M - 1 - int(o[r])
        m[r, k[M]] = 1
        m[r, fight[:n]] = rng.integers(8, 16, n) * 0.125
        if o[r]:
            lone = fight[-1]
            sit(place[r, 0], [1, C - A], [lone, 0])
            for g, s in ((1, 0), (2, A - 1), (5, C - A), (6, C - A), (7, C - 1)): sit(place[r, g], [s], [lone])
            sit(place[r, 3], np.append(np.arange(M), A), np.concatenate([k[M:M + 1], fight]))
            sit(place[r, 4], np.arange(A - M, A), fight)
            for g in (3, 4): a[r, g, fight] *= -1
            a[r, 4, lone] = -4
        else:
            sit(place[r, 0], [C - A], [0])
            sit(place[r, 3], np.arange(M + 1), np.concatenate([k[M:M + 1], fight]))
            sit(place[r, 6], (np.arange(4)[:, None] * A + np.arange(M)).reshape(-1), np.concatenate([fight, behind]))
            a[r, 6, behind] *= -1
    marks(d, a, m)
    x, u = d["x"].reshape(N, 8, 16, C, 4), d["u"].reshape(N, 128, 128, 4)
    x[:, 0, 8] = 0
    x[:, 0, 8, 0, 0] = np.roll(o, -1).astype(np.float32).astype(BF)
    u[:, 8, 1, 0] = 1
    return {**d, **weights(rng, layers(rng, [0, 8])), **lists_of(place, life)}
def setup_inputs_spread(rng):
    d = setup_inputs(rng)
    d["x"] = big(wide(rng, N, 128, 4 * C, cols=6))
    return d
def check_inputs(d):
    b = []
    for k in ("x", "u", "v"):
        a = np.abs(d[k].astype(np.float32))
        if not (np.isfinite(a).all() and ((a == 0) | (a >= 2.0 ** -30) & (a <= 2.0 ** 30)).all()): b.append("a value of " + k)
    if ((d["wc"] & 0x7F) == 0x7F).any(): b.append("a code of wc that is no number")
    z = np.zeros((128, 4, 4), np.float32)
    z[:, 1] = 2.0 ** -30
    z[:, 2] = 2.0 ** 30
    c, s = emit(mx_ref.quantize(z.reshape(128, 16).astype(BF)))
    for r in range(N):
        p = mx_ref.live(d["ws"][r])
        if not ((p == s[0, 0]) | (p >= s[0, 1]) & (p <= s[0, 2])).all(): b.append("a scale of ws")
        if not (np.sort(gentries(d["seat"][r]), axis=1) == np.arange(C)).all(): b.append("seat: a permutation for every group")
        e = entries(d["alive"][r])
        if not ((e == 0) | (e == 1)).all(): b.append("alive: zeros and ones")
        if int(np.sum(e == 1)) != L: b.append("alive: the number of ones")
    return b
def reference(x, u, v, wc, ws, seat, alive):
    qu = [mx_ref.quantize(u[r]) for r in range(N)]
    lay = [pk(wc[r], ws[r]) for r in range(N)]
    place = np.stack([gentries(seat[r]) for r in range(N)])
    life = np.stack([entries(alive[r]) == 1 for r in range(N)])
    now = [x[r] for r in range(N)]
    for t in range(R):
        came = decode(join(*[mx_ref.quantize(now[r]) for r in range(N)])).astype(BF)
        e, after, now = seen(place, life), life.copy(), []
        for r in range(N):
            above, own, below = [cut(came, (r + i) % N, 4 * C) for i in (-1, 0, 1)]
            q = mx_ref.quantize(gcols(np.concatenate([above, own, below], axis=1), e[r]))
            p = mx_ref.matmul(qu[r], q) + np.float32(0.0)
            made = tile([mx_ref.matmul(pick(lay[r], np.arange(128 * b, 128 * b + 128)), q) * np.float32(0.015625) + own[:, b::4].astype(np.float32) for b in range(4)])
            now.append(np.where(np.repeat(life[r], 4), made, own))
            c = np.argsort(-np.where(life[r], p[1], -np.inf), kind="stable")[:M]
            k = e[r][:, c]
            mine = (k >= C) & (k < 2 * C)
            g = np.argmin(np.where(mine, p[::16][:, c], np.inf), axis=0)
            named = k[g, np.arange(M)][mine.any(axis=0)] - C
            after[r, named[~np.isin(named, c)]] = False
        life = after
    y, ol = np.zeros((N, 128, C), np.float32), np.zeros((N, 1, C), np.float32)
    oc, osc = np.zeros((N, 128, 4 * C), np.uint8), np.zeros((N, 16, C), np.uint8)
    for r in range(N):
        q = mx_ref.quantize(now[r])
        y[r] = mx_ref.matmul(mx_ref.quantize(v[r]), q)
        ol[r, 0] = life[r]
        oc[r], osc[r] = emit(q)
    return {"y": y, "ol": ol, "oc": oc, "osc": osc}

@@ -1,0 +1,629 @@
+from concourse.bass import DstId, RemoteDMATransfer
+from concourse.mybir import dt, AluOpType, ActivationFunctionType
+
+A_ = AluOpType
+F_ = ActivationFunctionType
+C, L, NA, M, R = 352, 256, 88, 40, 3
+B = float(2 ** 20)
+BIG = 1e29
+PW = 448
+NONE = 433
+f32, bf, i32, u16, cod, pl = "float32", "bfloat16", "int32", "uint16", "float8_e4m3fn_x4", "uint8"
+f16 = "float16"
+
+
+def _sb(n, d):
+    return ("sbuf", [128, n], d)
+
+
+SCRATCH = {"ci": _sb(8, i32), "cf": _sb(64, f32), "sm": _sb(1024, f32), "aw": _sb(24, i32), "sw": _sb(24, i32), "si": _sb(96, i32)}
+for _n in "seatu l1 posl rayl one16 ciu ciu1 piu rayi lini cl".split():
+    SCRATCH[_n] = _sb(24, u16)
+for _n in "ipos ipos2 zl".split():
+    SCRATCH[_n] = _sb(16, u16)
+for _n in "j16 cray crow t1 t2 t3 t4 t5 v0 er".split():
+    SCRATCH[_n] = _sb(368, f32)
+for _n in "jj pm rmono nrow oi cum pirow rp val olr ysb".split():
+    SCRATCH[_n] = _sb(C, f32)
+for _n in "bo bi bic".split():
+    SCRATCH[_n] = _sb(360, f32)
+for _n in "h1 h2 h3 h4".split():
+    SCRATCH[_n] = _sb(368, f16)
+for _n, _w in dict(rst=368, diag=368, diagr=368, lr=360, ml=L, xo=8 + 4 * C, ub=512, vb=512, c64=520, eb=2048, tau=128, negi=128,
+                   cst=256, iot=L, ct=512, tw=4 * PW, zt=4 * L, sg=256, cmp=512, oh=4 * L).items():
+    SCRATCH[_n] = _sb(_w, bf)
+SCRATCH["et"], SCRATCH["ett"] = _sb(L, f32), _sb(L, f32)
+for _n, _w in dict(x=C, u=128, u1=144, v=128, w=512, e=512, o1=130, z=L, c=128, h=L, a0=C, a=C, a3=C, f=C, m0=128, m1=128, m2=128,
+                   r0=NA, r1=NA, r2=NA, l0=2 * NA, l1=2 * NA, l2=2 * NA).items():
+    SCRATCH["q" + _n], SCRATCH["p" + _n] = _sb(_w, cod), _sb(_w, pl)
+for _t in range(R):
+    SCRATCH["xn%d" % (_t + 1)] = _sb(4 + 4 * C, bf)
+for _b in range(8):
+    SCRATCH["bank%d" % _b] = ("psum", [128, 512], f32)
+
+SEMAPHORES = (["cV", "cS", "cT", "cG", "dal", "dse", "dx", "du", "dv", "dw", "dout", "sent"]
+              + ["arr%d" % t for t in range(R)] + ["rel%d" % t for t in range(R)])
+
+
+def _relays(T, topo, rank):
+    me, n = T.cores[rank], len(T.cores)
+    dsts = [(rank + 1) % n, (rank - 1) % n]
+    ok = [c for c in topo.cores_of(me) if T.rank_of(c) is None and all(topo.may_write(c, T.cores[d]) for d in dsts)]
+    ok.sort(key=lambda c: (topo.die(c) != topo.die(me), c))
+    return [(ok[0], dsts[0], True), (ok[2], dsts[1], True), (ok[3], dsts[0], False), (ok[1], dsts[1], False)]
+
+
+def _mask(es):
+    m = 0
+    for e in es:
+        m |= 1 << e
+    return m
+
+
+def _relay_program(g, core, T, topo):
+    n = len(T.cores)
+    for r in range(n):
+        if core not in topo.cores_of(T.cores[r]):
+            continue
+        for c, d, codes in _relays(T, topo, r):
+            if c != core:
+                continue
+            dst = T.cores[d]
+            rid, pid = topo.addr(dst, core)
+            off = 0 if d == (r + 1) % n else NA
+            ne = len(topo.engines(T.cores[r], core)) // 2
+            nout = len(topo.engines(core, dst))
+            for t in range(R):
+                g.wait_ge(T.sem["rel%d" % t], ne)
+                if codes:
+                    o, i = T["ql%d" % t][:, off:off + NA].bitcast(dt.uint8), T["qr%d" % t][:].bitcast(dt.uint8)
+                else:
+                    o, i = T["pl%d" % t][:, off:off + NA], T["pr%d" % t][:]
+                g.remote_dma(o, i, T.sem["arr%d" % t], T.sem.sent, pid, rid, topo.mask(core, dst))
+            g.wait_ge(T.sem.sent, R * nout)
+
+
+def rank_program(g, core, T, topo):
+    rank = T.rank_of(core)
+    if rank is None:
+        _relay_program(g, core, T, topo)
+        return
+    V, S, P, Y = g.vector, g.scalar, g.tensor, g.sync
+    Q = {"V": V, "S": S, "T": P, "G": g, "Y": Y}
+    cnt = {"V": 0, "S": 0, "T": 0, "G": 0}
+    know = {k: {} for k in Q}
+    lastw, reads = {}, {}
+
+    def need(e, toks):
+        want = {}
+        for s, n, snap in toks:
+            if know[e].get(s, 0) < n and want.get(s, (0, None))[0] < n:
+                want[s] = (n, snap)
+        for s in sorted(want, key=lambda s: -len(want[s][1])):
+            n, snap = want[s]
+            if know[e].get(s, 0) < n:
+                Q[e].wait_ge(T.sem[s], n)
+                know[e][s] = n
+                for k, v in snap.items():
+                    if know[e].get(k, 0) < v:
+                        know[e][k] = v
+
+    def deps(e, r, w):
+        toks = [lastw[k] for k in list(r) + list(w) if k in lastw]
+        for k in w:
+            toks += reads.get(k, [])
+        if e == "T":
+            toks = [x for x in toks if x[0] != "cT"]
+        need(e, toks)
+
+    def done(tok, r, w):
+        for k in r:
+            reads.setdefault(k, []).append(tok)
+        for k in w:
+            lastw[k] = tok
+            reads[k] = []
+
+    def op(e, fn, r, w):
+        r, w = r.split(), w.split()
+        w = w + [k for k in r if k.startswith("ps")]
+        deps(e, r, w)
+        cnt[e] += 1
+        fn().then_inc(T.sem["c" + e], 1)
+        done(("c" + e, cnt[e], dict(know[e])), r, w)
+
+    def dma(e, out, in_, sem, total, r, w):
+        r, w = r.split(), w.split()
+        deps(e, r, [])
+        Q[e].dma_start(out, in_).then_inc(T.sem[sem], 16)
+        done((sem, total, {}), r, w)
+
+    def ts(out, in0, s1, s2, o0, o1, r, w):
+        if o1 is None:
+            op("V", lambda: V.tensor_scalar(out, in0, s1, None, o0), r, w)
+        else:
+            op("V", lambda: V.tensor_scalar(out, in0, s1, s2, o0, o1), r, w)
+
+    def tt(out, a, b, o, r, w):
+        op("V", lambda: V.tensor_tensor(out, a, b, o), r, w)
+
+    def cp(out, a, r, w):
+        op("V", lambda: V.tensor_copy(out, a), r, w)
+
+    def scan(out, a, b, init, o0, o1, r, w):
+        op("V", lambda: V.tensor_tensor_scan(out, a, b, init, o0, o1), r, w)
+
+    def mset(ap, v, w):
+        op("V", lambda: V.memset(ap, v), "", w)
+
+    def qz(n, t, r):
+        op("V", lambda: V.quantize_mx(T["q" + n][:], T["p" + n][:], t), r, "q" + n)
+
+    def act(out, in_, f, r, w, bias=0.0, scale=1.0):
+        if f == F_.Copy:
+            op("S", lambda: S.activation(out, in_, f), r, w)
+        else:
+            op("S", lambda: S.activation(out, in_, f, bias=bias, scale=scale), r, w)
+
+    def sset(ap, n, v, w):
+        act(ap, T.crow[:, 0:n], F_.Identity, "crow", w, bias=float(v), scale=0.0)
+
+    def mm(b, l, l0, rr, r0, n, start=True, stop=True):
+        r = " ".join("q%s p%s" % (x, x) for x in (l, rr))
+        op("T", lambda: P.matmul_mx(ps[b][:, 0:n], T["q" + l][:, l0:l0 + 128], T["p" + l][:, l0:l0 + 128],
+                                    T["q" + rr][:, r0:r0 + n], T["p" + rr][:, r0:r0 + n], start, stop), r, "ps%d" % b)
+
+    def pick(to, fr, off, r):
+        act(T["p" + to][:], T["p" + fr][:].indirect(off), F_.Copy, "q%s %s" % (fr, r), "p" + to)
+        return lambda: cp(T["q" + to][:].bitcast(u32), T["q" + fr][:].bitcast(u32).indirect(off), "q%s %s" % (fr, r), "q" + to)
+
+    def iota(out, pat, w, base=0, ch=0, whole=False):
+        if whole:
+            op("G", lambda: g.iota(out, pat, base, ch), "", w)
+        else:
+            op("G", lambda: g.iota(out, pat, base, ch, allow_small_or_imprecise_dtypes=True), "", w)
+
+    names = {}
+
+    def col(n):
+        k = names.setdefault(n, len(names))
+        return T.cf[:, k:k + 1]
+
+    def arg(x):
+        return (col(x), " k." + x) if isinstance(x, str) else (x, "")
+
+    def vcol(n, a, s1, o0, s2=None, o1=None):
+        (x1, r1), (x2, r2) = arg(s1), arg(s2)
+        ts(col(n), col(a), x1, x2, o0, o1, "k." + a + r1 + r2, "k." + n)
+
+    def scol(n, a, scale=1.0, bias=0.0, f=F_.Identity):
+        (x1, r1), (x2, r2) = arg(scale), arg(bias)
+        act(col(n), col(a), f, "k." + a + r1 + r2, "k." + n, bias=x2, scale=x1)
+
+    smp = {}
+
+    def sm(n, w):
+        if n not in smp:
+            smp[n] = sum((x[1] + 7) // 8 * 8 for x in smp.values()), w
+        return T.sm[:, smp[n][0]:smp[n][0] + w]
+
+    def smv(n, a, b, s=1):
+        return T.sm[:, smp[n][0] + a:smp[n][0] + b:s]
+
+    fill = []
+
+    def gap(n=1):
+        for _ in range(min(n, len(fill))):
+            fill.pop(0)()
+
+    ps = [T["bank%d" % b] for b in range(8)]
+    add, sub, mul, mx, mn = A_.add, A_.subtract, A_.mult, A_.max, A_.min
+    u32, u8 = dt.uint32, dt.uint8
+    AND, SHR = A_.bitwise_and, A_.logical_shift_right
+    ID = F_.Identity
+    allec = " ".join("ec%d%d" % (a, a2) for a in range(4) for a2 in range(4))
+
+    for k in range(8):
+        dma("Y" if k % 2 else "S", T.aw[16 * k:16 * k + 16, 0:22], T.alive[:], "dal", 128, "", "aw")
+    dma("Y", T.sw[:, 0:22], T.seat[:], "dse", 16, "", "sw")
+    dma("Y", T.xo[:, 8:8 + 4 * C], T.x[:], "dx", 16, "", "xo")
+    dma("Y", T.ub[:], T.u[:], "du", 16, "", "ub")
+    dma("Y", T.qw[:].bitcast(u8), T.wc[:], "dw", 32, "", "qw")
+    dma("Y", T.pw[:], T.ws[:], "dw", 32, "", "qw")
+    dma("Y", T.vb[:], T.v[:], "dv", 16, "", "vb")
+
+    pi = T.ci[:, 7:8]
+    iota(pi, [[0, 1]], "pi", ch=1, whole=True)
+    iota(sm("m16", 22), [[16, 22]], "m16")
+    iota(sm("b2", 22), [[2, 11], [0, 2]], "b2")
+    iota(sm("m4", 23), [[4, 23]], "m4")
+    iota(T.jj[:], [[0, 22], [4096, 4], [512, 4]], "jj")
+    iota(T.j16[:], [[0, 23], [1, 16]], "j16")
+    iota(T.crow[:], [[1, 368]], "crow")
+    mset(T.c64[:], 64.0, "c64 c64x")
+    ts(T.ci[:, 0:1], pi, 15, None, AND, None, "pi", "ci0")
+    ts(T.ci[:, 1:2], pi, 4, None, SHR, None, "pi", "ci1")
+    ts(T.ci[:, 2:3], pi, 2, 3, SHR, AND, "pi", "ci2")
+    ts(T.ci[:, 3:4], pi, 3, None, AND, None, "pi", "ci3")
+    ts(T.ci[:, 4:5], pi, 4, 1, SHR, AND, "pi", "ci4")
+    ts(T.ci[:, 5:6], pi, 4, None, AND, None, "pi", "ci5")
+    mset(T.c64[:, 514:518], 0.0, "c64x")
+    for n in ("q", "g", "q4", "t4", "go", "h4"):
+        col(n)
+    cp(T.cf[:, 0:6], T.ci[:, 0:6], "ci0 ci1 ci2 ci3 ci4 ci5", "k.q k.g k.q4 k.t4 k.go k.h4")
+    mset(T.xo[:, 0:8], 0.0, "xoz")
+    vcol("a3", "g", 3.0, A_.is_ge)
+    vcol("gp", "g", 4.0, A_.is_ge, "g", add)
+    vcol("u3", "t4", -1.0, mul, 3.0, add)
+    vcol("dy1", "g", 5.0, A_.is_ge, "a3", add)
+    scol("pk", "q4", -4096.0, -1536.0)
+    scol("nq", "q", -1.0)
+    scol("rq", "q", 1e6, 1e6)
+    scol("y1", "t4", 1.0, -1.5)
+    scol("d", "t4", 1.0, -1.0)
+    scol("h0", "t4", -353.0, 353.0, F_.Relu)
+    scol("q176", "q", -1.0, 176.5)
+    scol("d15", "t4", 88.0, -220.0)
+    ts(sm("cw", 22), sm("m16", 22), col("q"), 2.0 + B, add, add, "m16 k.q", "cw")
+    vcol("dx1", "dy1", -3.0, mul, "gp", add)
+    vcol("dy", "dy1", -1.0, add)
+    ts(T.l1[:, 0:22], sm("b2", 22), col("go"), None, add, None, "b2 k.go", "l1")
+    vcol("dx", "dx1", -1.0, add)
+    vcol("vert", "dy", "dy", mul)
+    vcol("y2", "y1", "dy", mul, -88.0, mul)
+    vcol("w1", "dx", "u3", mul, "q4", add)
+    vcol("z", "vert", -1000.0, mul, 956.5, add)
+    mset(T.bo[:, C:C + 8], -B, "boz")
+    vcol("pa", "w1", "z", add)
+    vcol("pb", "y2", 132.0, add, "w1", add)
+    scol("ndy", "dy", -1.0)
+    scol("dn", "dy", 3.0, 0.0, F_.Relu)
+    scol("neg", "dx", -1.0, 0.0, F_.Relu)
+    scol("hz", "vert", -1.0, 1.0)
+    scol("v4", "vert", 4.0)
+    act(sm("ab", 23), sm("m4", 23), F_.Abs, "m4 k.pa", "ab", bias=col("pa"))
+    act(T.t5[:, 0:C], T.jj[:], F_.Abs, "jj k.pk", "t5", bias=col("pk"))
+    scol("k41", "dx", 4.0, 1.0)
+    act(T.pm[:], T.t5[:, 0:C], ID, "t5", "pm", bias=1536.0, scale=-1.0)
+    act(T.rst[:], T.j16[:], F_.Sign, "j16", "rst")
+    mset(T.ct[:, 4 * NA:512], 0.0, "ctz")
+    mset(T.cst[:, 0:128], 1.0, "cst0")
+    mset(T.cst[:, 128:256], -64.0, "cst1")
+
+    def esel(b):
+        op("G", lambda: g.affine_select(T.eb[:, 512 * b:512 * b + 512], T.c64[:, 0:512], [[4, 128], [1, 4]], A_.is_equal, 0.0, -b, -4),
+           "c64", "eb%d" % b)
+    esel(0)
+    esel(1)
+
+    rel = _relays(T, topo, rank)
+    eng = topo.engines(core, rel[0][0])
+    ne = len(eng) // 2
+    narr = sum(len(topo.engines(c, core)) for r2 in range(len(T.cores)) for c, d, _ in _relays(T, topo, r2) if d == rank)
+
+    def compose_send(t, v, rv, o, ro, xbuf, rx):
+        scan(o[:, 0:C], T.rst[:, 0:C], v[:, 0:C], 0.0, mul, mx, "rst " + rv, ro)
+        gap()
+        cp(T.si[:, 0:22], o[:, 15:C:16], ro, "si0")
+        gap()
+        ts(T.si[:, 24:46], T.si[:, 0:22], 511, None, AND, None, "si0", "si1")
+        gap()
+        ts(T.cl[:, 0:22], T.si[:, 24:46], 4.0, col("t4"), mul, add, "si1 k.t4", "cl")
+        gap()
+        act(T.ct[:, 192:C], xbuf[:].indirect(T.cl[:, 12:22]), F_.Copy, "cl " + rx, "ct1")
+        cp(T.ct[:, 0:192], xbuf[:].indirect(T.cl[:, 0:12]), "cl " + rx, "ct0")
+        qz("m%d" % t, T.ct[:], "ct0 ct1 ctz")
+        deps("G", ["qm%d" % t], [])
+        for codes in (True, False):
+            trs = []
+            for k, (c, d, cs) in enumerate(rel):
+                if cs == codes:
+                    rid, pid = topo.addr(c, core)
+                    src = T["qm%d" % t][:, 0:NA].bitcast(u8) if codes else T["pm%d" % t][:, 0:NA]
+                    dst = T["qr%d" % t][:].bitcast(u8) if codes else T["pr%d" % t][:]
+                    trs.append(RemoteDMATransfer(dst_ids=[DstId(rid=rid, pnc=pid)],
+                                                 dma_engine_mask=_mask(eng[ne * (k % 2):ne * (k % 2) + ne]),
+                                                 remote_sem=T.sem["rel%d" % t], src=src, dst=dst))
+            g.remote_dma_fused(trs, local_sem=T.sem.sent)
+        lastw["ql%d" % t] = ("arr%d" % t, narr, {})
+
+    tt(sm("oiw", 22), T.aw[:, 0:22], sm("cw", 22), mul, "aw cw", "oiw")
+    cp(T.seatu[:, 0:22], T.sw[:, 0:22], "sw", "seatu")
+    cp(T.t4[:, 0:C], sm("oiw", 22).indirect(T.l1[:, 0:22]), "oiw l1", "t4")
+    ts(sm("e1", 23), sm("ab", 23), 44.0, 1000.0, A_.is_gt, mul, "ab", "e1")
+    op("V", lambda: V.transpose(T.oi[:], T.t4[:, 0:C]), "t4", "oi")
+    act(T.rmono[:], T.j16[:, 0:C], F_.Relu, "j16 k.rq", "rmono", bias=col("rq"), scale=-1e6)
+    act(T.bo[:, 0:C], T.oi[:].indirect(T.seatu[:, 0:22]), ID, "oi seatu", "bo", bias=-B)
+    tt(sm("e2", 23), sm("e1", 23), sm("m4", 23), add, "e1 m4", "e2")
+    ts(T.t1[:, 0:C], T.oi[:], 1.0, None, mn, None, "oi", "t1")
+    ts(T.posl[:, 0:22], smv("e2", 0, 22), col("pb"), float(C), add, mn, "e2 k.pb", "posl")
+    scan(T.cum[:], T.t1[:, 0:C], T.t1[:, 0:C], 0.0, add, mx, "t1", "cum")
+    scol("hd", "dx", "hz")
+    scol("n12", "neg", 12.0)
+    scol("n3", "neg", -3.0, "q4")
+    scol("alpha", "hd", -1.0, "v4")
+    scol("h88", "hd", -88.0)
+    scol("g4", "hd", 351.0, 0.0, F_.Relu)
+    scol("ndx", "dx", -1.0)
+    scol("beta", "k41", "ndy", "h88")
+    scol("g1", "n12", "vert", "g4")
+    scol("cH", "neg", -3.0, "dx")
+    scol("gam", "k41", "dn", "g1")
+    scol("hdr", "h0", "vert")
+    act(sm("gi", 4), T.crow[:, 0:4], ID, "crow k.beta k.gam", "gi", bias=col("gam"), scale=col("beta"))
+    scol("r88", "d15", "ndy", 132.0)
+    for i in range(4):
+        act(T.nrow[:, NA * i:NA * i + NA], T.crow[:, 0:NA], ID, "crow gi k.alpha", "nrow%d" % i, bias=smv("gi", i, i + 1), scale=col("alpha"))
+    tt(T.t2[:, 0:C], T.bo[:].indirect(T.posl[:, 0:22]), T.pm[:], add, "bo boz posl pm", "t2")
+    ts(sm("na", 22), sm("oiw", 22), 0.0, None, A_.is_equal, None, "oiw", "na")
+    ts(sm("cz", 22), sm("cw", 22), 255.0 - B, None, add, None, "cw", "cz")
+    fill.extend([
+        lambda: scan(T.t1[:, 0:C], T.rmono[:], T.cum[:], 0.0, mx, mn, "rmono cum", "t1"),
+        lambda: None,
+        lambda: tt(sm("c2", 22), sm("cz", 22), T.t1[:, 15:C:16], sub, "cz t1", "c2"),
+        lambda: tt(sm("c3", 22), sm("c2", 22), sm("na", 22), mul, "c2 na", "c3"),
+    ])
+    compose_send(0, T.t2, "t2", T.t3, "t3", T.xo, "xo xoz")
+    esel(2)
+    esel(3)
+    iota(sm("g8i", 16), [[0, 2], [1, 2], [2, 4]], "g8i")
+    op("G", lambda: g.affine_select(T.tau[:], T.cst[:, 0:128], [[-1, 128]], A_.is_ge, 0.0, 0, 1), "cst0", "tau")
+    op("G", lambda: g.affine_select(T.negi[:], T.cst[:, 128:256], [[1, 128]], A_.is_equal, 0.0, 0, -1), "cst1", "negi")
+    act(T.t5[:], T.j16[:], F_.Abs, "j16 k.nq", "t5", bias=col("nq"))
+    scol("h16", "h4", 4.0)
+    scol("hno", "hz", float(NONE))
+    scol("lim", "hz", -264000.0, -88000.0)
+    act(T.diag[:], T.t5[:], F_.Relu, "t5", "diag", bias=1.0, scale=-1.0)
+    scol("slope", "hd", -16.0, "v4")
+    scol("po", "ndx", "d", "n3")
+    scol("sH", "hd", "q176")
+    scol("cH1", "hz", 1000.0, "cH")
+    scol("po1", "po", 1.0, -43.5)
+    scol("po2", "po", 1.0, "r88")
+    scol("sH2", "hz", 175.5, "sH")
+    scol("bs", "dy", 44.0, 301.0)
+    scol("cC", "po1", "vert", "sH")
+    scol("cH2", "cH1", 1.0, -43.5)
+    scol("sA", "po2", "vert", "sH2")
+    scol("cH3", "cH", 1.0, "bs")
+    act(sm("ab2", 23), T.crow[:, 0:23], F_.Abs, "crow k.slope k.cC", "ab2", bias=col("cC"), scale=col("slope"))
+    act(T.et[:, 0:92], T.crow[:, 0:92], F_.Abs, "crow k.cH2", "et", bias=col("cH2"))
+    act(sm("sr", 23), T.crow[:, 0:23], ID, "crow k.slope k.sA", "sr", bias=col("sA"), scale=col("slope"))
+    act(T.ett[:, 0:92], T.crow[:, 0:92], ID, "crow k.cH3", "ett", bias=col("cH3"))
+    act(sm("e3", 23), sm("ab2", 23), F_.Relu, "ab2 k.lim", "e3", bias=col("lim"), scale=2000.0)
+    act(T.et[:, 96:188], T.et[:, 0:92], F_.Relu, "et", "etb", bias=-88000.0, scale=2000.0)
+    act(T.cray[:], T.crow[:], ID, "crow", "cray", scale=512.0)
+
+    tt(sm("c4", 22), sm("c3", 22), T.t1[:, 15:C:16], mx, "c3 t1", "c4")
+    qz("x", T.xo[:, 8:8 + 4 * C], "xo")
+    ts(T.ciu[:, 0:22], sm("c4", 22), -1.0, None, add, None, "c4", "ciu")
+    qz("u", T.ub[:], "ub")
+    cp(T.pirow[:].indirect(T.ciu[:, 0:22]), T.crow[:, 0:C], "ciu crow", "pirow")
+    mset(T.one16[:, 1:9], 1, "one16")
+    scan(T.t1[:, 0:C], T.rmono[:], T.pirow[:], 0.0, mx, mn, "rmono pirow", "t1")
+    tt(sm("e4", 23), sm("e3", 23), sm("sr", 23), add, "e3 sr", "e4")
+    cp(T.piu[:, 0:22], T.t1[:, 15:C:16], "t1", "piu")
+    ts(T.rayl[:, 0:23], sm("e4", 23), float(C), col("hdr"), mn, mx, "e4 k.hdr", "rayl")
+    pick("a0", "x", T.piu[:, 0:22], "piu")()
+
+    def unpack_state(t, n):
+        xn, w = T["xn%d" % (t + 1)], (C if t == R - 1 else L)
+        for b in range(4):
+            mm(b, "e", 128 * b, n, 0, w)
+        for b in range(4):
+            mm(4 + b, "e", 128 * b, n, 0, C + L - w, True, False)
+
+        def one(b):
+            act(T.tw[:, PW * b + 1:PW * b + 1 + L], ps[b][:, 0:L], ID, "ps%d" % b, "tw%d" % b, scale=1.0 / 64)
+            if w == C:
+                act(xn[:, 4 + 4 * L + b:4 + 4 * C:4], ps[b][:, L:C], ID, "ps%d" % b, "xd%d_%d" % (t + 1, b), scale=1.0 / 64)
+        return one
+
+    cp(T.rp[:].indirect(T.seatu[:, 0:22]), T.nrow[:], "seatu nrow0 nrow1 nrow2 nrow3", "rp")
+    qz("e", T.eb[:], "eb0 eb1 eb2 eb3")
+    sset(T.bi[:, C:C + 1], 1, -B, "biz")
+    sset(T.bi[:, C + 1:C + 8], 7, 0, "biz2")
+    act(T.iot[:], T.crow[:, 1:L + 1], ID, "crow", "iot", scale=2.0 ** -13)
+    sset(T.tw[:, 0:4 * PW:PW], 4, 0, "twz")
+    sset(T.tw[:, NONE:4 * PW:PW], 4, 0, "twz2")
+    sset(sm("live", 2), 2, 1, "live0 live1")
+    sset(sm("nb", 2), 2, 0, "nb")
+    sset(sm("thr", 2), 2, 64 * (M - 0.5), "thr")
+    sset(T.oh[:, 514:1024:4], 128, 0, "ohz")
+    sset(T.oh[:, 3:512:4], 128, 0, "ohz2")
+    sset(T.xn1[:, 0:4], 4, 0, "xz1")
+    sset(T.xn2[:, 0:4], 4, 0, "xz2")
+    sset(T.lr[:, 1:L + 1], L, 1, "lr")
+    sset(T.lr[:, L + 1:359], 102, 0, "lrz")
+    sset(T.lr[:, 0:1], 1, 0, "lrz2")
+    sset(T.lr[:, 359:360], 1, 1, "lrz3")
+    one = unpack_state(0, "a0")
+    for b in range(4):
+        one(b)
+    act(sm("g8", 16), sm("g8i", 16), ID, "g8i", "g8", scale=0.125)
+    act(sm("r8", 16), sm("g8i", 16), F_.Relu, "g8i", "r8", bias=2 * BIG, scale=-4 * BIG)
+
+    tt(T.ett[:, 96:188], T.ett[:, 0:92], T.et[:, 96:188], add, "etb ett", "ettb")
+    tt(T.bi[:, 0:C], T.cum[:].indirect(T.seatu[:, 0:22]), T.bo[:, 0:C], mn, "cum seatu bo", "bi")
+    ts(T.ett[:, 0:92], T.ett[:, 96:188], float(NONE), col("vert"), mn, mul, "ettb k.vert", "ett")
+    tt(T.h1[:, 0:L], T.rp[:].indirect(T.piu[:, 0:16]), T.diag[:, 0:L], mul, "rp piu diag", "h1")
+    tt(T.cray[:, 0:368:4], T.cray[:, 0:368:4], T.ett[:, 0:92], add, "cray ett", "cray")
+    scan(T.h2[:, 0:L], T.rst[:, 0:L], T.h1[:, 0:L], 0.0, mul, mx, "rst h1", "h2")
+    ts(T.cray[:, 0:C:NA], T.cray[:, 0:C:NA], col("hno"), None, add, None, "cray k.hno", "cray")
+    cp(T.ipos[:], T.h2[:, 15:L:16], "h2", "ipos")
+    tt(T.v0[:], T.bi[:].indirect(T.rayl[:, 0:23]), T.cray[:], add, "bi biz biz2 rayl cray", "v0")
+    ts(T.one16[:, 0:1], col("t4"), 32.0, col("h16"), mul, add, "k.t4 k.h16", "one16c")
+    cp(T.v0[:, 0:C:NA], T.cray[:, 0:C:NA], "cray v0", "v0")
+    for k in range(2):
+        for h in range(2):
+            cp(T.ipos2[:, 2 * k + h:16:4], T.ipos[:, 8 * k + h:8 * k + 8:2], "ipos", "ip%d" % (2 * k + h))
+    act(T.bic[:], T.bi[:], F_.Relu, "bi biz biz2", "bic")
+    act(sm("r8b", 16), sm("r8", 16), ID, "r8", "r8b", bias=-BIG)
+
+    def z_list(v, rv, mask, rm, first):
+        scan(T.er[:], v, v, 0.0, mx, mx, rv, "er")
+        gap()
+        act(T.et[:], T.er[:].indirect(T.ipos2[:]), F_.Copy, "er ip0 ip1 ip2 ip3 etb", "et etb")
+        tt(T.t2[:, 0:L], T.er[:].indirect(T.ipos[:]), mask, mul, "er ipos " + rm, "t2")
+        op("V", lambda: V.transpose(T.ett[:], T.et[:]), "et ettb", "ett ettb")
+        gap()
+        cp(T.si[:, 48:64], T.ett[:, 0:L:16], "ett", "si2")
+        scan(T.t3[:, 0:L], T.rst[:, 0:L], T.t2[:, 0:L], 0.0, mul, mx, "rst t2", "t3")
+        ts(T.si[:, 64:80], T.si[:, 48:64], 511, None, AND, None, "si2", "si3")
+        cp(T.si[:, 0:16], T.t3[:, 15:L:16], "t3", "si0")
+        ts(sm("sf", 16), T.si[:, 64:80], 2.0 ** -13, None, mul, None, "si3", "sf")
+        ts(T.si[:, 24:40], T.si[:, 0:16], 511, None, AND, None, "si0", "si1")
+        gap()
+        cp(T.zl[:], T.si[:, 24:40], "si1", "zl")
+        sm("ec", 16)
+        o, i = smp["ec"][0], smp["sf"][0]
+        for a in range(4):
+            for a2 in range(4):
+                dst, src = T.sm[32 * a2:32 * a2 + 32, o + a:o + 16:4], T.sm[32 * a:32 * a + 32, i + 4 * a2:i + 4 * a2 + 4]
+                if a >= 2 and (a == 3 or a2 >= 2) and not first:
+                    cp(dst, src, "sf", "ec%d%d" % (a, a2))
+                else:
+                    act(dst, src, F_.Copy, "sf", "ec%d%d" % (a, a2))
+        act(sm("mk", 16), sm("ec", 16), ID, allec, "mk", bias=-256.5 * 2e23, scale=8192 * 2e23)
+
+    fill.extend([lambda: None, lambda: None, pick("u1", "u", T.one16[:, 0:9], "one16 one16c")])
+    z_list(T.v0[:], "v0", T.diag[:, 0:L], "diag", True)
+    tt(T.h1[:, 0:C], T.bic[:].indirect(T.posl[:, 0:22]), T.diag[:, 0:C], mul, "bic posl diag", "h1")
+    qz("o1", T.c64[:], "c64 c64x")
+    scan(T.h2[:, 0:C], T.rst[:, 0:C], T.h1[:, 0:C], 0.0, mul, mx, "rst h1", "h2")
+
+    for t in range(R):
+        last = t == R - 1
+        xn = T["xn%d" % (t + 1)]
+        for b in range(4):
+            mm(b, "e", 128 * b, "l%d" % t, 0, 2 * NA)
+        for b in range(4):
+            o = T.tw[:, PW * b + 1 + L:PW * b + 1 + L + 2 * NA]
+            if b % 2:
+                act(o, ps[b][:, 0:2 * NA], ID, "ps%d" % b, "ta%d" % b, scale=1.0 / 64)
+            else:
+                ts(o, ps[b][:, 0:2 * NA], 1.0 / 64, None, mul, None, "ps%d" % b, "ta%d" % b)
+        for b in range(4):
+            o, i = T.zt[:, b:4 * L:4], T.tw[:, PW * b:PW * b + NONE + 1].indirect(T.zl[:])
+            r = "zl twz twz2 tw%d ta%d" % (b, b)
+            if b % 2:
+                act(o, i, F_.Copy, r, "zt%d" % b)
+            else:
+                cp(o, i, r, "zt%d" % b)
+        qz("z", T.zt[:], "zt0 zt1 zt2 zt3")
+        mm(1, "z", 128, "u1", 0, 128)
+        mm(2, "u1", 16, "z", 0, 128)
+        mm(3, "u1", 16, "z", 128, 128)
+        mm(0, "z", 0, "u1", 0, 128)
+        for b in range(4):
+            mm(4 + b, "w", 128 * b, "z", 0, L, False, True)
+        sm("s", 2), sm("sa", 16)
+        if t == 0:
+            tt(T.val[:, 0:160], T.bic[:].indirect(T.posl[:, 0:10]), T.pm[:, 0:160], add, "bic posl pm", "val0")
+        tt(sm("key", 16), sm("ec", 16), sm("g8", 16), add, "g8 " + allec, "key")
+
+        def s_col(k):
+            act(smv("s", k, k + 1), ps[k][:, 16:17], ID, "ps%d live%d nb" % (k, k), "s%d" % k,
+                bias=smv("nb", k, k + 1), scale=smv("live", k, k + 1))
+
+        def a_op(k):
+            tt(smv("sa", 8 * k, 8 * k + 8), ps[k][:, 0:8], smv("mk", 8 * k, 8 * k + 8), mx, "ps%d mk" % k, "sa%d" % k)
+        s_col(1)
+        ts(T.cmp[:, 1:512:4], ps[2][:, 0:128], smv("s", 1, 2), None, A_.is_lt, None, "ps2 s1", "cm1")
+        act(T.sg[:, 128:256], ps[3][:, 0:128], F_.Sign, "ps3 s1", "sg1", bias=smv("s", 1, 2), scale=-1.0)
+        a_op(1)
+        s_col(0)
+        tt(T.cmp[:, 3:512:4], T.sg[:, 128:256], T.tau[:], A_.is_ge, "sg1 tau", "cm3")
+        act(T.sg[:, 0:128], ps[2][:, 0:128], F_.Sign, "ps2 s0", "sg0", bias=smv("s", 0, 1), scale=-1.0)
+        ts(T.cmp[:, 2:512:4], ps[3][:, 0:128], smv("s", 0, 1), None, A_.is_le, None, "ps3 s0", "cm2")
+        a_op(0)
+        tt(T.cmp[:, 0:512:4], T.sg[:, 0:128], T.tau[:], A_.is_ge, "sg0 tau", "cm0")
+        scan(sm("mi", 16), sm("r8b", 16), sm("sa", 16), 0.0, mx, mn, "r8b sa0 sa1", "mi")
+        qz("c", T.cmp[:], "cm0 cm1 cm2 cm3")
+
+        def x_copy(b):
+            w = L if last else C
+            act(xn[:, 4 + b:4 + 4 * w:4], ps[4 + b][:, 0:w], ID, "ps%d" % (4 + b), "xl%d_%d" % (t + 1, b), scale=1.0 / 64)
+        if last:
+            x_copy(0)
+        sm("nc", 16)
+        for k in range(2):
+            act(smv("nc", 8 * k, 8 * k + 8), smv("sa", 8 * k, 8 * k + 8), F_.Sign, "sa%d mi" % k, "nc%d" % k,
+                bias=smv("mi", 8 * k + 7, 8 * k + 8), scale=-1.0)
+        mm(2, "c", 0, "o1", 2, 128)
+        if last:
+            x_copy(1)
+            x_copy(2)
+            x_copy(3)
+        else:
+            x_copy(0)
+        tt(sm("w", 16), sm("key", 16), sm("nc", 16), sub, "key nc0 nc1", "w")
+        if t == 0:
+            cp(T.lini[:, 0:22], T.h2[:, 15:C:16], "h2", "lini")
+        scan(sm("wm", 16), sm("r8b", 16), sm("w", 16), 0.0, mx, mn, "r8b w", "wm")
+        tt(sm("con", 2), ps[2][:, 126:128], sm("thr", 2), A_.is_lt, "ps2 thr", "con")
+        ts(sm("wt", 2), smv("wm", 7, 16, 8), 1.5 * 2 ** 20, 1.5 * 2 ** 20, add, sub, "wm", "wt")
+        tt(sm("nam", 2), smv("wm", 7, 16, 8), sm("wt", 2), sub, "wm wt", "nam")
+        for k in range(2):
+            act(T.oh[:, 512 * k + 2 + k:512 * k + 512:4], T.negi[:], ID, "negi con", "oh%d" % (2 + k), scale=smv("con", k, k + 1))
+        for k in range(2):
+            ts(T.oh[:, k:4 * L:4], T.iot[:], smv("nam", k, k + 1), smv("con", k, k + 1), A_.is_equal, mul, "iot nam con", "oh%d" % k)
+        rx = " ".join("xl%d_%d xd%d_%d" % (t + 1, b, t + 1, b) for b in range(4))
+        if last:
+            qz("a3", xn[:, 4:4 + 4 * C], rx)
+            codes = pick("f", "a3", T.ciu[:, 0:22], "ciu")
+        else:
+            x_copy(1)
+            x_copy(2)
+            x_copy(3)
+        qz("h", T.oh[:], "oh0 oh1 oh2 oh3 ohz ohz2")
+        mm(3, "o1", 0, "h", 0, L)
+        if last:
+            codes()
+            H = C // 2
+            for k in range(2):
+                mm(k, "v", 0, "f", H * k, H)
+            tt(T.lr[:, 1:L + 1], ps[3][:, 0:L], T.lr[:, 1:L + 1], A_.is_lt, "ps3 lr", "lr")
+            for k in range(4):
+                dma("Y", T.osc[4 * k:4 * k + 4, :], T.pf[32 * k:32 * k + 4, :], "dout", 128, "pf", "")
+            dma("Y", T.oc[:], T.qf[:].bitcast(u8), "dout", 128, "qf", "")
+            for k in range(2):
+                act(T.ysb[:, H * k:H * k + H], ps[k][:, 0:H], F_.Copy, "ps%d" % k, "ysb%d" % k)
+                dma("S" if k else "Y", T.y[:, H * k:H * k + H], T.ysb[:, H * k:H * k + H], "dout", 128, "ysb%d" % k, "")
+            cp(T.olr[:], T.lr[:].indirect(T.ciu1[:, 0:22]), "lr lrz lrz2 lrz3 ciu1", "olr")
+            dma("Y", T.ol[:], T.olr[0:1, :], "dout", 128, "olr", "")
+            break
+        if t == 0:
+            tt(T.val[:, 160:C], T.bic[:].indirect(T.posl[:, 10:22]), T.pm[:, 160:C], add, "bic posl pm", "val1")
+        for k in range(2):
+            mm(k, "h", 128 * k, "o1", 0, 128)
+        tt(T.lr[:, 1:L + 1], ps[3][:, 0:L], T.lr[:, 1:L + 1], A_.is_lt, "ps3 lr", "lr")
+        tt(T.h3[:, 0:C], T.lr[:].indirect(T.lini[:, 0:22]), T.val[:], mul, "lr lrz lrz2 lrz3 lini val0 val1", "h3")
+        if t == 0:
+            act(T.diagr[:], T.t5[:], F_.Relu, "t5", "diagr", bias=1.0, scale=-1.0)
+            sset(T.diagr[:, 0:C:NA], 4, 0, "diagr")
+        for k in range(2):
+            fill.append(lambda k=k: tt(smv("live", k, k + 1), ps[k][:, 0:1], smv("live", k, k + 1), A_.is_lt, "ps%d live%d" % (k, k), "live%d" % k))
+        fill.append(lambda: ts(sm("nb", 2), sm("live", 2), -1.0, BIG, add, mul, "live0 live1", "nb"))
+        fill.append(lambda: ts(sm("thr", 2), sm("live", 2), 64 * (M - 0.5), None, mul, None, "live0 live1", "thr"))
+        compose_send(t + 1, T.h3, "h3", T.h4, "h4", xn, rx + " xz%d" % (t + 1))
+        qz("a", xn[:, 4:4 + 4 * C], rx)
+        one = unpack_state(t + 1, "a")
+        if t == 0:
+            tt(T.h1[:], T.bic[:].indirect(T.rayl[:, 0:23]), T.diagr[:], mul, "bic rayl diagr", "h1")
+            cp(T.ciu1[:, 0:22], sm("c4", 22), "c4", "ciu1")
+            scan(T.h2[:], T.rst[:], T.h1[:], 0.0, mul, mx, "rst h1", "h2")
+            fill.append(lambda: None)
+            tt(T.ml[:], T.lr[:, 1:L + 1], T.diag[:, 0:L], mul, "lr diag", "ml")
+            ts(sm("r0", 23), T.h2[:, 15:368:16], 0.0, 359.0, A_.is_equal, mul, "h2", "r0")
+            tt(sm("r1", 23), sm("r0", 23), T.h2[:, 15:368:16], add, "r0 h2", "r1")
+            cp(T.rayi[:, 0:23], sm("r1", 23), "r1", "rayi")
+        tt(T.t1[:], T.lr[:].indirect(T.rayi[:, 0:23]), T.v0[:], mul, "lr lrz lrz2 lrz3 rayi v0", "t1")
+        for b in range(4 if t == 0 else 2):
+            one(b)
+        if t:
+            fill.append(lambda: tt(T.ml[:], T.lr[:, 1:L + 1], T.diag[:, 0:L], mul, "lr diag", "ml"))
+            fill.append(lambda: (one(2), one(3)))
+            fill.append(lambda: qz("v", T.vb[:], "vb"))
+        z_list(T.t1[:], "t1", T.ml[:], "ml", False)
+
+    need("G", [("c" + e, cnt[e], {}) for e in cnt] + [("sent", R * 4 * ne, {}), ("dout", 128, {})])

@@ -4,40 +4,44 @@ from concourse.mybir import dt, AluOpType, ActivationFunctionType
 A_ = AluOpType
 F_ = ActivationFunctionType
 C, L, NA, M, R = 352, 256, 88, 40, 3
-B = float(2 ** 20)
-BIG = 1e29
+H, NC = L // 2, C // 16
+O = 2 * NA + 1
 PW = 448
-NONE = 433
+RW, LW, W = 368, 22 * 17, 384
+B = 4096.0
+BIG = 1e26
+TINY = 1e-35
+WT = 13.0 / 512
 f32, bf, i32, u16, cod, pl = "float32", "bfloat16", "int32", "uint16", "float8_e4m3fn_x4", "uint8"
 f16 = "float16"
+CYC, HOP, DMA, WAY, FIRST = 0.83e-3, 0.2, 1.8, 4.0, 8.0
+SPARE = 0.2
 
 
 def _sb(n, d):
     return ("sbuf", [128, n], d)
 
 
-SCRATCH = {"ci": _sb(8, i32), "cf": _sb(64, f32), "sm": _sb(1024, f32), "aw": _sb(24, i32), "sw": _sb(24, i32), "si": _sb(96, i32)}
-for _n in "seatu l1 posl rayl one16 ciu ciu1 piu rayi lini cl".split():
-    SCRATCH[_n] = _sb(24, u16)
-for _n in "ipos ipos2 zl".split():
-    SCRATCH[_n] = _sb(16, u16)
-for _n in "j16 cray crow t1 t2 t3 t4 t5 v0 er".split():
-    SCRATCH[_n] = _sb(368, f32)
-for _n in "jj pm rmono nrow oi cum pirow rp val olr ysb".split():
-    SCRATCH[_n] = _sb(C, f32)
-for _n in "bo bi bic".split():
-    SCRATCH[_n] = _sb(360, f32)
-for _n in "h1 h2 h3 h4".split():
-    SCRATCH[_n] = _sb(368, f16)
-for _n, _w in dict(rst=368, diag=368, diagr=368, lr=360, ml=L, xo=8 + 4 * C, ub=512, vb=512, c64=520, eb=2048, tau=128, negi=128,
-                   cst=256, iot=L, ct=512, tw=4 * PW, zt=4 * L, sg=256, cmp=512, oh=4 * L).items():
+SCRATCH = {"ci": _sb(8, i32), "cf": _sb(96, f32), "aw": _sb(24, i32), "sw": _sb(24, i32), "irow": _sb(23 * 17, f32)}
+PART = {}
+for _b, _d, _w, _names in (
+        ("offs", u16, 24, "seatu l1 posl pos2 rayl ones ciu ciu1 piu rayi lini cl0 cl1 cl2 ipos zl"),
+        ("whole", i32, 24, "s0 s1 s2 s3 s4 s5"),
+        ("small", f32, 24, "m4 b2 cw oiw e1 e2 cz c2 c3 ab2 sr e3 e4 gi sf ec idb dd mk sa pmn nn nm rs2 sc lv nb "
+                           "la lb lc ld le lf lg lh li lj lk ll"),
+        ("rows32", f32, W, "crow jj t5 t6 t7 pm olr ysb xr"),
+        ("rows16", f16, W, "h1 h2 h3 h4 h5"),
+        ("rows", bf, W, "rst diag rmono t4 a1 bo fl cum ca cs nrow pirow rp w1 w2 w3 w4 w5 w6 w7 w8 w9 w10 il g0 g1 g2 gn er t2 t3 ett et2 "
+                        "m0 m1 m2 o1 o2 nt dl n0 n1 n2 tau tat th iot sg"),
+        ("wide", bf, PW, "bc sv0 sv1 sv2")):
+    SCRATCH[_b] = _sb(_w * len(_names.split()), _d)
+    PART.update({_n: (_b, _w * _j, _w) for _j, _n in enumerate(_names.split())})
+for _n, _w in dict(xo=8 + 4 * C, ub=512, vb=512, c64=520, ea=520, eb=520, cwt=4 * L, ct=512, tw=4 * PW, zt=4 * L, cmp=512, oh=512,
+                   xn1=4 + 4 * C, xn2=4 + 4 * C, xn3=4 + 4 * C).items():
     SCRATCH[_n] = _sb(_w, bf)
-SCRATCH["et"], SCRATCH["ett"] = _sb(L, f32), _sb(L, f32)
-for _n, _w in dict(x=C, u=128, u1=144, v=128, w=512, e=512, o1=130, z=L, c=128, h=L, a0=C, a=C, a3=C, f=C, m0=128, m1=128, m2=128,
+for _n, _w in dict(x=C, u=128, u1=128, v=128, w=512, e=512, k=L, z=L, c=128, h=128, a0=C, a=C, a3=C, f=C, m0=128, m1=128, m2=128,
                    r0=NA, r1=NA, r2=NA, l0=2 * NA, l1=2 * NA, l2=2 * NA).items():
     SCRATCH["q" + _n], SCRATCH["p" + _n] = _sb(_w, cod), _sb(_w, pl)
-for _t in range(R):
-    SCRATCH["xn%d" % (_t + 1)] = _sb(4 + 4 * C, bf)
 for _b in range(8):
     SCRATCH["bank%d" % _b] = ("psum", [128, 512], f32)
 
@@ -83,6 +87,27 @@ def _relay_program(g, core, T, topo):
             g.wait_ge(T.sem.sent, R * nout)
 
 
+def _order(calls):
+    for c in reversed(calls):
+        c["chain"] = (min(x[0] for x in c["ways"].values()) + c["late"] + c.get("early", 0.0)
+                      + max([HOP + x["chain"] for x in c["next"]], default=0.0))
+    busy = {}
+    for c in sorted(calls, key=lambda c: (-c["chain"], c["n"])):
+        best = None
+        for e, (us, _) in c["ways"].items():
+            t = max([x["end"] + (0.0 if e == "T" == x["e"] else HOP) for x in c["deps"]], default=0.0)
+            for a, b in busy.get(e, []):
+                if t + us <= a:
+                    break
+                t = max(t, b)
+            if best is None or t + us + SPARE < best[0] + best[2]:
+                best = t, e, us
+        c["start"], c["e"] = best[0], best[1]
+        c["end"] = best[0] + best[2] + c["late"]
+        busy[c["e"]] = sorted(busy.get(c["e"], []) + [(best[0], best[0] + best[2])])
+    return sorted(calls, key=lambda c: (c["start"], c["n"]))
+
+
 def rank_program(g, core, T, topo):
     rank = T.rank_of(core)
     if rank is None:
@@ -90,9 +115,490 @@ def rank_program(g, core, T, topo):
         return
     V, S, P, Y = g.vector, g.scalar, g.tensor, g.sync
     Q = {"V": V, "S": S, "T": P, "G": g, "Y": Y}
+    calls = []
+    seen = {}
+
+    def v(n, a=0, b=None, s=1, p=(0, 128)):
+        if n in PART:
+            n, j, w = PART[n]
+            a, b = j + a, j + (w if b is None else b)
+        b = SCRATCH[n][1][1] if b is None else b
+        cols = range(a, b, s)
+        return T[n][p[0]:p[1], a:b:s], [(n, p[0], p[1], -1 if n.startswith("bank") else _mask(cols))], len(cols)
+
+    def words(w):
+        return w[0].bitcast(dt.uint32), w[1], w[2]
+
+    def ix(w, off):
+        return w[0].indirect(off[0]), w[1] + off[1], 16 * off[2]
+
+    def call(ways, outs, ins, tok=None, late=0.0):
+        r = [x for i in ins if isinstance(i, tuple) for x in i[1]] + [x for o in outs for x in o[1][1:]]
+        w = [o[1][0] for o in outs]
+        c = {"ways": ways, "tok": tok, "late": late, "n": len(calls), "deps": [], "next": []}
+        for regs, writes in ((r, False), (w, True)):
+            for n, a, b, bits in regs:
+                for x in seen.get(n, []):
+                    other = n.startswith("bank") and (len(ways) > 1 or list(ways) != list(x[3]["ways"]))
+                    if (writes or x[4] or other) and x[0] < b and a < x[1] and x[2] & bits and all(x[3] is not d for d in c["deps"]):
+                        c["deps"].append(x[3])
+                        x[3]["next"].append(c)
+        for n, a, b, bits in w:
+            seen[n] = [x for x in seen.get(n, []) if not (a <= x[0] and x[1] <= b and x[2] & ~bits == 0)] + [(a, b, bits, c, True)]
+        for n, a, b, bits in r:
+            seen.setdefault(n, []).append((a, b, bits, c, False))
+        calls.append(c)
+
+    def cost(out, ins, per=None):
+        if len(out[1]) > 1:
+            return 0.05 + 3.5 * CYC * out[2]
+        if len(ins[0][1]) > 1:
+            return 0.06 + 1.5 * CYC * out[2]
+        if per is None:
+            per = 0.5 if all(SCRATCH[x[1][0][0]][2] in (bf, f16, u16) for x in [out] + ins) else 1.0
+        return CYC * max(64, per * out[2])
+
+    names = {}
+
+    def k(n):
+        j = names.setdefault(n, len(names))
+        return v("cf", j, j + 1)
+
+    def arg(x):
+        return k(x) if isinstance(x, str) else x
+
+    def ap(x):
+        return x[0] if isinstance(x, tuple) else x
+
+    def load(e, out, in_, sem, total, late=DMA):
+        call({e: (0.05, lambda: Q[e].dma_start(out[0], in_).then_inc(T.sem[sem], 16))}, [out], [], (sem, total), late)
+
+    def store(e, out, in_, late):
+        call({e: (0.05, lambda: Q[e].dma_start(out, in_[0]).then_inc(T.sem.dout, 16))}, [], [in_], ("dout", 128), late)
+
+    def ts_way(out, a, s1, o0, s2, o1):
+        if o1 is None:
+            return cost(out, [a]), lambda: V.tensor_scalar(out[0], a[0], ap(s1), None, o0)
+        return cost(out, [a]), lambda: V.tensor_scalar(out[0], a[0], ap(s1), ap(s2), o0, o1)
+
+    def act_way(out, a, f, scale, bias):
+        if f == F_.Copy:
+            return cost(out, [a], 1.0) + 0.02, lambda: S.activation(out[0], a[0], f)
+        return cost(out, [a], 1.0) + 0.02, lambda: S.activation(out[0], a[0], f, bias=ap(bias), scale=ap(scale))
+
+    def ts(out, a, s1, o0, s2=None, o1=None):
+        s1, s2 = arg(s1), arg(s2)
+        call({"V": ts_way(out, a, s1, o0, s2, o1)}, [out], [a, s1, s2])
+
+    def act(out, a, f=F_.Identity, scale=1.0, bias=0.0):
+        scale, bias = arg(scale), arg(bias)
+        call({"S": act_way(out, a, f, scale, bias)}, [out], [a, scale, bias])
+
+    def aff(out, a, scale=1.0, bias=0.0):
+        scale, bias = arg(scale), arg(bias)
+        call({"S": act_way(out, a, F_.Identity, scale, bias), "V": ts_way(out, a, scale, mul, bias, add)}, [out], [a, scale, bias])
+
+    def move(out, a):
+        call({"S": act_way(out, a, F_.Copy, 1.0, 0.0), "V": (cost(out, [a]), lambda: V.tensor_copy(out[0], a[0]))}, [out], [a])
+
+    def tt(out, a, b, o):
+        per = 1.0 if a[1][0][0].startswith("bank") else 2.0
+        call({"V": (cost(out, [a], per), lambda: V.tensor_tensor(out[0], a[0], b[0], o))}, [out], [a, b])
+
+    def cp(out, a):
+        call({"V": (cost(out, [a]), lambda: V.tensor_copy(out[0], a[0]))}, [out], [a])
+
+    def scan(out, a, b, o0, o1, init=0.0):
+        call({"V": (cost(out, [a, b]), lambda: V.tensor_tensor_scan(out[0], a[0], b[0], init, o0, o1))}, [out], [a, b])
+
+    def turn(out, a):
+        call({"V": (cost(out, [a]), lambda: V.transpose(out[0], a[0]))}, [out], [a])
+
+    def mset(out, x):
+        call({"V": (cost(out, [out]), lambda: V.memset(out[0], x))}, [out], [])
+
+    def qz(n, t, a=0, b=None):
+        q, p = v("q" + n, a, b), v("p" + n, a, b)
+        call({"V": (0.012 + 0.22e-3 * t[2], lambda: V.quantize_mx(q[0], p[0], t[0]))}, [q, p], [t])
+
+    def ps(b, a=0, e=512, s=1):
+        return v("bank%d" % b, a, e, s)
+
+    def mm(b, l, l0, rr, r0, n, start=True, stop=True):
+        x = [v("q" + l, l0, l0 + 128), v("p" + l, l0, l0 + 128), v("q" + rr, r0, r0 + n), v("p" + rr, r0, r0 + n)]
+        o = ps(b, 0, n)
+        call({"T": (1.25 * CYC * (n + 16), lambda: P.matmul_mx(o[0], x[0][0], x[1][0], x[2][0], x[3][0], start, stop))}, [o], x)
+
+    def pick(to, fr, off):
+        act(v("p" + to), ix(v("p" + fr), off), F_.Copy)
+        cp(words(v("q" + to)), ix(words(v("q" + fr)), off))
+
+    def iota(out, pat, base=0):
+        call({"G": (0.13 + 2 * CYC * out[2], lambda: g.iota(out[0], pat, base, 0, allow_small_or_imprecise_dtypes=True))}, [out], [])
+
+    def select(out, a, pat, o, base, ch):
+        call({"G": (0.17 + 2 * CYC * out[2], lambda: g.affine_select(out[0], a[0], pat, o, 0.0, base, ch))}, [out], [a])
+
+    def col(n, a, scale=1.0, bias=0.0):
+        aff(k(n), k(a), scale, bias)
+
+    def relu(n, a, scale):
+        act(k(n), k(a), F_.Relu, scale)
+
+    def table(off, row, n, w, scale, bias):
+        scan(v(w, 0, 16 * n), v("rst", 0, 16 * n), v(row, 0, 16 * n), mul, add)
+        ts(v(off, 0, n), v(w, 15, 16 * n, 16), scale, mul, bias, add)
+
+    add, sub, mul, mx, mn = A_.add, A_.subtract, A_.mult, A_.max, A_.min
+    AND, SHR = A_.bitwise_and, A_.logical_shift_right
+
+    for j in range(8):
+        load("Y" if j % 2 else "S", v("aw", 0, NC, 1, (16 * j, 16 * j + 16)), T.alive[:], "dal", 128)
+    load("Y", v("sw", 0, NC), T.seat[:], "dse", 16)
+    load("Y", v("xo", 8, 8 + 4 * C), T.x[:], "dx", 16, 2 * DMA)
+    load("Y", v("ub"), T.u[:], "du", 16, 2 * DMA)
+    load("Y", (T.qw[:].bitcast(dt.uint8),) + v("qw")[1:], T.wc[:], "dw", 32, 3 * DMA)
+    load("Y", v("pw"), T.ws[:], "dw", 32, 3 * DMA)
+    load("Y", v("vb"), T.v[:], "dv", 16, 3 * DMA)
+    loads = len(calls)
+
+    pi = v("ci", 5, 6)
+    call({"G": (0.13, lambda: g.iota(pi[0], [[0, 1]], 0, 1))}, [pi], [])
+    iota(v("b2", 0, NC), [[2, 11], [0, 2]])
+    iota(v("m4"), [[4, 24]])
+    iota(v("jj"), [[0, 24], [4096, 4], [512, 4]])
+    iota(v("crow", 0, C), [[1, C]])
+    iota(v("irow"), [[0, 23], [1, 17]])
+    iota(v("iot", 0, L), [[1, H], [H, 2]], 1)
+    mset(v("c64"), 64.0)
+    calls[-1]["early"] = 2 * FIRST
+    for n, b in (("ea", 2), ("eb", 3)):
+        select(v(n, 0, 514), v("c64", 0, 514), [[1, 514]], A_.is_equal, -b, -4)
+    for b in range(4):
+        qz("e", v("eb" if b % 2 else "ea", 2 - b // 2 * 2, 514 - b // 2 * 2), 128 * b, 128 * b + 128)
+    for j in range(8):
+        mset(v("cwt", 512 * (j // 4) + j % 4, 512 * (j // 4) + 512, 4), WT if j // 4 == j % 4 // 2 else 0.0)
+    qz("k", v("cwt"))
+    for t in range(R):
+        mset(v("sv%d" % t, 0, O + 1), 1.0)
+        mset(v("sv%d" % t, O + 1 + L, O + 2 + L), 0.0)
+    select(v("tau", 0, H), v("sv0", 0, H), [[-1, H]], A_.is_ge, 0, 1)
+    aff(v("tat", 0, H), v("tau", 0, H), -TINY, TINY)
+    mset(v("rst"), 1.0)
+    mset(v("rst", 0, W, 16), 0.0)
+    for n, a, b, s, x in (("xo", 0, 8, 1, 0.0), ("xn1", 0, 4, 1, 0.0), ("xn2", 0, 4, 1, 0.0), ("ct", 4 * NA, 512, 1, 0.0),
+                          ("bo", C, C + 8, 1, -B), ("bc", C, PW, 93, 0.0), ("tw", 0, 4 * PW, PW, 0.0), ("tw", O, 4 * PW, PW, 0.0),
+                          ("ones", 0, 8, 1, 1), ("idb", 0, 24, 1, 0.0), ("sa", 0, 11, 10, BIG), ("sa", 9, 10, 1, 100 * BIG),
+                          ("rs2", 0, 24, 1, -100 * BIG), ("rs2", 9, 10, 1, 100 * BIG), ("pmn", 0, 1, 1, 100 * BIG)):
+        mset(v(n, a, b, s), x)
+    for j, n in enumerate(("q", "g", "q4", "t4", "go")):
+        k(n)
+    ts(v("ci", 0, 1), pi, 15, AND)
+    ts(v("ci", 1, 2), pi, 4, SHR)
+    ts(v("ci", 2, 3), pi, 2, SHR, 3, AND)
+    ts(v("ci", 3, 4), pi, 3, AND)
+    ts(v("ci", 4, 5), pi, 4, SHR, 1, AND)
+    cp(v("cf", 0, 5), v("ci", 0, 5))
+    ts(k("up"), pi, 16.0 * 3, A_.is_lt)
+    ts(k("lo"), pi, 16.0 * 4, A_.is_lt, 3.0, add)
+    ts(k("dy"), pi, 16.0 * 5, A_.is_ge, "up", sub)
+    ts(k("gp"), k("g"), "lo", sub)
+    col("dx", "dy", -3.0, "gp")
+    col("vert", "dy", "dy")
+    col("hz", "vert", -1.0, 1.0)
+    col("hd", "dx", "hz")
+    col("ndy", "dy", -1.0)
+    col("ndx", "dx", -1.0)
+    col("v4", "vert", 4.0)
+    relu("neg", "dx", -1.0)
+    relu("pos", "dx", 1.0)
+    relu("dn", "dy", 3.0)
+    col("j0", "q4", 4096.0)
+    col("jq", "t4", 512.0, "j0")
+    col("nq", "jq", -1.0)
+    col("rq", "jq", 2000.0, 5e5)
+    act(v("t6"), v("jj"), F_.Abs, bias="nq")
+    act(v("diag"), v("t6"), F_.Relu, -1.0, 1.0)
+    aff(v("rmono", 0, C), v("jj", 0, C), -2000.0, "rq")
+    aff(v("m0", 0, L), v("diag", 0, L), -1.0)
+
+    rel = _relays(T, topo, rank)
+    eng = topo.engines(core, rel[0][0])
+    ne = len(eng) // 2
+    narr = sum(len(topo.engines(c, core)) for r2 in range(len(T.cores)) for c, d, _ in _relays(T, topo, r2) if d == rank)
+
+    def both(out, win, off, bias=None):
+        for a, b, one in ((0, 12, cp), (12, NC, None)):
+            o, i = v(out, 16 * a, 16 * b), ix(win, v(off, a, b))
+            if bias is None:
+                cp(o, i) if one else act(o, i, F_.Copy)
+            else:
+                ts(o, i, bias, add) if one else act(o, i, bias=bias)
+
+    def compose_send(t, xbuf):
+        both("ct", v(xbuf), "cl%d" % t)
+        qz("m%d" % t, v("ct"))
+
+        def send():
+            for codes in (True, False):
+                trs = []
+                for j, (c, d, cs) in enumerate(rel):
+                    if cs == codes:
+                        rid, pid = topo.addr(c, core)
+                        src = T["qm%d" % t][:, 0:NA].bitcast(dt.uint8) if codes else T["pm%d" % t][:, 0:NA]
+                        dst = T["qr%d" % t][:].bitcast(dt.uint8) if codes else T["pr%d" % t][:]
+                        trs.append(RemoteDMATransfer(dst_ids=[DstId(rid=rid, pnc=pid)], dma_engine_mask=_mask(eng[j % 2::2]),
+                                                     remote_sem=T.sem["rel%d" % t], src=src, dst=dst))
+                g.remote_dma_fused(trs, local_sem=T.sem.sent)
+        call({"G": (1.0 if t else 3.0, send)}, [v("ql%d" % t), v("pl%d" % t)], [v("qm%d" % t), v("pm%d" % t)], ("arr%d" % t, narr),
+             WAY if t else FIRST)
+
+    col("cq", "q", 1.0, B - 176.0)
+    aff(v("cw", 0, NC), v("m4", 0, NC), 4.0, "cq")
+    ts(v("l1", 0, NC), v("b2", 0, NC), "go", add)
+    tt(v("oiw", 0, NC), v("aw", 0, NC), v("cw", 0, NC), mul)
+    cp(v("seatu", 0, NC), v("sw", 0, NC))
+    both("t4", v("oiw", 0, NC), "l1", -B)
+    turn(v("a1", 0, C), v("t4", 0, C))
+    both("bo", v("a1", 0, C), "seatu")
+    col("u3", "t4", -1.0, 3.0)
+    col("y1", "t4", 88.0, -132.0)
+    col("y2", "y1", "ndy", 132.0)
+    col("w1", "dx", "u3", "q4")
+    col("pb", "w1", 1.0, "y2")
+    ts(k("b0"), k("w1"), 0.0, A_.is_lt, 1000.0, mul)
+    ts(k("b1"), k("w1"), 3.0, A_.is_gt, 1000.0, mul)
+    ts(k("b2"), k("b1"), NA - 4.0, add, "pb", add)
+    ts(v("posl", 1, NC - 1), v("m4", 1, NC - 1), "pb", add)
+    ts(v("posl", 0, 1), k("b0"), "pb", add, float(C), mn)
+    ts(v("posl", NC - 1, NC), k("b2"), float(C), mn)
+    col("pk", "q4", -4096.0, -1536.0)
+    act(v("t5", 0, C), v("jj", 0, C), F_.Abs, bias="pk")
+    aff(v("pm", 0, C), v("t5", 0, C), -1.0, 1536.0 + O + 1)
+    tt(v("h1", 0, C), ix(v("bo", 0, C + 8), v("posl", 0, NC)), v("pm", 0, C), add)
+    scan(v("h2", 0, C), v("rst", 0, C), v("h1", 0, C), mul, mx)
+    cp(v("s0", 0, NC), v("h2", 15, C, 16))
+    ts(v("s1", 0, NC), v("s0", 0, NC), 511, AND)
+    ts(v("cl0", 0, NC), v("s1", 0, NC), 4.0, mul, "t4", add)
+    compose_send(0, "xo")
+
+    ts(v("fl", 0, C), v("a1", 0, C), -1000.0, A_.is_gt)
+    scan(v("cum", 0, C), v("fl", 0, C), v("fl", 0, C), add, mx)
+    scan(v("ca", 0, C), v("cum", 0, C), v("fl", 0, C), mx, mul)
+    act(v("bc", 0, C), ix(v("ca", 0, C), v("seatu", 0, NC)), F_.Copy)
+    scan(v("w1", 0, C), v("rmono", 0, C), v("cum", 0, C), mx, mn)
+    aff(v("e1", 0, NC), v("cw", 0, NC), 1.0, 176.0 + L + 1 - B)
+    ts(v("e2", 0, NC), v("aw", 0, NC), 0.0, A_.is_equal)
+    tt(v("cz", 0, NC), v("e1", 0, NC), v("e2", 0, NC), mul)
+    tt(v("c2", 0, NC), v("cz", 0, NC), v("w1", 15, C, 16), sub)
+    tt(v("c3", 0, NC), v("c2", 0, NC), v("w1", 15, C, 16), mx)
+    ts(v("ciu", 0, NC), v("c3", 0, NC), -1.0, add)
+    ts(v("ciu1", 0, NC), v("c3", 0, NC), L + 1.0, mn, float(O), add)
+    aff(v("cs", 0, C), v("crow", 0, C), 1.0, -176.0)
+    cp(ix(v("pirow", 0, C), v("ciu", 0, NC)), v("cs", 0, C))
+    scan(v("w2", 0, C), v("rmono", 0, C), v("pirow", 0, C), mx, mn)
+    ts(v("piu", 0, NC), v("w2", 15, C, 16), 176.0, add)
+    qz("x", v("xo", 8, 8 + 4 * C))
+    pick("a0", "x", v("piu", 0, NC))
+    qz("u", v("ub"))
+    pick("u1", "u", v("ones", 0, 8))
+    qz("v", v("vb"))
+
+    def unpack_state(t, n):
+        w = C if t == R - 1 else L
+        for b in range(4):
+            mm(b, "e", 128 * b, n, 0, w)
+        for b in range(4):
+            mm(4 + b, "e", 128 * b, n, 0, C + L - w, True, False)
+        for b in range(4):
+            aff(v("tw", PW * b + O + 1, PW * b + O + 1 + L), ps(b, 0, L), 1.0 / 64)
+            if w == C:
+                aff(v("xn%d" % (t + 1), 4 + 4 * L + b, 4 + 4 * C, 4), ps(b, L, C), 1.0 / 64)
+
+    unpack_state(0, "a0")
+
+    col("d", "t4", 1.0, -1.0)
+    relu("hd0", "d", -1.0)
+    col("d15", "t4", 88.0, -220.0)
+    col("q176", "q", -1.0, 176.5)
+    col("q353", "q4", 1.0, C + 1.0)
+    col("n3", "neg", -3.0, "q4")
+    col("slope", "hd", -16.0, "v4")
+    col("r88", "d15", "ndy", 132.0)
+    col("sH", "hd", "q176")
+    col("po", "ndx", "d", "n3")
+    col("off", "hd0", 1.0, "hz")
+    col("sH2", "hz", 175.5, "sH")
+    col("po1", "po", 1.0, -43.5)
+    col("po2", "po", 1.0, "r88")
+    col("df", "po2", -1.0, "q353")
+    col("lim", "off", -1e6, -88000.0)
+    col("po3", "df", "hd0", "po2")
+    col("sA", "po3", "vert", "sH2")
+    act(v("ab2", 0, 23), v("m4", 0, 23), F_.Abs, bias="po1")
+    act(v("e3", 0, 23), v("ab2", 0, 23), F_.Relu, 2000.0, "lim")
+    aff(v("sr", 0, 23), v("crow", 0, 23), "slope", "sA")
+    tt(v("e4", 0, 23), v("e3", 0, 23), v("sr", 0, 23), add)
+    ts(v("rayl", 0, 23), v("e4", 0, 23), C + 93.0, mn)
+    col("cH", "neg", -3.0, "dx")
+    col("bs", "dy", 44.0, -132.0)
+    col("cH3", "cH", 1.0, "bs")
+    col("nneg", "neg", -1.0, 1.0)
+    col("npos", "pos", -1.0, 1.0)
+    for n in ("neg", "pos", "nneg", "hz"):
+        col(n + "O", n, -float(O))
+    aff(v("w3", 0, 92), v("crow", 0, 92), 1.0, "cH3")
+    for a, b, s1, s2 in ((0, 4, "nneg", "negO"), (4, 87, 1.0, 0.0), (87, 88, "npos", "posO"), (88, 92, "neg", "nnegO")):
+        aff(v("bc", C + 1 + a, C + 1 + b), v("w3", a, b), s1, s2)
+    act(v("g0", 0, RW), ix(v("bc", 0, C + 94), v("rayl", 0, 23)), F_.Copy)
+    aff(v("g0", 0, C, NA), v("g0", 0, C, NA), "vert", "hzO")
+    ts(v("h3", 0, RW), v("g0", 0, RW), -float(L), add)
+    scan(v("h4", 0, RW), v("diag", 0, RW), v("h3", 0, RW), mx, mul)
+    table("rayi", "h4", 23, "h5", 1.0, float(O + L))
+    col("k41", "dx", 4.0, 1.0)
+    col("n12", "neg", 12.0)
+    relu("g4", "hd", 351.0)
+    col("g5", "g4", 1.0, -184.0)
+    col("alpha", "hd", -1.0, "v4")
+    col("h88", "hd", -88.0)
+    col("beta", "k41", "ndy", "h88")
+    col("g1", "n12", "vert", "g5")
+    col("gam", "k41", "dn", "g1")
+    aff(v("gi", 0, 4), v("crow", 0, 4), "beta", "gam")
+    for i in range(4):
+        aff(v("nrow", NA * i, NA * i + NA), v("crow", 0, NA), "alpha", v("gi", i, i + 1))
+    cp(ix(v("rp", 0, C), v("seatu", 0, NC)), v("nrow", 0, C))
+    tt(v("w6", 0, L), ix(v("rp", 0, C), v("piu", 0, 16)), v("diag", 0, L), mul)
+    table("ipos", "w6", 16, "w7", 1.0, 184.0)
+
+    def z_list(t):
+        gt = v("g%d" % t, 0, RW)
+        ts(v("gn", 0, RW), gt, 0.0, A_.is_equal)
+        scan(v("er", 0, RW), v("gn", 0, RW), gt, mul, add)
+        tt(v("t2", 0, L), ix(v("er", 0, RW), v("ipos", 0, 16)), v("m%d" % t, 0, L), mul)
+        table("zl", "t2", 16, "t3", -1.0, float(O))
+        turn(v("ett", 0, L), v("t2", 0, L))
+        scan(v("et2", 0, L), v("rst", 0, L), v("ett", 0, L), mul, add)
+        for h in range(2):
+            aff(v("sf", h, 16, 2), v("et2", H * h + 15, H * h + H, 16), -1.0)
+        for a in range(4):
+            for a2 in range(4):
+                move(v("ec", 4 * a, 4 * a + 4, 1, (32 * a2, 32 * a2 + 32)), v("sf", 4 * a2, 4 * a2 + 4, 1, (32 * a, 32 * a + 32)))
+        for h in range(2):
+            move(v("idb", 1 + 10 * h, 9 + 10 * h), v("ec", h, 16, 2))
+            aff(v("mk", 1 + 10 * h, 9 + 10 * h), v("ec", h, 16, 2), -20 * BIG, 10 * BIG)
+        tt(v("dd", 0, 19), v("idb", 0, 19), v("idb", 1, 20), sub)
+        ts(v("lv", 0, 2), v("ec", 0, 2), 0.0, A_.not_equal)
+        ts(v("nb", 0, 2), v("ec", 0, 2), 0.0, A_.is_equal, -BIG, mul)
+        aff(v("th", 0, H), v("tat", 0, H), 1.0, v("nb", 1, 2))
+
+    z_list(0)
+
+    col("q1", "q", 1.0, -1.0)
+    col("dn88", "dn", 88.0)
+    col("ndy88", "ndy", 88.0)
+    col("dx3", "dx", 3.0)
+    col("q25", "q4", -4.0, -2.5)
+    aff(v("la"), v("m4"), 4.0, "q1")
+    ts(v("s2"), v("la"), 1.0 / 17, mul, 1.0 / 17 - 0.47, add)
+    tt(v("s3"), v("la"), v("s2"), sub)
+    ts(v("lb"), v("s2"), 16.0, mul)
+    ts(v("s4"), v("s3"), 2, SHR)
+    ts(v("s5"), v("s3"), 3, AND)
+    tt(v("lc"), v("s3"), v("lb"), A_.is_lt)
+    ts(v("ld"), v("s5"), "ndx", mul, "dx3", add)
+    ts(v("le"), v("s5"), "ndy88", mul, "dn88", add)
+    tt(v("lf"), v("ld"), v("s4"), add)
+    act(v("lg"), v("lf"), F_.Abs, bias=-43.5)
+    act(v("lh"), v("lg"), F_.Relu, 2000.0, -88000.0)
+    aff(v("li"), v("lc"), 1000.0)
+    tt(v("lj"), v("lf"), v("le"), add)
+    tt(v("lk"), v("lj"), v("li"), add)
+    tt(v("ll"), v("lk"), v("lh"), add)
+    ts(v("pos2"), v("ll"), float(C), mn)
+    act(v("t7"), v("irow", 0, W), F_.Abs, bias="q25")
+    act(v("nt"), v("t7"), F_.Relu, -1.0, 2.0)
+    act(v("il"), ix(v("bc", 0, C + 1), v("pos2")), scale=-4.0)
+    scan(v("w10"), v("nt"), v("il"), mx, mul)
+    scan(v("w8"), v("diag"), v("il"), mx, mul)
+    act(v("n0"), v("w10"), F_.Relu, 1.0, 1.0)
+    mset(v("n0", 0, W, 17), 0.0)
+    tt(v("dl", 0, LW), v("il", 1, LW + 1), v("il", 0, LW), sub)
+    table("lini", "w8", 24, "w9", -0.25, float(O))
+
+    for t in range(R):
+        last = t == R - 1
+        xn, sv = "xn%d" % (t + 1), "sv%d" % t
+        for b in range(4):
+            mm(b, "e", 128 * b, "l%d" % t, 0, 2 * NA)
+        for b in range(4):
+            aff(v("tw", PW * b + 1, PW * b + O), ps(b, 0, 2 * NA), 1.0 / 64)
+        for h in range(2):
+            for b in range(4):
+                move(v("zt", 512 * h + b, 512 * h + 512, 4), ix(v("tw", PW * b, PW * b + O + 1 + L), v("zl", 8 * h, 8 * h + 8)))
+            qz("z", v("zt", 512 * h, 512 * h + 512), H * h, H * h + H)
+            calls[-1]["early"] = 0.5 * (1 - h)
+            mm(2 - h, "u1", 0, "z", H * h, H)
+            mm(3 * h, "z", H * h, "u", 0, H)
+        for b in range(4):
+            mm(4 + b, "w", 128 * b, "z", 0, L, False, True)
+            w = L if last else C
+            aff(v(xn, 4 + b, 4 + 4 * w, 4), ps(4 + b, 0, w), 1.0 / 64)
+        act(v("sc", 0, 1), ps(0, 1, 2), scale=v("lv", 0, 1), bias=v("nb", 0, 1))
+        act(v("sg", 0, H), ps(2, 0, H), F_.Sign, -1.0, v("sc", 0, 1))
+        tt(v("cmp", 0, 512, 4), v("sg", 0, H), v("tau", 0, H), A_.is_ge)
+        ts(v("cmp", 2, 512, 4), ps(1, 0, H), v("sc", 0, 1), A_.is_le)
+        ts(v("sg", H, L), ps(1, 0, H), ps(3, 1, 2), sub)
+        tt(v("cmp", 3, 512, 4), v("sg", H, L), v("th", 0, H), A_.is_lt)
+        ts(v("cmp", 1, 512, 4), ps(2, 0, H), ps(3, 1, 2), A_.is_lt, v("lv", 1, 2), mul)
+        qz("c", v("cmp"))
+        for h in range(2):
+            tt(v("sa", 1 + 10 * h, 9 + 10 * h), ps(3 * h, 0, H, 16), v("mk", 1 + 10 * h, 9 + 10 * h), mx)
+        scan(v("pmn", 1, 20), v("rs2", 0, 19), v("sa", 0, 19), mx, mn, 100 * BIG)
+        tt(v("nn", 0, 19), v("sa", 0, 19), v("pmn", 0, 19), A_.is_ge)
+        scan(v("nm", 0, 19), v("nn", 0, 19), v("dd", 0, 19), mul, add)
+        mm(2, "c", 0, "k", H // 2, H)
+        for h in range(2):
+            mm(3 * h, "k", H * h, "c", 0, H)
+            act(v("xr", H * h, H * h + H), ps(3 * h, 0, H), F_.Relu, -1024.0, 1024.0)
+            ts(v("oh", h, 512, 2), v("iot", 0, L), v("nm", 8 + 10 * h, 9 + 10 * h), A_.is_equal,
+               ps(2, H // 2 - 1 + h, H // 2 + h), A_.is_gt)
+        qz("h", v("oh"))
+        for h in range(2):
+            mm(1 + h, "k", H * h, "h", 0, H)
+            tt(v(sv, O + 1 + H * h, O + 1 + H * h + H), ps(1 + h, 0, H), v("xr", H * h, H * h + H), A_.is_le)
+        win = v(sv, 0, O + 2 + L)
+        if last:
+            break
+        tt(v("n%d" % (t + 1)), ix(win, v("lini")), v("n%d" % t), A_.is_le)
+        scan(v("w1", 0, LW), v("n%d" % (t + 1), 0, LW), v("dl", 0, LW), mul, add)
+        ts(v("cl%d" % (t + 1), 0, NC), v("w1", 16, LW, 17), "t4", add)
+        compose_send(t + 1, xn)
+        qz("a", v(xn, 4, 4 + 4 * C))
+        unpack_state(t + 1, "a")
+        tt(v("g%d" % (t + 1), 0, RW), ix(win, v("rayi", 0, 23)), v("g%d" % t, 0, RW), mul)
+        scan(v("m%d" % (t + 1), 0, L), v(sv, O + 1, O + 1 + L), v("m%d" % t, 0, L), mx, mul)
+        z_list(t + 1)
+        if t == 0:
+            act(v("o1", 0, C), ix(win, v("ciu1", 0, NC)), F_.Copy)
+        else:
+            tt(v("o2", 0, C), ix(win, v("ciu1", 0, NC)), v("o1", 0, C), mul)
+
+    tt(v("olr", 0, C), ix(win, v("ciu1", 0, NC)), v("o2", 0, C), mul)
+    store("Y", T.ol[:], v("olr", 0, C, 1, (0, 1)), DMA)
+    qz("a3", v(xn, 4, 4 + 4 * C))
+    pick("f", "a3", v("ciu", 0, NC))
+    store("Y", T.oc[:], (T.qf[:].bitcast(dt.uint8),) + v("qf")[1:], DMA + 0.6)
+    for j in range(4):
+        store("Y", T.osc[4 * j:4 * j + 4, :], v("pf", 0, C, 1, (32 * j, 32 * j + 4)), DMA)
+    for j in range(2):
+        a, b = C // 2 * j, C // 2 * (j + 1)
+        mm(4 + j, "v", 0, "f", a, C // 2)
+        move(v("ysb", a, b), ps(4 + j, 0, C // 2))
+        store("S" if j else "Y", T.y[:, a:b], v("ysb", a, b), DMA + 0.3)
+
     cnt = {"V": 0, "S": 0, "T": 0, "G": 0}
-    know = {k: {} for k in Q}
-    lastw, reads = {}, {}
+    know = {e: {} for e in Q}
 
     def need(e, toks):
         want = {}
@@ -104,526 +610,19 @@ def rank_program(g, core, T, topo):
             if know[e].get(s, 0) < n:
                 Q[e].wait_ge(T.sem[s], n)
                 know[e][s] = n
-                for k, v in snap.items():
-                    if know[e].get(k, 0) < v:
-                        know[e][k] = v
+                for j, x in snap.items():
+                    if know[e].get(j, 0) < x:
+                        know[e][j] = x
 
-    def deps(e, r, w):
-        toks = [lastw[k] for k in list(r) + list(w) if k in lastw]
-        for k in w:
-            toks += reads.get(k, [])
-        if e == "T":
-            toks = [x for x in toks if x[0] != "cT"]
-        need(e, toks)
-
-    def done(tok, r, w):
-        for k in r:
-            reads.setdefault(k, []).append(tok)
-        for k in w:
-            lastw[k] = tok
-            reads[k] = []
-
-    def op(e, fn, r, w):
-        r, w = r.split(), w.split()
-        w = w + [k for k in r if k.startswith("ps")]
-        deps(e, r, w)
-        cnt[e] += 1
-        fn().then_inc(T.sem["c" + e], 1)
-        done(("c" + e, cnt[e], dict(know[e])), r, w)
-
-    def dma(e, out, in_, sem, total, r, w):
-        r, w = r.split(), w.split()
-        deps(e, r, [])
-        Q[e].dma_start(out, in_).then_inc(T.sem[sem], 16)
-        done((sem, total, {}), r, w)
-
-    def ts(out, in0, s1, s2, o0, o1, r, w):
-        if o1 is None:
-            op("V", lambda: V.tensor_scalar(out, in0, s1, None, o0), r, w)
+    order = _order(calls)
+    for c in calls[:loads] + [c for c in order if c["n"] >= loads]:
+        e = c["e"]
+        need(e, [d["done"] for d in c["deps"] if not e == "T" == d["e"]])
+        if c["tok"]:
+            c["ways"][e][1]()
+            c["done"] = c["tok"] + ({},)
         else:
-            op("V", lambda: V.tensor_scalar(out, in0, s1, s2, o0, o1), r, w)
-
-    def tt(out, a, b, o, r, w):
-        op("V", lambda: V.tensor_tensor(out, a, b, o), r, w)
-
-    def cp(out, a, r, w):
-        op("V", lambda: V.tensor_copy(out, a), r, w)
-
-    def scan(out, a, b, init, o0, o1, r, w):
-        op("V", lambda: V.tensor_tensor_scan(out, a, b, init, o0, o1), r, w)
-
-    def mset(ap, v, w):
-        op("V", lambda: V.memset(ap, v), "", w)
-
-    def qz(n, t, r):
-        op("V", lambda: V.quantize_mx(T["q" + n][:], T["p" + n][:], t), r, "q" + n)
-
-    def act(out, in_, f, r, w, bias=0.0, scale=1.0):
-        if f == F_.Copy:
-            op("S", lambda: S.activation(out, in_, f), r, w)
-        else:
-            op("S", lambda: S.activation(out, in_, f, bias=bias, scale=scale), r, w)
-
-    def sset(ap, n, v, w):
-        act(ap, T.crow[:, 0:n], F_.Identity, "crow", w, bias=float(v), scale=0.0)
-
-    def mm(b, l, l0, rr, r0, n, start=True, stop=True):
-        r = " ".join("q%s p%s" % (x, x) for x in (l, rr))
-        op("T", lambda: P.matmul_mx(ps[b][:, 0:n], T["q" + l][:, l0:l0 + 128], T["p" + l][:, l0:l0 + 128],
-                                    T["q" + rr][:, r0:r0 + n], T["p" + rr][:, r0:r0 + n], start, stop), r, "ps%d" % b)
-
-    def pick(to, fr, off, r):
-        act(T["p" + to][:], T["p" + fr][:].indirect(off), F_.Copy, "q%s %s" % (fr, r), "p" + to)
-        return lambda: cp(T["q" + to][:].bitcast(u32), T["q" + fr][:].bitcast(u32).indirect(off), "q%s %s" % (fr, r), "q" + to)
-
-    def iota(out, pat, w, base=0, ch=0, whole=False):
-        if whole:
-            op("G", lambda: g.iota(out, pat, base, ch), "", w)
-        else:
-            op("G", lambda: g.iota(out, pat, base, ch, allow_small_or_imprecise_dtypes=True), "", w)
-
-    names = {}
-
-    def col(n):
-        k = names.setdefault(n, len(names))
-        return T.cf[:, k:k + 1]
-
-    def arg(x):
-        return (col(x), " k." + x) if isinstance(x, str) else (x, "")
-
-    def vcol(n, a, s1, o0, s2=None, o1=None):
-        (x1, r1), (x2, r2) = arg(s1), arg(s2)
-        ts(col(n), col(a), x1, x2, o0, o1, "k." + a + r1 + r2, "k." + n)
-
-    def scol(n, a, scale=1.0, bias=0.0, f=F_.Identity):
-        (x1, r1), (x2, r2) = arg(scale), arg(bias)
-        act(col(n), col(a), f, "k." + a + r1 + r2, "k." + n, bias=x2, scale=x1)
-
-    smp = {}
-
-    def sm(n, w):
-        if n not in smp:
-            smp[n] = sum((x[1] + 7) // 8 * 8 for x in smp.values()), w
-        return T.sm[:, smp[n][0]:smp[n][0] + w]
-
-    def smv(n, a, b, s=1):
-        return T.sm[:, smp[n][0] + a:smp[n][0] + b:s]
-
-    fill = []
-
-    def gap(n=1):
-        for _ in range(min(n, len(fill))):
-            fill.pop(0)()
-
-    ps = [T["bank%d" % b] for b in range(8)]
-    add, sub, mul, mx, mn = A_.add, A_.subtract, A_.mult, A_.max, A_.min
-    u32, u8 = dt.uint32, dt.uint8
-    AND, SHR = A_.bitwise_and, A_.logical_shift_right
-    ID = F_.Identity
-    allec = " ".join("ec%d%d" % (a, a2) for a in range(4) for a2 in range(4))
-
-    for k in range(8):
-        dma("Y" if k % 2 else "S", T.aw[16 * k:16 * k + 16, 0:22], T.alive[:], "dal", 128, "", "aw")
-    dma("Y", T.sw[:, 0:22], T.seat[:], "dse", 16, "", "sw")
-    dma("Y", T.xo[:, 8:8 + 4 * C], T.x[:], "dx", 16, "", "xo")
-    dma("Y", T.ub[:], T.u[:], "du", 16, "", "ub")
-    dma("Y", T.qw[:].bitcast(u8), T.wc[:], "dw", 32, "", "qw")
-    dma("Y", T.pw[:], T.ws[:], "dw", 32, "", "qw")
-    dma("Y", T.vb[:], T.v[:], "dv", 16, "", "vb")
-
-    pi = T.ci[:, 7:8]
-    iota(pi, [[0, 1]], "pi", ch=1, whole=True)
-    iota(sm("m16", 22), [[16, 22]], "m16")
-    iota(sm("b2", 22), [[2, 11], [0, 2]], "b2")
-    iota(sm("m4", 23), [[4, 23]], "m4")
-    iota(T.jj[:], [[0, 22], [4096, 4], [512, 4]], "jj")
-    iota(T.j16[:], [[0, 23], [1, 16]], "j16")
-    iota(T.crow[:], [[1, 368]], "crow")
-    mset(T.c64[:], 64.0, "c64 c64x")
-    ts(T.ci[:, 0:1], pi, 15, None, AND, None, "pi", "ci0")
-    ts(T.ci[:, 1:2], pi, 4, None, SHR, None, "pi", "ci1")
-    ts(T.ci[:, 2:3], pi, 2, 3, SHR, AND, "pi", "ci2")
-    ts(T.ci[:, 3:4], pi, 3, None, AND, None, "pi", "ci3")
-    ts(T.ci[:, 4:5], pi, 4, 1, SHR, AND, "pi", "ci4")
-    ts(T.ci[:, 5:6], pi, 4, None, AND, None, "pi", "ci5")
-    mset(T.c64[:, 514:518], 0.0, "c64x")
-    for n in ("q", "g", "q4", "t4", "go", "h4"):
-        col(n)
-    cp(T.cf[:, 0:6], T.ci[:, 0:6], "ci0 ci1 ci2 ci3 ci4 ci5", "k.q k.g k.q4 k.t4 k.go k.h4")
-    mset(T.xo[:, 0:8], 0.0, "xoz")
-    vcol("a3", "g", 3.0, A_.is_ge)
-    vcol("gp", "g", 4.0, A_.is_ge, "g", add)
-    vcol("u3", "t4", -1.0, mul, 3.0, add)
-    vcol("dy1", "g", 5.0, A_.is_ge, "a3", add)
-    scol("pk", "q4", -4096.0, -1536.0)
-    scol("nq", "q", -1.0)
-    scol("rq", "q", 1e6, 1e6)
-    scol("y1", "t4", 1.0, -1.5)
-    scol("d", "t4", 1.0, -1.0)
-    scol("h0", "t4", -353.0, 353.0, F_.Relu)
-    scol("q176", "q", -1.0, 176.5)
-    scol("d15", "t4", 88.0, -220.0)
-    ts(sm("cw", 22), sm("m16", 22), col("q"), 2.0 + B, add, add, "m16 k.q", "cw")
-    vcol("dx1", "dy1", -3.0, mul, "gp", add)
-    vcol("dy", "dy1", -1.0, add)
-    ts(T.l1[:, 0:22], sm("b2", 22), col("go"), None, add, None, "b2 k.go", "l1")
-    vcol("dx", "dx1", -1.0, add)
-    vcol("vert", "dy", "dy", mul)
-    vcol("y2", "y1", "dy", mul, -88.0, mul)
-    vcol("w1", "dx", "u3", mul, "q4", add)
-    vcol("z", "vert", -1000.0, mul, 956.5, add)
-    mset(T.bo[:, C:C + 8], -B, "boz")
-    vcol("pa", "w1", "z", add)
-    vcol("pb", "y2", 132.0, add, "w1", add)
-    scol("ndy", "dy", -1.0)
-    scol("dn", "dy", 3.0, 0.0, F_.Relu)
-    scol("neg", "dx", -1.0, 0.0, F_.Relu)
-    scol("hz", "vert", -1.0, 1.0)
-    scol("v4", "vert", 4.0)
-    act(sm("ab", 23), sm("m4", 23), F_.Abs, "m4 k.pa", "ab", bias=col("pa"))
-    act(T.t5[:, 0:C], T.jj[:], F_.Abs, "jj k.pk", "t5", bias=col("pk"))
-    scol("k41", "dx", 4.0, 1.0)
-    act(T.pm[:], T.t5[:, 0:C], ID, "t5", "pm", bias=1536.0, scale=-1.0)
-    act(T.rst[:], T.j16[:], F_.Sign, "j16", "rst")
-    mset(T.ct[:, 4 * NA:512], 0.0, "ctz")
-    mset(T.cst[:, 0:128], 1.0, "cst0")
-    mset(T.cst[:, 128:256], -64.0, "cst1")
-
-    def esel(b):
-        op("G", lambda: g.affine_select(T.eb[:, 512 * b:512 * b + 512], T.c64[:, 0:512], [[4, 128], [1, 4]], A_.is_equal, 0.0, -b, -4),
-           "c64", "eb%d" % b)
-    esel(0)
-    esel(1)
-
-    rel = _relays(T, topo, rank)
-    eng = topo.engines(core, rel[0][0])
-    ne = len(eng) // 2
-    narr = sum(len(topo.engines(c, core)) for r2 in range(len(T.cores)) for c, d, _ in _relays(T, topo, r2) if d == rank)
-
-    def compose_send(t, v, rv, o, ro, xbuf, rx):
-        scan(o[:, 0:C], T.rst[:, 0:C], v[:, 0:C], 0.0, mul, mx, "rst " + rv, ro)
-        gap()
-        cp(T.si[:, 0:22], o[:, 15:C:16], ro, "si0")
-        gap()
-        ts(T.si[:, 24:46], T.si[:, 0:22], 511, None, AND, None, "si0", "si1")
-        gap()
-        ts(T.cl[:, 0:22], T.si[:, 24:46], 4.0, col("t4"), mul, add, "si1 k.t4", "cl")
-        gap()
-        act(T.ct[:, 192:C], xbuf[:].indirect(T.cl[:, 12:22]), F_.Copy, "cl " + rx, "ct1")
-        cp(T.ct[:, 0:192], xbuf[:].indirect(T.cl[:, 0:12]), "cl " + rx, "ct0")
-        qz("m%d" % t, T.ct[:], "ct0 ct1 ctz")
-        deps("G", ["qm%d" % t], [])
-        for codes in (True, False):
-            trs = []
-            for k, (c, d, cs) in enumerate(rel):
-                if cs == codes:
-                    rid, pid = topo.addr(c, core)
-                    src = T["qm%d" % t][:, 0:NA].bitcast(u8) if codes else T["pm%d" % t][:, 0:NA]
-                    dst = T["qr%d" % t][:].bitcast(u8) if codes else T["pr%d" % t][:]
-                    trs.append(RemoteDMATransfer(dst_ids=[DstId(rid=rid, pnc=pid)],
-                                                 dma_engine_mask=_mask(eng[ne * (k % 2):ne * (k % 2) + ne]),
-                                                 remote_sem=T.sem["rel%d" % t], src=src, dst=dst))
-            g.remote_dma_fused(trs, local_sem=T.sem.sent)
-        lastw["ql%d" % t] = ("arr%d" % t, narr, {})
-
-    tt(sm("oiw", 22), T.aw[:, 0:22], sm("cw", 22), mul, "aw cw", "oiw")
-    cp(T.seatu[:, 0:22], T.sw[:, 0:22], "sw", "seatu")
-    cp(T.t4[:, 0:C], sm("oiw", 22).indirect(T.l1[:, 0:22]), "oiw l1", "t4")
-    ts(sm("e1", 23), sm("ab", 23), 44.0, 1000.0, A_.is_gt, mul, "ab", "e1")
-    op("V", lambda: V.transpose(T.oi[:], T.t4[:, 0:C]), "t4", "oi")
-    act(T.rmono[:], T.j16[:, 0:C], F_.Relu, "j16 k.rq", "rmono", bias=col("rq"), scale=-1e6)
-    act(T.bo[:, 0:C], T.oi[:].indirect(T.seatu[:, 0:22]), ID, "oi seatu", "bo", bias=-B)
-    tt(sm("e2", 23), sm("e1", 23), sm("m4", 23), add, "e1 m4", "e2")
-    ts(T.t1[:, 0:C], T.oi[:], 1.0, None, mn, None, "oi", "t1")
-    ts(T.posl[:, 0:22], smv("e2", 0, 22), col("pb"), float(C), add, mn, "e2 k.pb", "posl")
-    scan(T.cum[:], T.t1[:, 0:C], T.t1[:, 0:C], 0.0, add, mx, "t1", "cum")
-    scol("hd", "dx", "hz")
-    scol("n12", "neg", 12.0)
-    scol("n3", "neg", -3.0, "q4")
-    scol("alpha", "hd", -1.0, "v4")
-    scol("h88", "hd", -88.0)
-    scol("g4", "hd", 351.0, 0.0, F_.Relu)
-    scol("ndx", "dx", -1.0)
-    scol("beta", "k41", "ndy", "h88")
-    scol("g1", "n12", "vert", "g4")
-    scol("cH", "neg", -3.0, "dx")
-    scol("gam", "k41", "dn", "g1")
-    scol("hdr", "h0", "vert")
-    act(sm("gi", 4), T.crow[:, 0:4], ID, "crow k.beta k.gam", "gi", bias=col("gam"), scale=col("beta"))
-    scol("r88", "d15", "ndy", 132.0)
-    for i in range(4):
-        act(T.nrow[:, NA * i:NA * i + NA], T.crow[:, 0:NA], ID, "crow gi k.alpha", "nrow%d" % i, bias=smv("gi", i, i + 1), scale=col("alpha"))
-    tt(T.t2[:, 0:C], T.bo[:].indirect(T.posl[:, 0:22]), T.pm[:], add, "bo boz posl pm", "t2")
-    ts(sm("na", 22), sm("oiw", 22), 0.0, None, A_.is_equal, None, "oiw", "na")
-    ts(sm("cz", 22), sm("cw", 22), 255.0 - B, None, add, None, "cw", "cz")
-    fill.extend([
-        lambda: scan(T.t1[:, 0:C], T.rmono[:], T.cum[:], 0.0, mx, mn, "rmono cum", "t1"),
-        lambda: None,
-        lambda: tt(sm("c2", 22), sm("cz", 22), T.t1[:, 15:C:16], sub, "cz t1", "c2"),
-        lambda: tt(sm("c3", 22), sm("c2", 22), sm("na", 22), mul, "c2 na", "c3"),
-    ])
-    compose_send(0, T.t2, "t2", T.t3, "t3", T.xo, "xo xoz")
-    esel(2)
-    esel(3)
-    iota(sm("g8i", 16), [[0, 2], [1, 2], [2, 4]], "g8i")
-    op("G", lambda: g.affine_select(T.tau[:], T.cst[:, 0:128], [[-1, 128]], A_.is_ge, 0.0, 0, 1), "cst0", "tau")
-    op("G", lambda: g.affine_select(T.negi[:], T.cst[:, 128:256], [[1, 128]], A_.is_equal, 0.0, 0, -1), "cst1", "negi")
-    act(T.t5[:], T.j16[:], F_.Abs, "j16 k.nq", "t5", bias=col("nq"))
-    scol("h16", "h4", 4.0)
-    scol("hno", "hz", float(NONE))
-    scol("lim", "hz", -264000.0, -88000.0)
-    act(T.diag[:], T.t5[:], F_.Relu, "t5", "diag", bias=1.0, scale=-1.0)
-    scol("slope", "hd", -16.0, "v4")
-    scol("po", "ndx", "d", "n3")
-    scol("sH", "hd", "q176")
-    scol("cH1", "hz", 1000.0, "cH")
-    scol("po1", "po", 1.0, -43.5)
-    scol("po2", "po", 1.0, "r88")
-    scol("sH2", "hz", 175.5, "sH")
-    scol("bs", "dy", 44.0, 301.0)
-    scol("cC", "po1", "vert", "sH")
-    scol("cH2", "cH1", 1.0, -43.5)
-    scol("sA", "po2", "vert", "sH2")
-    scol("cH3", "cH", 1.0, "bs")
-    act(sm("ab2", 23), T.crow[:, 0:23], F_.Abs, "crow k.slope k.cC", "ab2", bias=col("cC"), scale=col("slope"))
-    act(T.et[:, 0:92], T.crow[:, 0:92], F_.Abs, "crow k.cH2", "et", bias=col("cH2"))
-    act(sm("sr", 23), T.crow[:, 0:23], ID, "crow k.slope k.sA", "sr", bias=col("sA"), scale=col("slope"))
-    act(T.ett[:, 0:92], T.crow[:, 0:92], ID, "crow k.cH3", "ett", bias=col("cH3"))
-    act(sm("e3", 23), sm("ab2", 23), F_.Relu, "ab2 k.lim", "e3", bias=col("lim"), scale=2000.0)
-    act(T.et[:, 96:188], T.et[:, 0:92], F_.Relu, "et", "etb", bias=-88000.0, scale=2000.0)
-    act(T.cray[:], T.crow[:], ID, "crow", "cray", scale=512.0)
-
-    tt(sm("c4", 22), sm("c3", 22), T.t1[:, 15:C:16], mx, "c3 t1", "c4")
-    qz("x", T.xo[:, 8:8 + 4 * C], "xo")
-    ts(T.ciu[:, 0:22], sm("c4", 22), -1.0, None, add, None, "c4", "ciu")
-    qz("u", T.ub[:], "ub")
-    cp(T.pirow[:].indirect(T.ciu[:, 0:22]), T.crow[:, 0:C], "ciu crow", "pirow")
-    mset(T.one16[:, 1:9], 1, "one16")
-    scan(T.t1[:, 0:C], T.rmono[:], T.pirow[:], 0.0, mx, mn, "rmono pirow", "t1")
-    tt(sm("e4", 23), sm("e3", 23), sm("sr", 23), add, "e3 sr", "e4")
-    cp(T.piu[:, 0:22], T.t1[:, 15:C:16], "t1", "piu")
-    ts(T.rayl[:, 0:23], sm("e4", 23), float(C), col("hdr"), mn, mx, "e4 k.hdr", "rayl")
-    pick("a0", "x", T.piu[:, 0:22], "piu")()
-
-    def unpack_state(t, n):
-        xn, w = T["xn%d" % (t + 1)], (C if t == R - 1 else L)
-        for b in range(4):
-            mm(b, "e", 128 * b, n, 0, w)
-        for b in range(4):
-            mm(4 + b, "e", 128 * b, n, 0, C + L - w, True, False)
-
-        def one(b):
-            act(T.tw[:, PW * b + 1:PW * b + 1 + L], ps[b][:, 0:L], ID, "ps%d" % b, "tw%d" % b, scale=1.0 / 64)
-            if w == C:
-                act(xn[:, 4 + 4 * L + b:4 + 4 * C:4], ps[b][:, L:C], ID, "ps%d" % b, "xd%d_%d" % (t + 1, b), scale=1.0 / 64)
-        return one
-
-    cp(T.rp[:].indirect(T.seatu[:, 0:22]), T.nrow[:], "seatu nrow0 nrow1 nrow2 nrow3", "rp")
-    qz("e", T.eb[:], "eb0 eb1 eb2 eb3")
-    sset(T.bi[:, C:C + 1], 1, -B, "biz")
-    sset(T.bi[:, C + 1:C + 8], 7, 0, "biz2")
-    act(T.iot[:], T.crow[:, 1:L + 1], ID, "crow", "iot", scale=2.0 ** -13)
-    sset(T.tw[:, 0:4 * PW:PW], 4, 0, "twz")
-    sset(T.tw[:, NONE:4 * PW:PW], 4, 0, "twz2")
-    sset(sm("live", 2), 2, 1, "live0 live1")
-    sset(sm("nb", 2), 2, 0, "nb")
-    sset(sm("thr", 2), 2, 64 * (M - 0.5), "thr")
-    sset(T.oh[:, 514:1024:4], 128, 0, "ohz")
-    sset(T.oh[:, 3:512:4], 128, 0, "ohz2")
-    sset(T.xn1[:, 0:4], 4, 0, "xz1")
-    sset(T.xn2[:, 0:4], 4, 0, "xz2")
-    sset(T.lr[:, 1:L + 1], L, 1, "lr")
-    sset(T.lr[:, L + 1:359], 102, 0, "lrz")
-    sset(T.lr[:, 0:1], 1, 0, "lrz2")
-    sset(T.lr[:, 359:360], 1, 1, "lrz3")
-    one = unpack_state(0, "a0")
-    for b in range(4):
-        one(b)
-    act(sm("g8", 16), sm("g8i", 16), ID, "g8i", "g8", scale=0.125)
-    act(sm("r8", 16), sm("g8i", 16), F_.Relu, "g8i", "r8", bias=2 * BIG, scale=-4 * BIG)
-
-    tt(T.ett[:, 96:188], T.ett[:, 0:92], T.et[:, 96:188], add, "etb ett", "ettb")
-    tt(T.bi[:, 0:C], T.cum[:].indirect(T.seatu[:, 0:22]), T.bo[:, 0:C], mn, "cum seatu bo", "bi")
-    ts(T.ett[:, 0:92], T.ett[:, 96:188], float(NONE), col("vert"), mn, mul, "ettb k.vert", "ett")
-    tt(T.h1[:, 0:L], T.rp[:].indirect(T.piu[:, 0:16]), T.diag[:, 0:L], mul, "rp piu diag", "h1")
-    tt(T.cray[:, 0:368:4], T.cray[:, 0:368:4], T.ett[:, 0:92], add, "cray ett", "cray")
-    scan(T.h2[:, 0:L], T.rst[:, 0:L], T.h1[:, 0:L], 0.0, mul, mx, "rst h1", "h2")
-    ts(T.cray[:, 0:C:NA], T.cray[:, 0:C:NA], col("hno"), None, add, None, "cray k.hno", "cray")
-    cp(T.ipos[:], T.h2[:, 15:L:16], "h2", "ipos")
-    tt(T.v0[:], T.bi[:].indirect(T.rayl[:, 0:23]), T.cray[:], add, "bi biz biz2 rayl cray", "v0")
-    ts(T.one16[:, 0:1], col("t4"), 32.0, col("h16"), mul, add, "k.t4 k.h16", "one16c")
-    cp(T.v0[:, 0:C:NA], T.cray[:, 0:C:NA], "cray v0", "v0")
-    for k in range(2):
-        for h in range(2):
-            cp(T.ipos2[:, 2 * k + h:16:4], T.ipos[:, 8 * k + h:8 * k + 8:2], "ipos", "ip%d" % (2 * k + h))
-    act(T.bic[:], T.bi[:], F_.Relu, "bi biz biz2", "bic")
-    act(sm("r8b", 16), sm("r8", 16), ID, "r8", "r8b", bias=-BIG)
-
-    def z_list(v, rv, mask, rm, first):
-        scan(T.er[:], v, v, 0.0, mx, mx, rv, "er")
-        gap()
-        act(T.et[:], T.er[:].indirect(T.ipos2[:]), F_.Copy, "er ip0 ip1 ip2 ip3 etb", "et etb")
-        tt(T.t2[:, 0:L], T.er[:].indirect(T.ipos[:]), mask, mul, "er ipos " + rm, "t2")
-        op("V", lambda: V.transpose(T.ett[:], T.et[:]), "et ettb", "ett ettb")
-        gap()
-        cp(T.si[:, 48:64], T.ett[:, 0:L:16], "ett", "si2")
-        scan(T.t3[:, 0:L], T.rst[:, 0:L], T.t2[:, 0:L], 0.0, mul, mx, "rst t2", "t3")
-        ts(T.si[:, 64:80], T.si[:, 48:64], 511, None, AND, None, "si2", "si3")
-        cp(T.si[:, 0:16], T.t3[:, 15:L:16], "t3", "si0")
-        ts(sm("sf", 16), T.si[:, 64:80], 2.0 ** -13, None, mul, None, "si3", "sf")
-        ts(T.si[:, 24:40], T.si[:, 0:16], 511, None, AND, None, "si0", "si1")
-        gap()
-        cp(T.zl[:], T.si[:, 24:40], "si1", "zl")
-        sm("ec", 16)
-        o, i = smp["ec"][0], smp["sf"][0]
-        for a in range(4):
-            for a2 in range(4):
-                dst, src = T.sm[32 * a2:32 * a2 + 32, o + a:o + 16:4], T.sm[32 * a:32 * a + 32, i + 4 * a2:i + 4 * a2 + 4]
-                if a >= 2 and (a == 3 or a2 >= 2) and not first:
-                    cp(dst, src, "sf", "ec%d%d" % (a, a2))
-                else:
-                    act(dst, src, F_.Copy, "sf", "ec%d%d" % (a, a2))
-        act(sm("mk", 16), sm("ec", 16), ID, allec, "mk", bias=-256.5 * 2e23, scale=8192 * 2e23)
-
-    fill.extend([lambda: None, lambda: None, pick("u1", "u", T.one16[:, 0:9], "one16 one16c")])
-    z_list(T.v0[:], "v0", T.diag[:, 0:L], "diag", True)
-    tt(T.h1[:, 0:C], T.bic[:].indirect(T.posl[:, 0:22]), T.diag[:, 0:C], mul, "bic posl diag", "h1")
-    qz("o1", T.c64[:], "c64 c64x")
-    scan(T.h2[:, 0:C], T.rst[:, 0:C], T.h1[:, 0:C], 0.0, mul, mx, "rst h1", "h2")
-
-    for t in range(R):
-        last = t == R - 1
-        xn = T["xn%d" % (t + 1)]
-        for b in range(4):
-            mm(b, "e", 128 * b, "l%d" % t, 0, 2 * NA)
-        for b in range(4):
-            o = T.tw[:, PW * b + 1 + L:PW * b + 1 + L + 2 * NA]
-            if b % 2:
-                act(o, ps[b][:, 0:2 * NA], ID, "ps%d" % b, "ta%d" % b, scale=1.0 / 64)
-            else:
-                ts(o, ps[b][:, 0:2 * NA], 1.0 / 64, None, mul, None, "ps%d" % b, "ta%d" % b)
-        for b in range(4):
-            o, i = T.zt[:, b:4 * L:4], T.tw[:, PW * b:PW * b + NONE + 1].indirect(T.zl[:])
-            r = "zl twz twz2 tw%d ta%d" % (b, b)
-            if b % 2:
-                act(o, i, F_.Copy, r, "zt%d" % b)
-            else:
-                cp(o, i, r, "zt%d" % b)
-        qz("z", T.zt[:], "zt0 zt1 zt2 zt3")
-        mm(1, "z", 128, "u1", 0, 128)
-        mm(2, "u1", 16, "z", 0, 128)
-        mm(3, "u1", 16, "z", 128, 128)
-        mm(0, "z", 0, "u1", 0, 128)
-        for b in range(4):
-            mm(4 + b, "w", 128 * b, "z", 0, L, False, True)
-        sm("s", 2), sm("sa", 16)
-        if t == 0:
-            tt(T.val[:, 0:160], T.bic[:].indirect(T.posl[:, 0:10]), T.pm[:, 0:160], add, "bic posl pm", "val0")
-        tt(sm("key", 16), sm("ec", 16), sm("g8", 16), add, "g8 " + allec, "key")
-
-        def s_col(k):
-            act(smv("s", k, k + 1), ps[k][:, 16:17], ID, "ps%d live%d nb" % (k, k), "s%d" % k,
-                bias=smv("nb", k, k + 1), scale=smv("live", k, k + 1))
-
-        def a_op(k):
-            tt(smv("sa", 8 * k, 8 * k + 8), ps[k][:, 0:8], smv("mk", 8 * k, 8 * k + 8), mx, "ps%d mk" % k, "sa%d" % k)
-        s_col(1)
-        ts(T.cmp[:, 1:512:4], ps[2][:, 0:128], smv("s", 1, 2), None, A_.is_lt, None, "ps2 s1", "cm1")
-        act(T.sg[:, 128:256], ps[3][:, 0:128], F_.Sign, "ps3 s1", "sg1", bias=smv("s", 1, 2), scale=-1.0)
-        a_op(1)
-        s_col(0)
-        tt(T.cmp[:, 3:512:4], T.sg[:, 128:256], T.tau[:], A_.is_ge, "sg1 tau", "cm3")
-        act(T.sg[:, 0:128], ps[2][:, 0:128], F_.Sign, "ps2 s0", "sg0", bias=smv("s", 0, 1), scale=-1.0)
-        ts(T.cmp[:, 2:512:4], ps[3][:, 0:128], smv("s", 0, 1), None, A_.is_le, None, "ps3 s0", "cm2")
-        a_op(0)
-        tt(T.cmp[:, 0:512:4], T.sg[:, 0:128], T.tau[:], A_.is_ge, "sg0 tau", "cm0")
-        scan(sm("mi", 16), sm("r8b", 16), sm("sa", 16), 0.0, mx, mn, "r8b sa0 sa1", "mi")
-        qz("c", T.cmp[:], "cm0 cm1 cm2 cm3")
-
-        def x_copy(b):
-            w = L if last else C
-            act(xn[:, 4 + b:4 + 4 * w:4], ps[4 + b][:, 0:w], ID, "ps%d" % (4 + b), "xl%d_%d" % (t + 1, b), scale=1.0 / 64)
-        if last:
-            x_copy(0)
-        sm("nc", 16)
-        for k in range(2):
-            act(smv("nc", 8 * k, 8 * k + 8), smv("sa", 8 * k, 8 * k + 8), F_.Sign, "sa%d mi" % k, "nc%d" % k,
-                bias=smv("mi", 8 * k + 7, 8 * k + 8), scale=-1.0)
-        mm(2, "c", 0, "o1", 2, 128)
-        if last:
-            x_copy(1)
-            x_copy(2)
-            x_copy(3)
-        else:
-            x_copy(0)
-        tt(sm("w", 16), sm("key", 16), sm("nc", 16), sub, "key nc0 nc1", "w")
-        if t == 0:
-            cp(T.lini[:, 0:22], T.h2[:, 15:C:16], "h2", "lini")
-        scan(sm("wm", 16), sm("r8b", 16), sm("w", 16), 0.0, mx, mn, "r8b w", "wm")
-        tt(sm("con", 2), ps[2][:, 126:128], sm("thr", 2), A_.is_lt, "ps2 thr", "con")
-        ts(sm("wt", 2), smv("wm", 7, 16, 8), 1.5 * 2 ** 20, 1.5 * 2 ** 20, add, sub, "wm", "wt")
-        tt(sm("nam", 2), smv("wm", 7, 16, 8), sm("wt", 2), sub, "wm wt", "nam")
-        for k in range(2):
-            act(T.oh[:, 512 * k + 2 + k:512 * k + 512:4], T.negi[:], ID, "negi con", "oh%d" % (2 + k), scale=smv("con", k, k + 1))
-        for k in range(2):
-            ts(T.oh[:, k:4 * L:4], T.iot[:], smv("nam", k, k + 1), smv("con", k, k + 1), A_.is_equal, mul, "iot nam con", "oh%d" % k)
-        rx = " ".join("xl%d_%d xd%d_%d" % (t + 1, b, t + 1, b) for b in range(4))
-        if last:
-            qz("a3", xn[:, 4:4 + 4 * C], rx)
-            codes = pick("f", "a3", T.ciu[:, 0:22], "ciu")
-        else:
-            x_copy(1)
-            x_copy(2)
-            x_copy(3)
-        qz("h", T.oh[:], "oh0 oh1 oh2 oh3 ohz ohz2")
-        mm(3, "o1", 0, "h", 0, L)
-        if last:
-            codes()
-            H = C // 2
-            for k in range(2):
-                mm(k, "v", 0, "f", H * k, H)
-            tt(T.lr[:, 1:L + 1], ps[3][:, 0:L], T.lr[:, 1:L + 1], A_.is_lt, "ps3 lr", "lr")
-            for k in range(4):
-                dma("Y", T.osc[4 * k:4 * k + 4, :], T.pf[32 * k:32 * k + 4, :], "dout", 128, "pf", "")
-            dma("Y", T.oc[:], T.qf[:].bitcast(u8), "dout", 128, "qf", "")
-            for k in range(2):
-                act(T.ysb[:, H * k:H * k + H], ps[k][:, 0:H], F_.Copy, "ps%d" % k, "ysb%d" % k)
-                dma("S" if k else "Y", T.y[:, H * k:H * k + H], T.ysb[:, H * k:H * k + H], "dout", 128, "ysb%d" % k, "")
-            cp(T.olr[:], T.lr[:].indirect(T.ciu1[:, 0:22]), "lr lrz lrz2 lrz3 ciu1", "olr")
-            dma("Y", T.ol[:], T.olr[0:1, :], "dout", 128, "olr", "")
-            break
-        if t == 0:
-            tt(T.val[:, 160:C], T.bic[:].indirect(T.posl[:, 10:22]), T.pm[:, 160:C], add, "bic posl pm", "val1")
-        for k in range(2):
-            mm(k, "h", 128 * k, "o1", 0, 128)
-        tt(T.lr[:, 1:L + 1], ps[3][:, 0:L], T.lr[:, 1:L + 1], A_.is_lt, "ps3 lr", "lr")
-        tt(T.h3[:, 0:C], T.lr[:].indirect(T.lini[:, 0:22]), T.val[:], mul, "lr lrz lrz2 lrz3 lini val0 val1", "h3")
-        if t == 0:
-            act(T.diagr[:], T.t5[:], F_.Relu, "t5", "diagr", bias=1.0, scale=-1.0)
-            sset(T.diagr[:, 0:C:NA], 4, 0, "diagr")
-        for k in range(2):
-            fill.append(lambda k=k: tt(smv("live", k, k + 1), ps[k][:, 0:1], smv("live", k, k + 1), A_.is_lt, "ps%d live%d" % (k, k), "live%d" % k))
-        fill.append(lambda: ts(sm("nb", 2), sm("live", 2), -1.0, BIG, add, mul, "live0 live1", "nb"))
-        fill.append(lambda: ts(sm("thr", 2), sm("live", 2), 64 * (M - 0.5), None, mul, None, "live0 live1", "thr"))
-        compose_send(t + 1, T.h3, "h3", T.h4, "h4", xn, rx + " xz%d" % (t + 1))
-        qz("a", xn[:, 4:4 + 4 * C], rx)
-        one = unpack_state(t + 1, "a")
-        if t == 0:
-            tt(T.h1[:], T.bic[:].indirect(T.rayl[:, 0:23]), T.diagr[:], mul, "bic rayl diagr", "h1")
-            cp(T.ciu1[:, 0:22], sm("c4", 22), "c4", "ciu1")
-            scan(T.h2[:], T.rst[:], T.h1[:], 0.0, mul, mx, "rst h1", "h2")
-            fill.append(lambda: None)
-            tt(T.ml[:], T.lr[:, 1:L + 1], T.diag[:, 0:L], mul, "lr diag", "ml")
-            ts(sm("r0", 23), T.h2[:, 15:368:16], 0.0, 359.0, A_.is_equal, mul, "h2", "r0")
-            tt(sm("r1", 23), sm("r0", 23), T.h2[:, 15:368:16], add, "r0 h2", "r1")
-            cp(T.rayi[:, 0:23], sm("r1", 23), "r1", "rayi")
-        tt(T.t1[:], T.lr[:].indirect(T.rayi[:, 0:23]), T.v0[:], mul, "lr lrz lrz2 lrz3 rayi v0", "t1")
-        for b in range(4 if t == 0 else 2):
-            one(b)
-        if t:
-            fill.append(lambda: tt(T.ml[:], T.lr[:, 1:L + 1], T.diag[:, 0:L], mul, "lr diag", "ml"))
-            fill.append(lambda: (one(2), one(3)))
-            fill.append(lambda: qz("v", T.vb[:], "vb"))
-        z_list(T.t1[:], "t1", T.ml[:], "ml", False)
-
+            cnt[e] += 1
+            c["ways"][e][1]().then_inc(T.sem["c" + e], 1)
+            c["done"] = ("c" + e, cnt[e], dict(know[e]))
     need("G", [("c" + e, cnt[e], {}) for e in cnt] + [("sent", R * 4 * ne, {}), ("dout", 128, {})])

@@ -14,7 +14,7 @@ TINY = 1e-35
 WT = 13.0 / 512
 f32, bf, i32, u16, cod, pl = "float32", "bfloat16", "int32", "uint16", "float8_e4m3fn_x4", "uint8"
 f16 = "float16"
-CYC, HOP, DMA, WAY, FIRST = 0.83e-3, 0.2, 1.8, 4.0, 8.0
+CYC, HOP, DMA, WAY, FIRST = 0.83e-3, 0.2, 1.5, 2.7, 4.0
 SPARE = 0.2
 
 
@@ -29,7 +29,7 @@ for _b, _d, _w, _names in (
         ("whole", i32, 24, "s0 s1 s2 s3 s4 s5"),
         ("small", f32, 24, "m4 b2 cw oiw e1 e2 cz c2 c3 ab2 sr e3 e4 gi sf ec idb dd mk sa pmn nn nm rs2 sc lv nb "
                            "la lb lc ld le lf lg lh li lj lk ll"),
-        ("rows32", f32, W, "crow jj t5 t6 t7 pm olr ysb xr"),
+        ("rows32", f32, W, "crow jj t5 t6 t7 t8 pm olr ysb xr"),
         ("rows16", f16, W, "h1 h2 h3 h4 h5"),
         ("rows", bf, W, "rst diag rmono t4 a1 bo fl cum ca cs nrow pirow rp w1 w2 w3 w4 w5 w6 w7 w8 w9 w10 il g0 g1 g2 gn er t2 t3 ett et2 "
                         "m0 m1 m2 o1 o2 nt dl n0 n1 n2 tau tat th iot sg"),
@@ -104,7 +104,7 @@ def _order(calls):
                 best = t, e, us
         c["start"], c["e"] = best[0], best[1]
         c["end"] = best[0] + best[2] + c["late"]
-        busy[c["e"]] = sorted(busy.get(c["e"], []) + [(best[0], best[0] + best[2])])
+        busy[c["e"]] = sorted(busy.get(c["e"], []) + [(best[0] - c.get("clear", 0.0), best[0] + best[2])])
     return sorted(calls, key=lambda c: (c["start"], c["n"]))
 
 
@@ -217,6 +217,10 @@ def rank_program(g, core, T, topo):
     def mset(out, x):
         call({"V": (cost(out, [out]), lambda: V.memset(out[0], x))}, [out], [])
 
+    def fill(out, x):
+        a = v("jj", 0, out[2])
+        call({"S": act_way(out, a, F_.Identity, 0.0, float(x)), "V": (cost(out, [out]), lambda: V.memset(out[0], x))}, [out], [a])
+
     def qz(n, t, a=0, b=None):
         q, p = v("q" + n, a, b), v("p" + n, a, b)
         call({"V": (0.012 + 0.22e-3 * t[2], lambda: V.quantize_mx(q[0], p[0], t[0]))}, [q, p], [t])
@@ -277,20 +281,22 @@ def rank_program(g, core, T, topo):
     for b in range(4):
         qz("e", v("eb" if b % 2 else "ea", 2 - b // 2 * 2, 514 - b // 2 * 2), 128 * b, 128 * b + 128)
     for j in range(8):
-        mset(v("cwt", 512 * (j // 4) + j % 4, 512 * (j // 4) + 512, 4), WT if j // 4 == j % 4 // 2 else 0.0)
+        fill(v("cwt", 512 * (j // 4) + j % 4, 512 * (j // 4) + 512, 4), WT if j // 4 == j % 4 // 2 else 0.0)
     qz("k", v("cwt"))
     for t in range(R):
-        mset(v("sv%d" % t, 0, O + 1), 1.0)
-        mset(v("sv%d" % t, O + 1 + L, O + 2 + L), 0.0)
-    select(v("tau", 0, H), v("sv0", 0, H), [[-1, H]], A_.is_ge, 0, 1)
-    aff(v("tat", 0, H), v("tau", 0, H), -TINY, TINY)
+        iota(v("sv%d" % t, 0, O + 1), [[0, O + 1]], 1)
+        iota(v("sv%d" % t, O + 1 + L, O + 2 + L), [[0, 1]])
+    select(v("tat", 0, H), v("sv0", 0, H), [[1, H]], A_.is_gt, 0, -1)
     mset(v("rst"), 1.0)
     mset(v("rst", 0, W, 16), 0.0)
-    for n, a, b, s, x in (("xo", 0, 8, 1, 0.0), ("xn1", 0, 4, 1, 0.0), ("xn2", 0, 4, 1, 0.0), ("ct", 4 * NA, 512, 1, 0.0),
-                          ("bo", C, C + 8, 1, -B), ("bc", C, PW, 93, 0.0), ("tw", 0, 4 * PW, PW, 0.0), ("tw", O, 4 * PW, PW, 0.0),
-                          ("ones", 0, 8, 1, 1), ("idb", 0, 24, 1, 0.0), ("sa", 0, 11, 10, BIG), ("sa", 9, 10, 1, 100 * BIG),
-                          ("rs2", 0, 24, 1, -100 * BIG), ("rs2", 9, 10, 1, 100 * BIG), ("pmn", 0, 1, 1, 100 * BIG)):
-        mset(v(n, a, b, s), x)
+    mset(v("ones", 0, 8), 1)
+    for n, a, b, s in (("xn1", 0, 4, 1), ("xn2", 0, 4, 1), ("bc", C, PW, 93), ("tw", 0, 4 * PW, PW), ("tw", O, 4 * PW, PW),
+                       ("idb", 0, 24, 1)):
+        iota(v(n, a, b, s), [[0, len(range(a, b, s))]])
+    for n, a, b, s, x in (("xo", 0, 8, 1, 0.0), ("ct", 4 * NA, 512, 1, 0.0), ("bo", C, C + 8, 1, -B), ("sa", 0, 11, 10, BIG),
+                          ("sa", 9, 10, 1, 100 * BIG), ("rs2", 0, 9, 1, -100 * BIG), ("rs2", 10, 19, 1, -100 * BIG),
+                          ("rs2", 9, 10, 1, 100 * BIG), ("pmn", 0, 1, 1, 100 * BIG)):
+        fill(v(n, a, b, s), x)
     for j, n in enumerate(("q", "g", "q4", "t4", "go")):
         k(n)
     ts(v("ci", 0, 1), pi, 15, AND)
@@ -352,6 +358,7 @@ def rank_program(g, core, T, topo):
                 g.remote_dma_fused(trs, local_sem=T.sem.sent)
         call({"G": (1.0 if t else 3.0, send)}, [v("ql%d" % t), v("pl%d" % t)], [v("qm%d" % t), v("pm%d" % t)], ("arr%d" % t, narr),
              WAY if t else FIRST)
+        calls[-1]["clear"] = 1.0
 
     col("cq", "q", 1.0, B - 176.0)
     aff(v("cw", 0, NC), v("m4", 0, NC), 4.0, "cq")
@@ -490,7 +497,8 @@ def rank_program(g, core, T, topo):
         tt(v("dd", 0, 19), v("idb", 0, 19), v("idb", 1, 20), sub)
         ts(v("lv", 0, 2), v("ec", 0, 2), 0.0, A_.not_equal)
         ts(v("nb", 0, 2), v("ec", 0, 2), 0.0, A_.is_equal, -BIG, mul)
-        aff(v("th", 0, H), v("tat", 0, H), 1.0, v("nb", 1, 2))
+        for h in range(2):
+            aff(v("th", H * h, H * h + H), v("tat", 0, H), TINY, v("nb", h, h + 1))
 
     z_list(0)
 
@@ -522,8 +530,9 @@ def rank_program(g, core, T, topo):
     scan(v("w10"), v("nt"), v("il"), mx, mul)
     scan(v("w8"), v("diag"), v("il"), mx, mul)
     act(v("n0"), v("w10"), F_.Relu, 1.0, 1.0)
-    mset(v("n0", 0, W, 17), 0.0)
-    tt(v("dl", 0, LW), v("il", 1, LW + 1), v("il", 0, LW), sub)
+    fill(v("n0", 0, W, 17), 0.0)
+    act(v("t8"), v("il"), bias=-2048.0)
+    scan(v("dl", 0, LW), v("t8", 1, LW + 1), v("t8", 0, LW), mn, sub)
     table("lini", "w8", 24, "w9", -0.25, float(O))
 
     for t in range(R):
@@ -532,10 +541,11 @@ def rank_program(g, core, T, topo):
         for b in range(4):
             mm(b, "e", 128 * b, "l%d" % t, 0, 2 * NA)
         for b in range(4):
-            aff(v("tw", PW * b + 1, PW * b + O), ps(b, 0, 2 * NA), 1.0 / 64)
+            act(v("tw", PW * b + 1, PW * b + O), ps(b, 0, 2 * NA), scale=1.0 / 64)
         for h in range(2):
             for b in range(4):
-                move(v("zt", 512 * h + b, 512 * h + 512, 4), ix(v("tw", PW * b, PW * b + O + 1 + L), v("zl", 8 * h, 8 * h + 8)))
+                o, i = v("zt", 512 * h + b, 512 * h + 512, 4), ix(v("tw", PW * b, PW * b + O + 1 + L), v("zl", 8 * h, 8 * h + 8))
+                act(o, i, F_.Copy) if b % 2 else cp(o, i)
             qz("z", v("zt", 512 * h, 512 * h + 512), H * h, H * h + H)
             calls[-1]["early"] = 0.5 * (1 - h)
             mm(2 - h, "u1", 0, "z", H * h, H)
@@ -544,16 +554,14 @@ def rank_program(g, core, T, topo):
             mm(4 + b, "w", 128 * b, "z", 0, L, False, True)
             w = L if last else C
             aff(v(xn, 4 + b, 4 + 4 * w, 4), ps(4 + b, 0, w), 1.0 / 64)
-        act(v("sc", 0, 1), ps(0, 1, 2), scale=v("lv", 0, 1), bias=v("nb", 0, 1))
-        act(v("sg", 0, H), ps(2, 0, H), F_.Sign, -1.0, v("sc", 0, 1))
-        tt(v("cmp", 0, 512, 4), v("sg", 0, H), v("tau", 0, H), A_.is_ge)
-        ts(v("cmp", 2, 512, 4), ps(1, 0, H), v("sc", 0, 1), A_.is_le)
-        ts(v("sg", H, L), ps(1, 0, H), ps(3, 1, 2), sub)
-        tt(v("cmp", 3, 512, 4), v("sg", H, L), v("th", 0, H), A_.is_lt)
-        ts(v("cmp", 1, 512, 4), ps(2, 0, H), ps(3, 1, 2), A_.is_lt, v("lv", 1, 2), mul)
+        for h in range(2):
+            ts(v("sg", H * h, H * h + H), ps(2 - h, 0, H), ps(3 * h, 1, 2), sub)
+            tt(v("cmp", 3 * h, 512, 4), v("sg", H * h, H * h + H), v("th", H * h, H * h + H), A_.is_lt)
+            ts(v("cmp", 2 - h, 512, 4), ps(1 + h, 0, H), ps(3 * h, 1, 2), A_.is_lt if h else A_.is_le, v("lv", h, h + 1), mul)
         qz("c", v("cmp"))
         for h in range(2):
             tt(v("sa", 1 + 10 * h, 9 + 10 * h), ps(3 * h, 0, H, 16), v("mk", 1 + 10 * h, 9 + 10 * h), mx)
+            calls[-1]["early"] = 0.3
         scan(v("pmn", 1, 20), v("rs2", 0, 19), v("sa", 0, 19), mx, mn, 100 * BIG)
         tt(v("nn", 0, 19), v("sa", 0, 19), v("pmn", 0, 19), A_.is_ge)
         scan(v("nm", 0, 19), v("nn", 0, 19), v("dd", 0, 19), mul, add)

@@ -14,7 +14,12 @@ TINY = 1e-35
 WT = 13.0 / 512
 f32, bf, i32, u16, cod, pl = "float32", "bfloat16", "int32", "uint16", "float8_e4m3fn_x4", "uint8"
 f16 = "float16"
-CYC, HOP, DMA, WAY, FIRST = 0.83e-3, 0.2, 1.5, 2.7, 4.0
+CYC, HOP, DMA = 0.83e-3, 0.22, 1.5
+WAYS = [(1.5, 1.0), (2.5, 1.0), (3.0, 1.5), (3.5, 1.0), (3.5, 2.0), (4.0, 1.5), (4.0, 2.7)]
+X1, X2 = (0.6, 0.2, 0.4, 0.0), "VSVSVSVV"
+PASSES = 3
+X3 = 0.0
+ORDER = []
 SPARE = 0.2
 
 
@@ -25,21 +30,21 @@ def _sb(n, d):
 SCRATCH = {"ci": _sb(8, i32), "cf": _sb(96, f32), "aw": _sb(24, i32), "sw": _sb(24, i32), "irow": _sb(23 * 17, f32)}
 PART = {}
 for _b, _d, _w, _names in (
-        ("offs", u16, 24, "seatu l1 posl pos2 rayl ones ciu ciu1 piu rayi lini cl0 cl1 cl2 ipos zl"),
+        ("offs", u16, 24, "seatu l1 posl pos2 rayl ones ciu ciu1 ciu2 piu rayi lini cl0 cl1 cl2 ipos zl"),
         ("whole", i32, 24, "s0 s1 s2 s3 s4 s5"),
         ("small", f32, 24, "m4 b2 cw oiw e1 e2 cz c2 c3 ab2 sr e3 e4 gi sf ec idb dd mk sa pmn nn nm rs2 sc lv nb "
                            "la lb lc ld le lf lg lh li lj lk ll"),
         ("rows32", f32, W, "crow jj t5 t6 t7 t8 pm olr ysb xr"),
         ("rows16", f16, W, "h1 h2 h3 h4 h5"),
         ("rows", bf, W, "rst diag rmono t4 a1 bo fl cum ca cs nrow pirow rp w1 w2 w3 w4 w5 w6 w7 w8 w9 w10 il g0 g1 g2 gn er t2 t3 ett et2 "
-                        "m0 m1 m2 o1 o2 nt dl n0 n1 n2 tau tat th iot sg"),
-        ("wide", bf, PW, "bc sv0 sv1 sv2")):
+                        "m0 m1 m2 o1 o2 nt dl n0 n1 n2 tau tat th iot iol sg"),
+        ("wide", bf, PW, "bc sv0 sv1 nv0 nv1 nv2")):
     SCRATCH[_b] = _sb(_w * len(_names.split()), _d)
     PART.update({_n: (_b, _w * _j, _w) for _j, _n in enumerate(_names.split())})
-for _n, _w in dict(xo=8 + 4 * C, ub=512, vb=512, c64=520, ea=520, eb=520, cwt=4 * L, ct=512, tw=4 * PW, zt=4 * L, cmp=512, oh=512,
+for _n, _w in dict(xo=8 + 4 * C, ub=512, vb=512, c64=520, ea=520, eb=520, cwt=4 * L, ct=512, tw=4 * PW, zt=4 * L, cmp=512, oh=2 * C,
                    xn1=4 + 4 * C, xn2=4 + 4 * C, xn3=4 + 4 * C).items():
     SCRATCH[_n] = _sb(_w, bf)
-for _n, _w in dict(x=C, u=128, u1=128, v=128, w=512, e=512, k=L, z=L, c=128, h=128, a0=C, a=C, a3=C, f=C, m0=128, m1=128, m2=128,
+for _n, _w in dict(x=C, u=128, u1=128, v=128, w=512, e=512, k=L, z=L, c=128, h=C // 2, a0=C, a=C, a3=C, f=C, m0=128, m1=128, m2=128,
                    r0=NA, r1=NA, r2=NA, l0=2 * NA, l1=2 * NA, l2=2 * NA).items():
     SCRATCH["q" + _n], SCRATCH["p" + _n] = _sb(_w, cod), _sb(_w, pl)
 for _b in range(8):
@@ -88,24 +93,47 @@ def _relay_program(g, core, T, topo):
 
 
 def _order(calls):
-    for c in reversed(calls):
-        c["chain"] = (min(x[0] for x in c["ways"].values()) + c["late"] + c.get("early", 0.0)
-                      + max([HOP + x["chain"] for x in c["next"]], default=0.0))
-    busy = {}
-    for c in sorted(calls, key=lambda c: (-c["chain"], c["n"])):
-        best = None
-        for e, (us, _) in c["ways"].items():
-            t = max([x["end"] + (0.0 if e == "T" == x["e"] else HOP) for x in c["deps"]], default=0.0)
-            for a, b in busy.get(e, []):
-                if t + us <= a:
-                    break
-                t = max(t, b)
-            if best is None or t + us + SPARE < best[0] + best[2]:
-                best = t, e, us
-        c["start"], c["e"] = best[0], best[1]
-        c["end"] = best[0] + best[2] + c["late"]
-        busy[c["e"]] = sorted(busy.get(c["e"], []) + [(best[0] - c.get("clear", 0.0), best[0] + best[2])])
-    return sorted(calls, key=lambda c: (c["start"], c["n"]))
+    def late(c, way):
+        return way[c["way"]] if "way" in c else c["late"]
+
+    def place(rank, back, way):
+        busy = {}
+        for c in sorted(calls, key=lambda c: (rank[c["n"]], -c["n"] if back else c["n"])):
+            best = None
+            for e, (us, _) in c["ways"].items():
+                t = max([x["end"] + (0.0 if e == "T" == x["e"] else HOP) for x in c["next" if back else "deps"]], default=0.0)
+                t += late(c, way) if back else 0.0
+                for a, b in busy.get(e, []):
+                    if t + us <= a:
+                        break
+                    t = max(t, b)
+                if best is None or t + us + SPARE < best[0] + best[2]:
+                    best = t, e, us
+            t, e, us = best
+            c["start"], c["e"], c["end"] = t, e, t + us + (0.0 if back else late(c, way))
+            clear = c.get("clear", 0.0)
+            busy[e] = sorted(busy.get(e, []) + [(t, t + us + clear) if back else (t - clear, t + us)])
+        return [(c["n"], c["e"]) for c in sorted(calls, key=lambda c: (c["start"], c["n"]))]
+
+    def takes(order, way):
+        free, end = {}, {}
+        for n, e in order:
+            c = calls[n]
+            t = max([free.get(e, 0.0)] + [end[x["n"]][0] + (0.0 if e == "T" == end[x["n"]][1] else HOP) for x in c["deps"]])
+            free[e] = t + c["ways"][e][0]
+            end[n] = free[e] + late(c, way), e
+        return max(x[0] for x in end.values())
+
+    orders = []
+    for way in WAYS:
+        for c in reversed(calls):
+            c["chain"] = (min(x[0] for x in c["ways"].values()) + late(c, way) + c.get("early", 0.0)
+                          + max([HOP + x["chain"] for x in c["next"]], default=0.0))
+        orders.append(place([-c["chain"] for c in calls], False, way))
+        for _ in range(PASSES):
+            place([-c["end"] for c in calls], True, way)
+            orders.append(place([-c["end"] for c in calls], False, way))
+    return min(orders, key=lambda o: takes(o, WAYS[0]) + takes(o, WAYS[-1]))
 
 
 def rank_program(g, core, T, topo):
@@ -233,9 +261,9 @@ def rank_program(g, core, T, topo):
         o = ps(b, 0, n)
         call({"T": (1.25 * CYC * (n + 16), lambda: P.matmul_mx(o[0], x[0][0], x[1][0], x[2][0], x[3][0], start, stop))}, [o], x)
 
-    def pick(to, fr, off):
-        act(v("p" + to), ix(v("p" + fr), off), F_.Copy)
-        cp(words(v("q" + to)), ix(words(v("q" + fr)), off))
+    def pick(to, fr, off, a, b):
+        act(v("p" + to, 16 * a, 16 * b), ix(v("p" + fr), v(off, a, b)), F_.Copy)
+        cp(words(v("q" + to, 16 * a, 16 * b)), ix(words(v("q" + fr)), v(off, a, b)))
 
     def iota(out, pat, base=0):
         call({"G": (0.13 + 2 * CYC * out[2], lambda: g.iota(out[0], pat, base, 0, allow_small_or_imprecise_dtypes=True))}, [out], [])
@@ -258,7 +286,7 @@ def rank_program(g, core, T, topo):
 
     for j in range(8):
         load("Y" if j % 2 else "S", v("aw", 0, NC, 1, (16 * j, 16 * j + 16)), T.alive[:], "dal", 128)
-    load("Y", v("sw", 0, NC), T.seat[:], "dse", 16)
+    load("S", v("sw", 0, NC), T.seat[:], "dse", 16)
     load("Y", v("xo", 8, 8 + 4 * C), T.x[:], "dx", 16, 2 * DMA)
     load("Y", v("ub"), T.u[:], "du", 16, 2 * DMA)
     load("Y", (T.qw[:].bitcast(dt.uint8),) + v("qw")[1:], T.wc[:], "dw", 32, 3 * DMA)
@@ -275,7 +303,7 @@ def rank_program(g, core, T, topo):
     iota(v("irow"), [[0, 23], [1, 17]])
     iota(v("iot", 0, L), [[1, H], [H, 2]], 1)
     mset(v("c64"), 64.0)
-    calls[-1]["early"] = 2 * FIRST
+    calls[-1]["early"] = 8.0
     for n, b in (("ea", 2), ("eb", 3)):
         select(v(n, 0, 514), v("c64", 0, 514), [[1, 514]], A_.is_equal, -b, -4)
     for b in range(4):
@@ -283,10 +311,14 @@ def rank_program(g, core, T, topo):
     for j in range(8):
         fill(v("cwt", 512 * (j // 4) + j % 4, 512 * (j // 4) + 512, 4), WT if j // 4 == j % 4 // 2 else 0.0)
     qz("k", v("cwt"))
+    iota(v("xr", 0, 1), [[0, 1]], -1)
     for t in range(R):
-        iota(v("sv%d" % t, 0, O + 1), [[0, O + 1]], 1)
-        iota(v("sv%d" % t, O + 1 + L, O + 2 + L), [[0, 1]])
-    select(v("tat", 0, H), v("sv0", 0, H), [[1, H]], A_.is_gt, 0, -1)
+        if t < R - 1:
+            iota(v("sv%d" % t, O - 1, O + 1), [[0, 2]], 1)
+        a, b = (0, O + 1) if t else (O + 1, O + 1 + L)
+        iota(v("nv%d" % t, a, b), [[-1, b - a]], O - a)
+    iota(v("nv2", O + 1 + L, O + 2 + L), [[0, 1]])
+    select(v("tat", 0, H), v("c64", 0, H), [[1, H]], A_.is_gt, 0, -1)
     mset(v("rst"), 1.0)
     mset(v("rst", 0, W, 16), 0.0)
     mset(v("ones", 0, 8), 1)
@@ -356,8 +388,8 @@ def rank_program(g, core, T, topo):
                         trs.append(RemoteDMATransfer(dst_ids=[DstId(rid=rid, pnc=pid)], dma_engine_mask=_mask(eng[j % 2::2]),
                                                      remote_sem=T.sem["rel%d" % t], src=src, dst=dst))
                 g.remote_dma_fused(trs, local_sem=T.sem.sent)
-        call({"G": (1.0 if t else 3.0, send)}, [v("ql%d" % t), v("pl%d" % t)], [v("qm%d" % t), v("pm%d" % t)], ("arr%d" % t, narr),
-             WAY if t else FIRST)
+        call({"G": (1.0 if t else 3.0, send)}, [v("ql%d" % t), v("pl%d" % t)], [v("qm%d" % t), v("pm%d" % t)], ("arr%d" % t, narr))
+        calls[-1]["way"] = min(t, 1)
         calls[-1]["clear"] = 1.0
 
     col("cq", "q", 1.0, B - 176.0)
@@ -400,15 +432,18 @@ def rank_program(g, core, T, topo):
     tt(v("c2", 0, NC), v("cz", 0, NC), v("w1", 15, C, 16), sub)
     tt(v("c3", 0, NC), v("c2", 0, NC), v("w1", 15, C, 16), mx)
     ts(v("ciu", 0, NC), v("c3", 0, NC), -1.0, add)
-    ts(v("ciu1", 0, NC), v("c3", 0, NC), L + 1.0, mn, float(O), add)
+    ts(v("ciu2", 0, NC), v("c3", 0, NC), L + 1.0, mn, 1.0, add)
+    for h in range(2):
+        move(v("iol", h, C, 2), v("ca", C // 2 * h, C // 2 * (h + 1)))
     aff(v("cs", 0, C), v("crow", 0, C), 1.0, -176.0)
     cp(ix(v("pirow", 0, C), v("ciu", 0, NC)), v("cs", 0, C))
     scan(v("w2", 0, C), v("rmono", 0, C), v("pirow", 0, C), mx, mn)
     ts(v("piu", 0, NC), v("w2", 15, C, 16), 176.0, add)
     qz("x", v("xo", 8, 8 + 4 * C))
-    pick("a0", "x", v("piu", 0, NC))
+    pick("a0", "x", "piu", 0, 16)
+    pick("a0", "x", "piu", 16, NC)
     qz("u", v("ub"))
-    pick("u1", "u", v("ones", 0, 8))
+    pick("u1", "u", "ones", 0, 8)
     qz("v", v("vb"))
 
     def unpack_state(t, n):
@@ -498,42 +533,32 @@ def rank_program(g, core, T, topo):
         ts(v("lv", 0, 2), v("ec", 0, 2), 0.0, A_.not_equal)
         ts(v("nb", 0, 2), v("ec", 0, 2), 0.0, A_.is_equal, -BIG, mul)
         for h in range(2):
-            aff(v("th", H * h, H * h + H), v("tat", 0, H), TINY, v("nb", h, h + 1))
+            aff(v("th", H * h, H * h + H), v("tat", 0, H), TINY / 64, v("nb", h, h + 1))
 
     z_list(0)
 
     col("q1", "q", 1.0, -1.0)
-    col("dn88", "dn", 88.0)
-    col("ndy88", "ndy", 88.0)
-    col("dx3", "dx", 3.0)
     col("q25", "q4", -4.0, -2.5)
     aff(v("la"), v("m4"), 4.0, "q1")
     ts(v("s2"), v("la"), 1.0 / 17, mul, 1.0 / 17 - 0.47, add)
-    tt(v("s3"), v("la"), v("s2"), sub)
-    ts(v("lb"), v("s2"), 16.0, mul)
-    ts(v("s4"), v("s3"), 2, SHR)
-    ts(v("s5"), v("s3"), 3, AND)
-    tt(v("lc"), v("s3"), v("lb"), A_.is_lt)
-    ts(v("ld"), v("s5"), "ndx", mul, "dx3", add)
-    ts(v("le"), v("s5"), "ndy88", mul, "dn88", add)
-    tt(v("lf"), v("ld"), v("s4"), add)
-    act(v("lg"), v("lf"), F_.Abs, bias=-43.5)
-    act(v("lh"), v("lg"), F_.Relu, 2000.0, -88000.0)
-    aff(v("li"), v("lc"), 1000.0)
-    tt(v("lj"), v("lf"), v("le"), add)
-    tt(v("lk"), v("lj"), v("li"), add)
-    tt(v("ll"), v("lk"), v("lh"), add)
-    ts(v("pos2"), v("ll"), float(C), mn)
+    ts(v("s3"), v("la"), 1.0 / 17, mul, -0.47, add)
+    ts(v("lb"), v("s2"), 999.0, mul)
+    ts(v("lc"), v("s3"), -1000.0, mul)
+    tt(v("ld"), v("la"), v("lb"), add)
+    tt(v("le"), v("ld"), v("lc"), add)
+    ts(v("pos2"), v("le"), float(C), mn)
     act(v("t7"), v("irow", 0, W), F_.Abs, bias="q25")
     act(v("nt"), v("t7"), F_.Relu, -1.0, 2.0)
-    act(v("il"), ix(v("bc", 0, C + 1), v("pos2")), scale=-4.0)
+    act(v("o1", 0, C), ix(v("bc", 0, C + 1), v("posl", 0, NC)), scale=-4.0)
+    iota(v("o1", C, C + 1), [[0, 1]])
+    act(v("il"), ix(v("o1", 0, C + 1), v("pos2")), F_.Copy)
     scan(v("w10"), v("nt"), v("il"), mx, mul)
     scan(v("w8"), v("diag"), v("il"), mx, mul)
     act(v("n0"), v("w10"), F_.Relu, 1.0, 1.0)
     fill(v("n0", 0, W, 17), 0.0)
     act(v("t8"), v("il"), bias=-2048.0)
     scan(v("dl", 0, LW), v("t8", 1, LW + 1), v("t8", 0, LW), mn, sub)
-    table("lini", "w8", 24, "w9", -0.25, float(O))
+    table("lini", "w8", 24, "w9", -0.25, 1.0)
 
     for t in range(R):
         last = t == R - 1
@@ -542,24 +567,25 @@ def rank_program(g, core, T, topo):
             mm(b, "e", 128 * b, "l%d" % t, 0, 2 * NA)
         for b in range(4):
             act(v("tw", PW * b + 1, PW * b + O), ps(b, 0, 2 * NA), scale=1.0 / 64)
-        for h in range(2):
+            calls[-1]["early"] = X1[b]
+        for h in (1, 0):
             for b in range(4):
                 o, i = v("zt", 512 * h + b, 512 * h + 512, 4), ix(v("tw", PW * b, PW * b + O + 1 + L), v("zl", 8 * h, 8 * h + 8))
-                act(o, i, F_.Copy) if b % 2 else cp(o, i)
+                act(o, i, F_.Copy) if X2[4 * (1 - h) + b] == "S" else cp(o, i)
             qz("z", v("zt", 512 * h, 512 * h + 512), H * h, H * h + H)
-            calls[-1]["early"] = 0.5 * (1 - h)
+            calls[-1]["early"] = 0.5 * h
             mm(2 - h, "u1", 0, "z", H * h, H)
             mm(3 * h, "z", H * h, "u", 0, H)
         for b in range(4):
             mm(4 + b, "w", 128 * b, "z", 0, L, False, True)
             w = L if last else C
             aff(v(xn, 4 + b, 4 + 4 * w, 4), ps(4 + b, 0, w), 1.0 / 64)
-        for h in range(2):
+        for h in (1, 0):
             ts(v("sg", H * h, H * h + H), ps(2 - h, 0, H), ps(3 * h, 1, 2), sub)
             tt(v("cmp", 3 * h, 512, 4), v("sg", H * h, H * h + H), v("th", H * h, H * h + H), A_.is_lt)
             ts(v("cmp", 2 - h, 512, 4), ps(1 + h, 0, H), ps(3 * h, 1, 2), A_.is_lt if h else A_.is_le, v("lv", h, h + 1), mul)
         qz("c", v("cmp"))
-        for h in range(2):
+        for h in (1, 0):
             tt(v("sa", 1 + 10 * h, 9 + 10 * h), ps(3 * h, 0, H, 16), v("mk", 1 + 10 * h, 9 + 10 * h), mx)
             calls[-1]["early"] = 0.3
         scan(v("pmn", 1, 20), v("rs2", 0, 19), v("sa", 0, 19), mx, mn, 100 * BIG)
@@ -568,42 +594,48 @@ def rank_program(g, core, T, topo):
         mm(2, "c", 0, "k", H // 2, H)
         for h in range(2):
             mm(3 * h, "k", H * h, "c", 0, H)
-            act(v("xr", H * h, H * h + H), ps(3 * h, 0, H), F_.Relu, -1024.0, 1024.0)
-            ts(v("oh", h, 512, 2), v("iot", 0, L), v("nm", 8 + 10 * h, 9 + 10 * h), A_.is_equal,
-               ps(2, H // 2 - 1 + h, H // 2 + h), A_.is_gt)
-        qz("h", v("oh"))
+            act(v("xr", 1 + H * h, 1 + H * h + H), ps(3 * h, 0, H), F_.Relu, -1024.0, 1024.0)
+        w = C // 2 if last else H
         for h in range(2):
-            mm(1 + h, "k", H * h, "h", 0, H)
-            tt(v(sv, O + 1 + H * h, O + 1 + H * h + H), ps(1 + h, 0, H), v("xr", H * h, H * h + H), A_.is_le)
-        win = v(sv, 0, O + 2 + L)
+            ts(v("oh", h, 4 * w, 2), v("iol" if last else "iot", 0, 2 * w), v("nm", 8 + 10 * h, 9 + 10 * h), A_.is_equal,
+               ps(2, H // 2 - 1 + h, H // 2 + h), A_.is_gt)
+        qz("h", v("oh", 0, 4 * w), 0, w)
+        if last:
+            act(v("t5", 0, C), ix(v("xr", 0, L + 1), v("ciu1", 0, NC)), F_.Copy)
+        for h in range(2):
+            mm(1 + h, "k", H * h, "h", 0, w)
+            if last:
+                tt(v("olr", w * h, w * h + w), ps(1 + h, 0, w), v("t5", w * h, w * h + w), A_.is_le)
+            else:
+                tt(v(sv, O + 1 + H * h, O + 1 + H * h + H), ps(1 + h, 0, H), v("xr", 1 + H * h, 1 + H * h + H), A_.is_le)
         if last:
             break
+        win = v(sv, O - 1, O + 1 + L)
         tt(v("n%d" % (t + 1)), ix(win, v("lini")), v("n%d" % t), A_.is_le)
         scan(v("w1", 0, LW), v("n%d" % (t + 1), 0, LW), v("dl", 0, LW), mul, add)
         ts(v("cl%d" % (t + 1), 0, NC), v("w1", 16, LW, 17), "t4", add)
         compose_send(t + 1, xn)
         qz("a", v(xn, 4, 4 + 4 * C))
         unpack_state(t + 1, "a")
-        tt(v("g%d" % (t + 1), 0, RW), ix(win, v("rayi", 0, 23)), v("g%d" % t, 0, RW), mul)
-        scan(v("m%d" % (t + 1), 0, L), v(sv, O + 1, O + 1 + L), v("m%d" % t, 0, L), mx, mul)
+        for n, a in (("nv", O + 1), ("m", 0)):
+            scan(v(n + str(t + 1), a, a + L), v(sv, O + 1, O + 1 + L), v(n + str(t), a, a + L), mx, mul)
+        act(v("g%d" % (t + 1), 0, RW), ix(v("nv%d" % (t + 1), 0, O + 1 + L), v("rayi", 0, 23)), scale=-1.0)
         z_list(t + 1)
-        if t == 0:
-            act(v("o1", 0, C), ix(win, v("ciu1", 0, NC)), F_.Copy)
-        else:
-            tt(v("o2", 0, C), ix(win, v("ciu1", 0, NC)), v("o1", 0, C), mul)
+        if t == R - 2:
+            act(v("o1", 0, C), ix(v("nv2", O - 1, O + 2 + L), v("ciu2", 0, NC)), F_.Copy)
+            scan(v("o2", 0, C), v("diag", 0, C), v("o1", 0, C), mx, mul)
+            table("ciu1", "o2", NC, "w4", -1.0, 0.0)
 
-    tt(v("olr", 0, C), ix(win, v("ciu1", 0, NC)), v("o2", 0, C), mul)
-    store("Y", T.ol[:], v("olr", 0, C, 1, (0, 1)), DMA)
+    store("Y", T.ol[:], v("olr", 0, C, 1, (0, 1)), DMA + X3)
     qz("a3", v(xn, 4, 4 + 4 * C))
-    pick("f", "a3", v("ciu", 0, NC))
-    store("Y", T.oc[:], (T.qf[:].bitcast(dt.uint8),) + v("qf")[1:], DMA + 0.6)
+    for j, (a, b) in enumerate(((0, 192), (192, C))):
+        pick("f", "a3", "ciu", a // 16, b // 16)
+        store("Y", T.oc[:, 4 * a:4 * b], (T.qf[:, a:b].bitcast(dt.uint8),) + v("qf", a, b)[1:], DMA + 0.3)
+        mm(4 + j, "v", 0, "f", a, b - a)
+        move(v("ysb", a, b), ps(4 + j, 0, b - a))
+        store("S" if j else "Y", T.y[:, a:b], v("ysb", a, b), DMA + 0.3)
     for j in range(4):
         store("Y", T.osc[4 * j:4 * j + 4, :], v("pf", 0, C, 1, (32 * j, 32 * j + 4)), DMA)
-    for j in range(2):
-        a, b = C // 2 * j, C // 2 * (j + 1)
-        mm(4 + j, "v", 0, "f", a, C // 2)
-        move(v("ysb", a, b), ps(4 + j, 0, C // 2))
-        store("S" if j else "Y", T.y[:, a:b], v("ysb", a, b), DMA + 0.3)
 
     cnt = {"V": 0, "S": 0, "T": 0, "G": 0}
     know = {e: {} for e in Q}
@@ -622,10 +654,11 @@ def rank_program(g, core, T, topo):
                     if know[e].get(j, 0) < x:
                         know[e][j] = x
 
-    order = _order(calls)
-    for c in calls[:loads] + [c for c in order if c["n"] >= loads]:
-        e = c["e"]
-        need(e, [d["done"] for d in c["deps"] if not e == "T" == d["e"]])
+    if not ORDER:
+        ORDER.extend(_order(calls))
+    for n, e in sorted(x for x in ORDER if x[0] < loads) + [x for x in ORDER if x[0] >= loads]:
+        c = calls[n]
+        need(e, [d["done"] for d in c["deps"] if not (e == "T" and "T" in d["ways"])])
         if c["tok"]:
             c["ways"][e][1]()
             c["done"] = c["tok"] + ({},)
@@ -633,4 +666,4 @@ def rank_program(g, core, T, topo):
             cnt[e] += 1
             c["ways"][e][1]().then_inc(T.sem["c" + e], 1)
             c["done"] = ("c" + e, cnt[e], dict(know[e]))
-    need("G", [("c" + e, cnt[e], {}) for e in cnt] + [("sent", R * 4 * ne, {}), ("dout", 128, {})])
+    need("G", [("c" + e, cnt[e], {}) for e in cnt] + [("sent", R * 4 * ne, {}), ("dout", 16 * 9, {})])

from concourse.bass import DstId, RemoteDMATransfer
from concourse.mybir import dt, AluOpType, ActivationFunctionType

A_ = AluOpType
F_ = ActivationFunctionType
C, L, NA, M, R = 352, 256, 88, 40, 3
H, NC = L // 2, C // 16
O = 2 * NA + 1
PW = 448
RW, LW, W = 368, 22 * 17, 384
B = 4096.0
BIG = 1e26
TINY = 1e-35
WT = 13.0 / 512
f32, bf, i32, u16, cod, pl = "float32", "bfloat16", "int32", "uint16", "float8_e4m3fn_x4", "uint8"
f16 = "float16"
CYC, HOP, DMA = 0.83e-3, 0.22, 1.5
WAYS = [(1.5, 1.0), (2.5, 1.0), (3.0, 1.5), (3.5, 1.0), (3.5, 2.0), (4.0, 1.5), (4.0, 2.7)]
X1, X2 = (0.6, 0.2, 0.4, 0.0), "VSVSVSVV"
PASSES = 3
X3 = 0.0
ORDER = []
SPARE = 0.2


def _sb(n, d):
    return ("sbuf", [128, n], d)


SCRATCH = {"ci": _sb(8, i32), "cf": _sb(96, f32), "aw": _sb(24, i32), "sw": _sb(24, i32), "irow": _sb(23 * 17, f32)}
PART = {}
for _b, _d, _w, _names in (
        ("offs", u16, 24, "seatu l1 posl pos2 rayl ones ciu ciu1 ciu2 piu rayi lini cl0 cl1 cl2 ipos zl"),
        ("whole", i32, 24, "s0 s1 s2 s3 s4 s5"),
        ("small", f32, 24, "m4 b2 cw oiw e1 e2 cz c2 c3 ab2 sr e3 e4 gi sf ec idb dd mk sa pmn nn nm rs2 sc lv nb "
                           "la lb lc ld le lf lg lh li lj lk ll"),
        ("rows32", f32, W, "crow jj t5 t6 t7 t8 pm olr ysb xr"),
        ("rows16", f16, W, "h1 h2 h3 h4 h5"),
        ("rows", bf, W, "rst diag rmono t4 a1 bo fl cum ca cs nrow pirow rp w1 w2 w3 w4 w5 w6 w7 w8 w9 w10 il g0 g1 g2 gn er t2 t3 ett et2 "
                        "m0 m1 m2 o1 o2 nt dl n0 n1 n2 tau tat th iot iol sg"),
        ("wide", bf, PW, "bc sv0 sv1 nv0 nv1 nv2")):
    SCRATCH[_b] = _sb(_w * len(_names.split()), _d)
    PART.update({_n: (_b, _w * _j, _w) for _j, _n in enumerate(_names.split())})
for _n, _w in dict(xo=8 + 4 * C, ub=512, vb=512, c64=520, ea=520, eb=520, cwt=4 * L, ct=512, tw=4 * PW, zt=4 * L, cmp=512, oh=2 * C,
                   xn1=4 + 4 * C, xn2=4 + 4 * C, xn3=4 + 4 * C).items():
    SCRATCH[_n] = _sb(_w, bf)
for _n, _w in dict(x=C, u=128, u1=128, v=128, w=512, e=512, k=L, z=L, c=128, h=C // 2, a0=C, a=C, a3=C, f=C, m0=128, m1=128, m2=128,
                   r0=NA, r1=NA, r2=NA, l0=2 * NA, l1=2 * NA, l2=2 * NA).items():
    SCRATCH["q" + _n], SCRATCH["p" + _n] = _sb(_w, cod), _sb(_w, pl)
for _b in range(8):
    SCRATCH["bank%d" % _b] = ("psum", [128, 512], f32)

SEMAPHORES = (["cV", "cS", "cT", "cG", "dal", "dse", "dx", "du", "dv", "dw", "dout", "sent"]
              + ["arr%d" % t for t in range(R)] + ["rel%d" % t for t in range(R)])


def _relays(T, topo, rank):
    me, n = T.cores[rank], len(T.cores)
    dsts = [(rank + 1) % n, (rank - 1) % n]
    ok = [c for c in topo.cores_of(me) if T.rank_of(c) is None and all(topo.may_write(c, T.cores[d]) for d in dsts)]
    ok.sort(key=lambda c: (topo.die(c) != topo.die(me), c))
    return [(ok[0], dsts[0], True), (ok[2], dsts[1], True), (ok[3], dsts[0], False), (ok[1], dsts[1], False)]


def _mask(es):
    m = 0
    for e in es:
        m |= 1 << e
    return m


def _relay_program(g, core, T, topo):
    n = len(T.cores)
    for r in range(n):
        if core not in topo.cores_of(T.cores[r]):
            continue
        for c, d, codes in _relays(T, topo, r):
            if c != core:
                continue
            dst = T.cores[d]
            rid, pid = topo.addr(dst, core)
            off = 0 if d == (r + 1) % n else NA
            ne = len(topo.engines(T.cores[r], core)) // 2
            nout = len(topo.engines(core, dst))
            for t in range(R):
                g.wait_ge(T.sem["rel%d" % t], ne)
                if codes:
                    o, i = T["ql%d" % t][:, off:off + NA].bitcast(dt.uint8), T["qr%d" % t][:].bitcast(dt.uint8)
                else:
                    o, i = T["pl%d" % t][:, off:off + NA], T["pr%d" % t][:]
                g.remote_dma(o, i, T.sem["arr%d" % t], T.sem.sent, pid, rid, topo.mask(core, dst))
            g.wait_ge(T.sem.sent, R * nout)


def _order(calls):
    def late(c, way):
        return way[c["way"]] if "way" in c else c["late"]

    def place(rank, back, way):
        busy = {}
        for c in sorted(calls, key=lambda c: (rank[c["n"]], -c["n"] if back else c["n"])):
            best = None
            for e, (us, _) in c["ways"].items():
                t = max([x["end"] + (0.0 if e == "T" == x["e"] else HOP) for x in c["next" if back else "deps"]], default=0.0)
                t += late(c, way) if back else 0.0
                for a, b in busy.get(e, []):
                    if t + us <= a:
                        break
                    t = max(t, b)
                if best is None or t + us + SPARE < best[0] + best[2]:
                    best = t, e, us
            t, e, us = best
            c["start"], c["e"], c["end"] = t, e, t + us + (0.0 if back else late(c, way))
            clear = c.get("clear", 0.0)
            busy[e] = sorted(busy.get(e, []) + [(t, t + us + clear) if back else (t - clear, t + us)])
        return [(c["n"], c["e"]) for c in sorted(calls, key=lambda c: (c["start"], c["n"]))]

    def takes(order, way):
        free, end = {}, {}
        for n, e in order:
            c = calls[n]
            t = max([free.get(e, 0.0)] + [end[x["n"]][0] + (0.0 if e == "T" == end[x["n"]][1] else HOP) for x in c["deps"]])
            free[e] = t + c["ways"][e][0]
            end[n] = free[e] + late(c, way), e
        return max(x[0] for x in end.values())

    orders = []
    for way in WAYS:
        for c in reversed(calls):
            c["chain"] = (min(x[0] for x in c["ways"].values()) + late(c, way) + c.get("early", 0.0)
                          + max([HOP + x["chain"] for x in c["next"]], default=0.0))
        orders.append(place([-c["chain"] for c in calls], False, way))
        for _ in range(PASSES):
            place([-c["end"] for c in calls], True, way)
            orders.append(place([-c["end"] for c in calls], False, way))
    return min(orders, key=lambda o: takes(o, WAYS[0]) + takes(o, WAYS[-1]))


def rank_program(g, core, T, topo):
    rank = T.rank_of(core)
    if rank is None:
        _relay_program(g, core, T, topo)
        return
    V, S, P, Y = g.vector, g.scalar, g.tensor, g.sync
    Q = {"V": V, "S": S, "T": P, "G": g, "Y": Y}
    calls = []
    seen = {}

    def v(n, a=0, b=None, s=1, p=(0, 128)):
        if n in PART:
            n, j, w = PART[n]
            a, b = j + a, j + (w if b is None else b)
        b = SCRATCH[n][1][1] if b is None else b
        cols = range(a, b, s)
        return T[n][p[0]:p[1], a:b:s], [(n, p[0], p[1], -1 if n.startswith("bank") else _mask(cols))], len(cols)

    def words(w):
        return w[0].bitcast(dt.uint32), w[1], w[2]

    def ix(w, off):
        return w[0].indirect(off[0]), w[1] + off[1], 16 * off[2]

    def call(ways, outs, ins, tok=None, late=0.0):
        r = [x for i in ins if isinstance(i, tuple) for x in i[1]] + [x for o in outs for x in o[1][1:]]
        w = [o[1][0] for o in outs]
        c = {"ways": ways, "tok": tok, "late": late, "n": len(calls), "deps": [], "next": []}
        for regs, writes in ((r, False), (w, True)):
            for n, a, b, bits in regs:
                for x in seen.get(n, []):
                    other = n.startswith("bank") and (len(ways) > 1 or list(ways) != list(x[3]["ways"]))
                    if (writes or x[4] or other) and x[0] < b and a < x[1] and x[2] & bits and all(x[3] is not d for d in c["deps"]):
                        c["deps"].append(x[3])
                        x[3]["next"].append(c)
        for n, a, b, bits in w:
            seen[n] = [x for x in seen.get(n, []) if not (a <= x[0] and x[1] <= b and x[2] & ~bits == 0)] + [(a, b, bits, c, True)]
        for n, a, b, bits in r:
            seen.setdefault(n, []).append((a, b, bits, c, False))
        calls.append(c)

    def cost(out, ins, per=None):
        if len(out[1]) > 1:
            return 0.05 + 3.5 * CYC * out[2]
        if len(ins[0][1]) > 1:
            return 0.06 + 1.5 * CYC * out[2]
        if per is None:
            per = 0.5 if all(SCRATCH[x[1][0][0]][2] in (bf, f16, u16) for x in [out] + ins) else 1.0
        return CYC * max(64, per * out[2])

    names = {}

    def k(n):
        j = names.setdefault(n, len(names))
        return v("cf", j, j + 1)

    def arg(x):
        return k(x) if isinstance(x, str) else x

    def ap(x):
        return x[0] if isinstance(x, tuple) else x

    def load(e, out, in_, sem, total, late=DMA):
        call({e: (0.05, lambda: Q[e].dma_start(out[0], in_).then_inc(T.sem[sem], 16))}, [out], [], (sem, total), late)

    def store(e, out, in_, late):
        call({e: (0.05, lambda: Q[e].dma_start(out, in_[0]).then_inc(T.sem.dout, 16))}, [], [in_], ("dout", 128), late)

    def ts_way(out, a, s1, o0, s2, o1):
        if o1 is None:
            return cost(out, [a]), lambda: V.tensor_scalar(out[0], a[0], ap(s1), None, o0)
        return cost(out, [a]), lambda: V.tensor_scalar(out[0], a[0], ap(s1), ap(s2), o0, o1)

    def act_way(out, a, f, scale, bias):
        if f == F_.Copy:
            return cost(out, [a], 1.0) + 0.02, lambda: S.activation(out[0], a[0], f)
        return cost(out, [a], 1.0) + 0.02, lambda: S.activation(out[0], a[0], f, bias=ap(bias), scale=ap(scale))

    def ts(out, a, s1, o0, s2=None, o1=None):
        s1, s2 = arg(s1), arg(s2)
        call({"V": ts_way(out, a, s1, o0, s2, o1)}, [out], [a, s1, s2])

    def act(out, a, f=F_.Identity, scale=1.0, bias=0.0):
        scale, bias = arg(scale), arg(bias)
        call({"S": act_way(out, a, f, scale, bias)}, [out], [a, scale, bias])

    def aff(out, a, scale=1.0, bias=0.0):
        scale, bias = arg(scale), arg(bias)
        call({"S": act_way(out, a, F_.Identity, scale, bias), "V": ts_way(out, a, scale, mul, bias, add)}, [out], [a, scale, bias])

    def move(out, a):
        call({"S": act_way(out, a, F_.Copy, 1.0, 0.0), "V": (cost(out, [a]), lambda: V.tensor_copy(out[0], a[0]))}, [out], [a])

    def tt(out, a, b, o):
        per = 1.0 if a[1][0][0].startswith("bank") else 2.0
        call({"V": (cost(out, [a], per), lambda: V.tensor_tensor(out[0], a[0], b[0], o))}, [out], [a, b])

    def cp(out, a):
        call({"V": (cost(out, [a]), lambda: V.tensor_copy(out[0], a[0]))}, [out], [a])

    def scan(out, a, b, o0, o1, init=0.0):
        call({"V": (cost(out, [a, b]), lambda: V.tensor_tensor_scan(out[0], a[0], b[0], init, o0, o1))}, [out], [a, b])

    def turn(out, a):
        call({"V": (cost(out, [a]), lambda: V.transpose(out[0], a[0]))}, [out], [a])

    def mset(out, x):
        call({"V": (cost(out, [out]), lambda: V.memset(out[0], x))}, [out], [])

    def fill(out, x):
        a = v("jj", 0, out[2])
        call({"S": act_way(out, a, F_.Identity, 0.0, float(x)), "V": (cost(out, [out]), lambda: V.memset(out[0], x))}, [out], [a])

    def qz(n, t, a=0, b=None):
        q, p = v("q" + n, a, b), v("p" + n, a, b)
        call({"V": (0.012 + 0.22e-3 * t[2], lambda: V.quantize_mx(q[0], p[0], t[0]))}, [q, p], [t])

    def ps(b, a=0, e=512, s=1):
        return v("bank%d" % b, a, e, s)

    def mm(b, l, l0, rr, r0, n, start=True, stop=True):
        x = [v("q" + l, l0, l0 + 128), v("p" + l, l0, l0 + 128), v("q" + rr, r0, r0 + n), v("p" + rr, r0, r0 + n)]
        o = ps(b, 0, n)
        call({"T": (1.25 * CYC * (n + 16), lambda: P.matmul_mx(o[0], x[0][0], x[1][0], x[2][0], x[3][0], start, stop))}, [o], x)

    def pick(to, fr, off, a, b):
        act(v("p" + to, 16 * a, 16 * b), ix(v("p" + fr), v(off, a, b)), F_.Copy)
        cp(words(v("q" + to, 16 * a, 16 * b)), ix(words(v("q" + fr)), v(off, a, b)))

    def iota(out, pat, base=0):
        call({"G": (0.13 + 2 * CYC * out[2], lambda: g.iota(out[0], pat, base, 0, allow_small_or_imprecise_dtypes=True))}, [out], [])

    def select(out, a, pat, o, base, ch):
        call({"G": (0.17 + 2 * CYC * out[2], lambda: g.affine_select(out[0], a[0], pat, o, 0.0, base, ch))}, [out], [a])

    def col(n, a, scale=1.0, bias=0.0):
        aff(k(n), k(a), scale, bias)

    def relu(n, a, scale):
        act(k(n), k(a), F_.Relu, scale)

    def table(off, row, n, w, scale, bias):
        scan(v(w, 0, 16 * n), v("rst", 0, 16 * n), v(row, 0, 16 * n), mul, add)
        ts(v(off, 0, n), v(w, 15, 16 * n, 16), scale, mul, bias, add)

    add, sub, mul, mx, mn = A_.add, A_.subtract, A_.mult, A_.max, A_.min
    AND, SHR = A_.bitwise_and, A_.logical_shift_right

    for j in range(8):
        load("Y" if j % 2 else "S", v("aw", 0, NC, 1, (16 * j, 16 * j + 16)), T.alive[:], "dal", 128)
    load("S", v("sw", 0, NC), T.seat[:], "dse", 16)
    load("Y", v("xo", 8, 8 + 4 * C), T.x[:], "dx", 16, 2 * DMA)
    load("Y", v("ub"), T.u[:], "du", 16, 2 * DMA)
    load("Y", (T.qw[:].bitcast(dt.uint8),) + v("qw")[1:], T.wc[:], "dw", 32, 3 * DMA)
    load("Y", v("pw"), T.ws[:], "dw", 32, 3 * DMA)
    load("Y", v("vb"), T.v[:], "dv", 16, 3 * DMA)
    loads = len(calls)

    pi = v("ci", 5, 6)
    call({"G": (0.13, lambda: g.iota(pi[0], [[0, 1]], 0, 1))}, [pi], [])
    iota(v("b2", 0, NC), [[2, 11], [0, 2]])
    iota(v("m4"), [[4, 24]])
    iota(v("jj"), [[0, 24], [4096, 4], [512, 4]])
    iota(v("crow", 0, C), [[1, C]])
    iota(v("irow"), [[0, 23], [1, 17]])
    iota(v("iot", 0, L), [[1, H], [H, 2]], 1)
    mset(v("c64"), 64.0)
    calls[-1]["early"] = 8.0
    for n, b in (("ea", 2), ("eb", 3)):
        select(v(n, 0, 514), v("c64", 0, 514), [[1, 514]], A_.is_equal, -b, -4)
    for b in range(4):
        qz("e", v("eb" if b % 2 else "ea", 2 - b // 2 * 2, 514 - b // 2 * 2), 128 * b, 128 * b + 128)
    for j in range(8):
        fill(v("cwt", 512 * (j // 4) + j % 4, 512 * (j // 4) + 512, 4), WT if j // 4 == j % 4 // 2 else 0.0)
    qz("k", v("cwt"))
    iota(v("xr", 0, 1), [[0, 1]], -1)
    for t in range(R):
        if t < R - 1:
            iota(v("sv%d" % t, O - 1, O + 1), [[0, 2]], 1)
        a, b = (0, O + 1) if t else (O + 1, O + 1 + L)
        iota(v("nv%d" % t, a, b), [[-1, b - a]], O - a)
    iota(v("nv2", O + 1 + L, O + 2 + L), [[0, 1]])
    select(v("tat", 0, H), v("c64", 0, H), [[1, H]], A_.is_gt, 0, -1)
    mset(v("rst"), 1.0)
    mset(v("rst", 0, W, 16), 0.0)
    mset(v("ones", 0, 8), 1)
    for n, a, b, s in (("xn1", 0, 4, 1), ("xn2", 0, 4, 1), ("bc", C, PW, 93), ("tw", 0, 4 * PW, PW), ("tw", O, 4 * PW, PW),
                       ("idb", 0, 24, 1)):
        iota(v(n, a, b, s), [[0, len(range(a, b, s))]])
    for n, a, b, s, x in (("xo", 0, 8, 1, 0.0), ("ct", 4 * NA, 512, 1, 0.0), ("bo", C, C + 8, 1, -B), ("sa", 0, 11, 10, BIG),
                          ("sa", 9, 10, 1, 100 * BIG), ("rs2", 0, 9, 1, -100 * BIG), ("rs2", 10, 19, 1, -100 * BIG),
                          ("rs2", 9, 10, 1, 100 * BIG), ("pmn", 0, 1, 1, 100 * BIG)):
        fill(v(n, a, b, s), x)
    for j, n in enumerate(("q", "g", "q4", "t4", "go")):
        k(n)
    ts(v("ci", 0, 1), pi, 15, AND)
    ts(v("ci", 1, 2), pi, 4, SHR)
    ts(v("ci", 2, 3), pi, 2, SHR, 3, AND)
    ts(v("ci", 3, 4), pi, 3, AND)
    ts(v("ci", 4, 5), pi, 4, SHR, 1, AND)
    cp(v("cf", 0, 5), v("ci", 0, 5))
    ts(k("up"), pi, 16.0 * 3, A_.is_lt)
    ts(k("lo"), pi, 16.0 * 4, A_.is_lt, 3.0, add)
    ts(k("dy"), pi, 16.0 * 5, A_.is_ge, "up", sub)
    ts(k("gp"), k("g"), "lo", sub)
    col("dx", "dy", -3.0, "gp")
    col("vert", "dy", "dy")
    col("hz", "vert", -1.0, 1.0)
    col("hd", "dx", "hz")
    col("ndy", "dy", -1.0)
    col("ndx", "dx", -1.0)
    col("v4", "vert", 4.0)
    relu("neg", "dx", -1.0)
    relu("pos", "dx", 1.0)
    relu("dn", "dy", 3.0)
    col("j0", "q4", 4096.0)
    col("jq", "t4", 512.0, "j0")
    col("nq", "jq", -1.0)
    col("rq", "jq", 2000.0, 5e5)
    act(v("t6"), v("jj"), F_.Abs, bias="nq")
    act(v("diag"), v("t6"), F_.Relu, -1.0, 1.0)
    aff(v("rmono", 0, C), v("jj", 0, C), -2000.0, "rq")
    aff(v("m0", 0, L), v("diag", 0, L), -1.0)

    rel = _relays(T, topo, rank)
    eng = topo.engines(core, rel[0][0])
    ne = len(eng) // 2
    narr = sum(len(topo.engines(c, core)) for r2 in range(len(T.cores)) for c, d, _ in _relays(T, topo, r2) if d == rank)

    def both(out, win, off, bias=None):
        for a, b, one in ((0, 12, cp), (12, NC, None)):
            o, i = v(out, 16 * a, 16 * b), ix(win, v(off, a, b))
            if bias is None:
                cp(o, i) if one else act(o, i, F_.Copy)
            else:
                ts(o, i, bias, add) if one else act(o, i, bias=bias)

    def compose_send(t, xbuf):
        both("ct", v(xbuf), "cl%d" % t)
        qz("m%d" % t, v("ct"))

        def send():
            for codes in (True, False):
                trs = []
                for j, (c, d, cs) in enumerate(rel):
                    if cs == codes:
                        rid, pid = topo.addr(c, core)
                        src = T["qm%d" % t][:, 0:NA].bitcast(dt.uint8) if codes else T["pm%d" % t][:, 0:NA]
                        dst = T["qr%d" % t][:].bitcast(dt.uint8) if codes else T["pr%d" % t][:]
                        trs.append(RemoteDMATransfer(dst_ids=[DstId(rid=rid, pnc=pid)], dma_engine_mask=_mask(eng[j % 2::2]),
                                                     remote_sem=T.sem["rel%d" % t], src=src, dst=dst))
                g.remote_dma_fused(trs, local_sem=T.sem.sent)
        call({"G": (1.0 if t else 3.0, send)}, [v("ql%d" % t), v("pl%d" % t)], [v("qm%d" % t), v("pm%d" % t)], ("arr%d" % t, narr))
        calls[-1]["way"] = min(t, 1)
        calls[-1]["clear"] = 1.0

    col("cq", "q", 1.0, B - 176.0)
    aff(v("cw", 0, NC), v("m4", 0, NC), 4.0, "cq")
    ts(v("l1", 0, NC), v("b2", 0, NC), "go", add)
    tt(v("oiw", 0, NC), v("aw", 0, NC), v("cw", 0, NC), mul)
    cp(v("seatu", 0, NC), v("sw", 0, NC))
    both("t4", v("oiw", 0, NC), "l1", -B)
    turn(v("a1", 0, C), v("t4", 0, C))
    both("bo", v("a1", 0, C), "seatu")
    col("u3", "t4", -1.0, 3.0)
    col("y1", "t4", 88.0, -132.0)
    col("y2", "y1", "ndy", 132.0)
    col("w1", "dx", "u3", "q4")
    col("pb", "w1", 1.0, "y2")
    ts(k("b0"), k("w1"), 0.0, A_.is_lt, 1000.0, mul)
    ts(k("b1"), k("w1"), 3.0, A_.is_gt, 1000.0, mul)
    ts(k("b2"), k("b1"), NA - 4.0, add, "pb", add)
    ts(v("posl", 1, NC - 1), v("m4", 1, NC - 1), "pb", add)
    ts(v("posl", 0, 1), k("b0"), "pb", add, float(C), mn)
    ts(v("posl", NC - 1, NC), k("b2"), float(C), mn)
    col("pk", "q4", -4096.0, -1536.0)
    act(v("t5", 0, C), v("jj", 0, C), F_.Abs, bias="pk")
    aff(v("pm", 0, C), v("t5", 0, C), -1.0, 1536.0 + O + 1)
    tt(v("h1", 0, C), ix(v("bo", 0, C + 8), v("posl", 0, NC)), v("pm", 0, C), add)
    scan(v("h2", 0, C), v("rst", 0, C), v("h1", 0, C), mul, mx)
    cp(v("s0", 0, NC), v("h2", 15, C, 16))
    ts(v("s1", 0, NC), v("s0", 0, NC), 511, AND)
    ts(v("cl0", 0, NC), v("s1", 0, NC), 4.0, mul, "t4", add)
    compose_send(0, "xo")

    ts(v("fl", 0, C), v("a1", 0, C), -1000.0, A_.is_gt)
    scan(v("cum", 0, C), v("fl", 0, C), v("fl", 0, C), add, mx)
    scan(v("ca", 0, C), v("cum", 0, C), v("fl", 0, C), mx, mul)
    act(v("bc", 0, C), ix(v("ca", 0, C), v("seatu", 0, NC)), F_.Copy)
    scan(v("w1", 0, C), v("rmono", 0, C), v("cum", 0, C), mx, mn)
    aff(v("e1", 0, NC), v("cw", 0, NC), 1.0, 176.0 + L + 1 - B)
    ts(v("e2", 0, NC), v("aw", 0, NC), 0.0, A_.is_equal)
    tt(v("cz", 0, NC), v("e1", 0, NC), v("e2", 0, NC), mul)
    tt(v("c2", 0, NC), v("cz", 0, NC), v("w1", 15, C, 16), sub)
    tt(v("c3", 0, NC), v("c2", 0, NC), v("w1", 15, C, 16), mx)
    ts(v("ciu", 0, NC), v("c3", 0, NC), -1.0, add)
    ts(v("ciu2", 0, NC), v("c3", 0, NC), L + 1.0, mn, 1.0, add)
    for h in range(2):
        move(v("iol", h, C, 2), v("ca", C // 2 * h, C // 2 * (h + 1)))
    aff(v("cs", 0, C), v("crow", 0, C), 1.0, -176.0)
    cp(ix(v("pirow", 0, C), v("ciu", 0, NC)), v("cs", 0, C))
    scan(v("w2", 0, C), v("rmono", 0, C), v("pirow", 0, C), mx, mn)
    ts(v("piu", 0, NC), v("w2", 15, C, 16), 176.0, add)
    qz("x", v("xo", 8, 8 + 4 * C))
    pick("a0", "x", "piu", 0, 16)
    pick("a0", "x", "piu", 16, NC)
    qz("u", v("ub"))
    pick("u1", "u", "ones", 0, 8)
    qz("v", v("vb"))

    def unpack_state(t, n):
        w = C if t == R - 1 else L
        for b in range(4):
            mm(b, "e", 128 * b, n, 0, w)
        for b in range(4):
            mm(4 + b, "e", 128 * b, n, 0, C + L - w, True, False)
        for b in range(4):
            aff(v("tw", PW * b + O + 1, PW * b + O + 1 + L), ps(b, 0, L), 1.0 / 64)
            if w == C:
                aff(v("xn%d" % (t + 1), 4 + 4 * L + b, 4 + 4 * C, 4), ps(b, L, C), 1.0 / 64)

    unpack_state(0, "a0")

    col("d", "t4", 1.0, -1.0)
    relu("hd0", "d", -1.0)
    col("d15", "t4", 88.0, -220.0)
    col("q176", "q", -1.0, 176.5)
    col("q353", "q4", 1.0, C + 1.0)
    col("n3", "neg", -3.0, "q4")
    col("slope", "hd", -16.0, "v4")
    col("r88", "d15", "ndy", 132.0)
    col("sH", "hd", "q176")
    col("po", "ndx", "d", "n3")
    col("off", "hd0", 1.0, "hz")
    col("sH2", "hz", 175.5, "sH")
    col("po1", "po", 1.0, -43.5)
    col("po2", "po", 1.0, "r88")
    col("df", "po2", -1.0, "q353")
    col("lim", "off", -1e6, -88000.0)
    col("po3", "df", "hd0", "po2")
    col("sA", "po3", "vert", "sH2")
    act(v("ab2", 0, 23), v("m4", 0, 23), F_.Abs, bias="po1")
    act(v("e3", 0, 23), v("ab2", 0, 23), F_.Relu, 2000.0, "lim")
    aff(v("sr", 0, 23), v("crow", 0, 23), "slope", "sA")
    tt(v("e4", 0, 23), v("e3", 0, 23), v("sr", 0, 23), add)
    ts(v("rayl", 0, 23), v("e4", 0, 23), C + 93.0, mn)
    col("cH", "neg", -3.0, "dx")
    col("bs", "dy", 44.0, -132.0)
    col("cH3", "cH", 1.0, "bs")
    col("nneg", "neg", -1.0, 1.0)
    col("npos", "pos", -1.0, 1.0)
    for n in ("neg", "pos", "nneg", "hz"):
        col(n + "O", n, -float(O))
    aff(v("w3", 0, 92), v("crow", 0, 92), 1.0, "cH3")
    for a, b, s1, s2 in ((0, 4, "nneg", "negO"), (4, 87, 1.0, 0.0), (87, 88, "npos", "posO"), (88, 92, "neg", "nnegO")):
        aff(v("bc", C + 1 + a, C + 1 + b), v("w3", a, b), s1, s2)
    act(v("g0", 0, RW), ix(v("bc", 0, C + 94), v("rayl", 0, 23)), F_.Copy)
    aff(v("g0", 0, C, NA), v("g0", 0, C, NA), "vert", "hzO")
    ts(v("h3", 0, RW), v("g0", 0, RW), -float(L), add)
    scan(v("h4", 0, RW), v("diag", 0, RW), v("h3", 0, RW), mx, mul)
    table("rayi", "h4", 23, "h5", 1.0, float(O + L))
    col("k41", "dx", 4.0, 1.0)
    col("n12", "neg", 12.0)
    relu("g4", "hd", 351.0)
    col("g5", "g4", 1.0, -184.0)
    col("alpha", "hd", -1.0, "v4")
    col("h88", "hd", -88.0)
    col("beta", "k41", "ndy", "h88")
    col("g1", "n12", "vert", "g5")
    col("gam", "k41", "dn", "g1")
    aff(v("gi", 0, 4), v("crow", 0, 4), "beta", "gam")
    for i in range(4):
        aff(v("nrow", NA * i, NA * i + NA), v("crow", 0, NA), "alpha", v("gi", i, i + 1))
    cp(ix(v("rp", 0, C), v("seatu", 0, NC)), v("nrow", 0, C))
    tt(v("w6", 0, L), ix(v("rp", 0, C), v("piu", 0, 16)), v("diag", 0, L), mul)
    table("ipos", "w6", 16, "w7", 1.0, 184.0)

    def z_list(t):
        gt = v("g%d" % t, 0, RW)
        ts(v("gn", 0, RW), gt, 0.0, A_.is_equal)
        scan(v("er", 0, RW), v("gn", 0, RW), gt, mul, add)
        tt(v("t2", 0, L), ix(v("er", 0, RW), v("ipos", 0, 16)), v("m%d" % t, 0, L), mul)
        table("zl", "t2", 16, "t3", -1.0, float(O))
        turn(v("ett", 0, L), v("t2", 0, L))
        scan(v("et2", 0, L), v("rst", 0, L), v("ett", 0, L), mul, add)
        for h in range(2):
            aff(v("sf", h, 16, 2), v("et2", H * h + 15, H * h + H, 16), -1.0)
        for a in range(4):
            for a2 in range(4):
                move(v("ec", 4 * a, 4 * a + 4, 1, (32 * a2, 32 * a2 + 32)), v("sf", 4 * a2, 4 * a2 + 4, 1, (32 * a, 32 * a + 32)))
        for h in range(2):
            move(v("idb", 1 + 10 * h, 9 + 10 * h), v("ec", h, 16, 2))
            aff(v("mk", 1 + 10 * h, 9 + 10 * h), v("ec", h, 16, 2), -20 * BIG, 10 * BIG)
        tt(v("dd", 0, 19), v("idb", 0, 19), v("idb", 1, 20), sub)
        ts(v("lv", 0, 2), v("ec", 0, 2), 0.0, A_.not_equal)
        ts(v("nb", 0, 2), v("ec", 0, 2), 0.0, A_.is_equal, -BIG, mul)
        for h in range(2):
            aff(v("th", H * h, H * h + H), v("tat", 0, H), TINY / 64, v("nb", h, h + 1))

    z_list(0)

    col("q1", "q", 1.0, -1.0)
    col("q25", "q4", -4.0, -2.5)
    aff(v("la"), v("m4"), 4.0, "q1")
    ts(v("s2"), v("la"), 1.0 / 17, mul, 1.0 / 17 - 0.47, add)
    ts(v("s3"), v("la"), 1.0 / 17, mul, -0.47, add)
    ts(v("lb"), v("s2"), 999.0, mul)
    ts(v("lc"), v("s3"), -1000.0, mul)
    tt(v("ld"), v("la"), v("lb"), add)
    tt(v("le"), v("ld"), v("lc"), add)
    ts(v("pos2"), v("le"), float(C), mn)
    act(v("t7"), v("irow", 0, W), F_.Abs, bias="q25")
    act(v("nt"), v("t7"), F_.Relu, -1.0, 2.0)
    act(v("o1", 0, C), ix(v("bc", 0, C + 1), v("posl", 0, NC)), scale=-4.0)
    iota(v("o1", C, C + 1), [[0, 1]])
    act(v("il"), ix(v("o1", 0, C + 1), v("pos2")), F_.Copy)
    scan(v("w10"), v("nt"), v("il"), mx, mul)
    scan(v("w8"), v("diag"), v("il"), mx, mul)
    act(v("n0"), v("w10"), F_.Relu, 1.0, 1.0)
    fill(v("n0", 0, W, 17), 0.0)
    act(v("t8"), v("il"), bias=-2048.0)
    scan(v("dl", 0, LW), v("t8", 1, LW + 1), v("t8", 0, LW), mn, sub)
    table("lini", "w8", 24, "w9", -0.25, 1.0)

    for t in range(R):
        last = t == R - 1
        xn, sv = "xn%d" % (t + 1), "sv%d" % t
        for b in range(4):
            mm(b, "e", 128 * b, "l%d" % t, 0, 2 * NA)
        for b in range(4):
            act(v("tw", PW * b + 1, PW * b + O), ps(b, 0, 2 * NA), scale=1.0 / 64)
            calls[-1]["early"] = X1[b]
        for h in (1, 0):
            for b in range(4):
                o, i = v("zt", 512 * h + b, 512 * h + 512, 4), ix(v("tw", PW * b, PW * b + O + 1 + L), v("zl", 8 * h, 8 * h + 8))
                act(o, i, F_.Copy) if X2[4 * (1 - h) + b] == "S" else cp(o, i)
            qz("z", v("zt", 512 * h, 512 * h + 512), H * h, H * h + H)
            calls[-1]["early"] = 0.5 * h
            mm(2 - h, "u1", 0, "z", H * h, H)
            mm(3 * h, "z", H * h, "u", 0, H)
        for b in range(4):
            mm(4 + b, "w", 128 * b, "z", 0, L, False, True)
            w = L if last else C
            aff(v(xn, 4 + b, 4 + 4 * w, 4), ps(4 + b, 0, w), 1.0 / 64)
        for h in (1, 0):
            ts(v("sg", H * h, H * h + H), ps(2 - h, 0, H), ps(3 * h, 1, 2), sub)
            tt(v("cmp", 3 * h, 512, 4), v("sg", H * h, H * h + H), v("th", H * h, H * h + H), A_.is_lt)
            ts(v("cmp", 2 - h, 512, 4), ps(1 + h, 0, H), ps(3 * h, 1, 2), A_.is_lt if h else A_.is_le, v("lv", h, h + 1), mul)
        qz("c", v("cmp"))
        for h in (1, 0):
            tt(v("sa", 1 + 10 * h, 9 + 10 * h), ps(3 * h, 0, H, 16), v("mk", 1 + 10 * h, 9 + 10 * h), mx)
            calls[-1]["early"] = 0.3
        scan(v("pmn", 1, 20), v("rs2", 0, 19), v("sa", 0, 19), mx, mn, 100 * BIG)
        tt(v("nn", 0, 19), v("sa", 0, 19), v("pmn", 0, 19), A_.is_ge)
        scan(v("nm", 0, 19), v("nn", 0, 19), v("dd", 0, 19), mul, add)
        mm(2, "c", 0, "k", H // 2, H)
        for h in range(2):
            mm(3 * h, "k", H * h, "c", 0, H)
            act(v("xr", 1 + H * h, 1 + H * h + H), ps(3 * h, 0, H), F_.Relu, -1024.0, 1024.0)
        w = C // 2 if last else H
        for h in range(2):
            ts(v("oh", h, 4 * w, 2), v("iol" if last else "iot", 0, 2 * w), v("nm", 8 + 10 * h, 9 + 10 * h), A_.is_equal,
               ps(2, H // 2 - 1 + h, H // 2 + h), A_.is_gt)
        qz("h", v("oh", 0, 4 * w), 0, w)
        if last:
            act(v("t5", 0, C), ix(v("xr", 0, L + 1), v("ciu1", 0, NC)), F_.Copy)
        for h in range(2):
            mm(1 + h, "k", H * h, "h", 0, w)
            if last:
                tt(v("olr", w * h, w * h + w), ps(1 + h, 0, w), v("t5", w * h, w * h + w), A_.is_le)
            else:
                tt(v(sv, O + 1 + H * h, O + 1 + H * h + H), ps(1 + h, 0, H), v("xr", 1 + H * h, 1 + H * h + H), A_.is_le)
        if last:
            break
        win = v(sv, O - 1, O + 1 + L)
        tt(v("n%d" % (t + 1)), ix(win, v("lini")), v("n%d" % t), A_.is_le)
        scan(v("w1", 0, LW), v("n%d" % (t + 1), 0, LW), v("dl", 0, LW), mul, add)
        ts(v("cl%d" % (t + 1), 0, NC), v("w1", 16, LW, 17), "t4", add)
        compose_send(t + 1, xn)
        qz("a", v(xn, 4, 4 + 4 * C))
        unpack_state(t + 1, "a")
        for n, a in (("nv", O + 1), ("m", 0)):
            scan(v(n + str(t + 1), a, a + L), v(sv, O + 1, O + 1 + L), v(n + str(t), a, a + L), mx, mul)
        act(v("g%d" % (t + 1), 0, RW), ix(v("nv%d" % (t + 1), 0, O + 1 + L), v("rayi", 0, 23)), scale=-1.0)
        z_list(t + 1)
        if t == R - 2:
            act(v("o1", 0, C), ix(v("nv2", O - 1, O + 2 + L), v("ciu2", 0, NC)), F_.Copy)
            scan(v("o2", 0, C), v("diag", 0, C), v("o1", 0, C), mx, mul)
            table("ciu1", "o2", NC, "w4", -1.0, 0.0)

    store("Y", T.ol[:], v("olr", 0, C, 1, (0, 1)), DMA + X3)
    qz("a3", v(xn, 4, 4 + 4 * C))
    for j, (a, b) in enumerate(((0, 192), (192, C))):
        pick("f", "a3", "ciu", a // 16, b // 16)
        store("Y", T.oc[:, 4 * a:4 * b], (T.qf[:, a:b].bitcast(dt.uint8),) + v("qf", a, b)[1:], DMA + 0.3)
        mm(4 + j, "v", 0, "f", a, b - a)
        move(v("ysb", a, b), ps(4 + j, 0, b - a))
        store("S" if j else "Y", T.y[:, a:b], v("ysb", a, b), DMA + 0.3)
    for j in range(4):
        store("Y", T.osc[4 * j:4 * j + 4, :], v("pf", 0, C, 1, (32 * j, 32 * j + 4)), DMA)

    cnt = {"V": 0, "S": 0, "T": 0, "G": 0}
    know = {e: {} for e in Q}

    def need(e, toks):
        want = {}
        for s, n, snap in toks:
            if know[e].get(s, 0) < n and want.get(s, (0, None))[0] < n:
                want[s] = (n, snap)
        for s in sorted(want, key=lambda s: -len(want[s][1])):
            n, snap = want[s]
            if know[e].get(s, 0) < n:
                Q[e].wait_ge(T.sem[s], n)
                know[e][s] = n
                for j, x in snap.items():
                    if know[e].get(j, 0) < x:
                        know[e][j] = x

    if not ORDER:
        ORDER.extend(_order(calls))
    for n, e in sorted(x for x in ORDER if x[0] < loads) + [x for x in ORDER if x[0] >= loads]:
        c = calls[n]
        need(e, [d["done"] for d in c["deps"] if not (e == "T" and "T" in d["ways"])])
        if c["tok"]:
            c["ways"][e][1]()
            c["done"] = c["tok"] + ({},)
        else:
            cnt[e] += 1
            c["ways"][e][1]().then_inc(T.sem["c" + e], 1)
            c["done"] = ("c" + e, cnt[e], dict(know[e]))
    need("G", [("c" + e, cnt[e], {}) for e in cnt] + [("sent", R * 4 * ne, {}), ("dout", 16 * 9, {})])
